import numpy as np, ml_dtypes
CORES = [3,7,11,15,131,135,139,143]
N = 8
BF = ml_dtypes.bfloat16
W, K, I, M, VIS = 2048, 256, 16, 128, 6
def mark(u, a):
    return ((u * u >> 5) + 37 * u + a) & (M - 1)
def parts(rng):
    pop = rng.integers(0, M, (N, 8, 16))
    nm = np.where(rng.random((N, 8, W)) < 0.5, np.take_along_axis(pop, rng.integers(0, 16, (N, 8, W)), 2), rng.integers(0, M, (N, 8, W)))
    vo = rng.integers(0, 256, (N, 8, 16, W)); vn = rng.integers(0, 256, (N, 8, 16, W)); x = rng.integers(0, 256, (N, 8, 16, M))
    c = rng.integers(0, W, (N, 8, K)); s = 2 * rng.integers(0, 512, (N, 8, K)) + 1
    z = np.minimum(rng.integers(0, 160, (N, 8, 1, K)) + rng.integers(0, 64, (N, 8, 16, K)), 255)
    return nm, vo, vn, x, c, s, z
def bf(a):
    return np.ascontiguousarray(a.reshape(N, 128, -1)).astype(np.float32).astype(BF)
def pack(nm, vo, vn, x, c, s, z):
    return {"nm": nm.astype(np.int32), "vo": bf(vo), "vn": bf(vn), "xo": bf(x), "c0": c.astype(np.int32), "s0": s.astype(np.int32), "z0": bf(z)}
def share16(rng, S):
    S = np.asarray(S); b = S >> 4
    v = b[..., None] + (np.arange(16) < (S & 15)[..., None])
    d = (rng.random(S.shape + (8,)) * (np.minimum(b, np.maximum(254 - b, 0))[..., None] + 1)).astype(np.int64)
    v = v + np.concatenate([d, -d], axis=-1)
    return np.take_along_axis(v, np.argsort(rng.random(v.shape), axis=-1), -1)
def sums(rng, lo, hi):
    a = np.arange(lo, hi + 1); h = mark(a, 0); o = np.argsort(h + rng.random(len(a)))
    return a[o[np.minimum(np.searchsorted(h[o], np.arange(M)), len(a) - 1)]]
def setup_inputs(rng):
    return pack(*parts(rng))
def setup_inputs_spread(rng):
    nm, vo, vn, x, c, s, z = parts(rng)
    def sized(n):
        return np.minimum((np.exp2(8 * rng.random((N, 8, 1, n))) * rng.random((N, 8, 16, n))).astype(np.int64), 255)
    nm = np.minimum((M * rng.random((N, 8, W)) ** 3).astype(np.int64), M - 1)
    s = 2 * np.exp2(9 * rng.random((N, 8, K))).astype(np.int64) - 1
    return pack(nm, sized(W), sized(W), sized(M), c, s, sized(K))
def setup_inputs_ends(rng):
    nm, vo, vn, x, c, s, z = parts(rng)
    def ends(n):
        return 255 * np.where(rng.random((N, 8, 1, n)) < 0.5, rng.integers(0, 2, (N, 8, 1, n)), rng.integers(0, 2, (N, 8, 16, n)))
    vo, vn, x, z = ends(W), ends(W), ends(M), ends(K)
    nm = np.where(rng.random(nm.shape) < 0.7, (M - 1) * rng.integers(0, 2, nm.shape), nm)
    c = np.where(rng.random(c.shape) < 0.7, (W - 1) * rng.integers(0, 2, c.shape), c)
    s = np.where(rng.random(s.shape) < 0.7, 1 + 1022 * rng.integers(0, 2, s.shape), s)
    up = rng.integers(0, 2, (N, 8, 1))
    nm[..., W - 1] = M - 1; nm[..., 0] = 0; nm[..., 1:I - 3] = (M - 1) * rng.integers(0, 2, (N, 8, I - 4)); nm[..., I - 3] = 0; nm[..., I - 2] = M - 1
    vo[..., W - 1] = 255 * up; vn[..., I - 2] = 255 * (1 - up); vo[..., 0] = 255 * (1 - up); vn[..., I - 3] = 255 * up
    h = W // 2; vo[..., h:h + I] = 255 * up[..., None]; vn[..., h:h + I] = 255 * up[..., None]
    for k, a in ((0, W - 1), (1, h), (2, h), (K - 1, W - 1)):
        c[..., k] = a; s[..., k] = 1
    z[..., 1] = 0; z[..., 2] = 255; z[..., K - 1] = 255
    return pack(nm, vo, vn, x, c, s, z)
def setup_inputs_corners(rng):
    nm, vo, vn, x, c, s, z = parts(rng); pl = np.arange(W)
    ty = (np.arange(8)[None, :] + 3 * np.arange(N)[:, None] + int(rng.integers(0, 8))) % 8
    first = int(rng.integers(0, N)); ty[(first + 1) % N, int(np.argmin(ty[first]))] = 0
    for q in range(N):
        for g in range(8):
            t = int(ty[q, g])
            if t == 0:
                vo[q, g] = 0; vn[q, g] = rng.integers(0, 4, (16, W)); vn[q, g][:, I - 1::I] = share16(rng, sums(rng, 64, 4080)[rng.permutation(M)]).T
                c[q, g] = I * rng.permutation(np.arange(K) % M); s[q, g] = 1; z[q, g] = 0
            elif t == 1:
                vo[q, g] = vo[q, g] >> 1; vn[q, g] = vn[q, g] >> 1; z[q, g] = 255
            elif t == 2: nm[q, g] = (M - 1) * int(rng.integers(0, 2))
            elif t == 3: nm[q, g] = pl & (M - 1)
            elif t == 4:
                nm[q, g] = np.where(pl % I == I - 1, pl - (I - 1), pl) & (M - 1); c[q, g] = I * rng.integers(0, M, K); s[q, g] = 1
            elif t == 5:
                v = rng.integers(0, 256, (16, 1)); vo[q, g] = v; vn[q, g] = v
                z[q, g] = np.argsort(np.argsort(rng.random((16, K)), axis=0), axis=0) >= rng.choice(np.array([0, 8, 9, 16]), K)
            elif t == 6: x[q, g] = 255 * rng.integers(0, 2, (16, M))
            else:
                c[q, g] = rng.choice(np.array([0, W - 2, W - 1, W - I, W - I + 1]), K); s[q, g] = rng.choice(np.array([1, 3, 1021, 1023]), K)
    return pack(nm, vo, vn, x, c, s, z)
def setup_inputs_crowd(rng):
    nm, vo, vn, x, c, s, z = parts(rng); pl = np.arange(W); vo[:] = 0; z[:] = 0
    for g in range(8):
        for q in range(N):
            if q == 0 or g & 1:
                sm = sums(rng, 960, 3200); pick = sm[2 * rng.integers(0, M // 2, 2) + ((g >> 1) & 1)]
            S = np.full(W, int(pick[0]))
            if g >= 6:
                S = np.where(pl < W // 2, int(pick[0]), int(pick[1])); s[q, g] = 1
            vn[q, g] = share16(rng, S).T
            if g & 3: z[q, g, :, (0, K - 1, int(rng.integers(0, K)))[(g & 3) - 1]] = 255
    v = rng.integers(0, 256, (16, 1)); vo[:, 0] = v; vn[:, 0] = v; nm[:, 0] = np.maximum(nm[:, 0], 1)
    return pack(nm, vo, vn, x, c, s, z)
def setup_inputs_ties(rng):
    nm, vo, vn, x, c, s, z = parts(rng)
    vo[:, ::2] = 85 * rng.integers(0, 4, (N, 4, 16, W)); vn[:, ::2] = 85 * rng.integers(0, 4, (N, 4, 16, W))
    z[:, ::2] = np.minimum(85 * rng.integers(0, 4, (N, 4, 16, K)) + rng.integers(0, 2, (N, 4, 16, K)), 255)
    for q in range(N):
        for g in (1, 3, 5, 7):
            hi = int(rng.integers(1600, 3201)); lo = hi if g > 4 else hi - int(rng.integers(1, 400))
            v1 = share16(rng, hi); v2 = share16(rng, lo); ix = np.argsort(rng.random((16, W)), axis=0)
            vo[q, g] = 0; vn[q, g] = np.where(rng.random(W) < 0.3, v1[ix], v2[ix])
            a = int(np.sort(v1)[7]); b = int(np.sort(v2)[7])
            z[q, g] = rng.choice(np.array([a, a + 1, b, b + 1]), K)
    return pack(nm, vo, vn, x, c, s, z)
def check_inputs(d):
    bad = []
    for k, lo, hi in (("nm", 0, M - 1), ("c0", 0, W - 1), ("s0", 1, 1023), ("vo", 0, 255), ("vn", 0, 255), ("xo", 0, 255), ("z0", 0, 255)):
        v = np.asarray(d[k]).astype(np.float64)
        if not np.all((v >= lo) & (v <= hi)): bad.append("range of " + k)
        elif not np.all(v == np.floor(v)): bad.append("whole numbers in " + k)
    if not np.all((np.asarray(d["s0"]).astype(np.int64) & 1) == 1): bad.append("odd numbers in s0")
    return bad
def reference(nm, vo, vn, xo, c0, s0, z0):
    name = nm.astype(np.int64)
    O = vo.astype(np.float32).astype(np.int32).reshape(N, 8, 16, W); V = vn.astype(np.float32).astype(np.int32).reshape(N, 8, 16, W)
    X = xo.astype(np.float32).astype(np.int32).reshape(N, 8, 16, M); z = z0.astype(np.float32).astype(np.int32).reshape(N, 8, 16, K)
    c = c0.astype(np.int64); s = s0.astype(np.int64); A = np.zeros((N, 8, K), np.int64)
    row = np.arange(I); rule = np.arange(K); obj = np.arange(M); odd = (obj & 1) == 1
    for t in range(VIS):
        e = (c[..., None] + s[..., None] * row) & (W - 1)
        n = np.take_along_axis(name, e.reshape(N, 8, K * I), 2).reshape(N, 8, K, I)
        eq = n[..., :, None] == n[..., None, :]
        head = np.argmax(eq, axis=-1) == row; last = I - 1 - np.argmax(eq[..., ::-1], axis=-1)
        el = np.take_along_axis(e, last, 3)
        D = np.take_along_axis(V, el.reshape(N, 8, 1, K * I), 3) - np.take_along_axis(O, e.reshape(N, 8, 1, K * I), 3)
        D = D.reshape(N, 8, 16, K, I); S = np.add.reduce(np.abs(D), axis=2).astype(np.int64)
        f = np.argmax(np.where(head, S, -1), axis=-1)
        df = np.take_along_axis(D, f[:, :, None, :, None], 4)[..., 0]; B = np.abs(df)
        u = np.take_along_axis(S, f[..., None], 3)[..., 0]
        fire = np.add.reduce((B >= z).astype(np.int64), axis=2) >= 9
        m = mark(u, A)
        low = np.full((N, 8, M), K)
        np.minimum.at(low, (np.arange(N)[:, None, None], np.arange(8)[None, :, None], m), np.where(fire, rule, K))
        act = fire & (np.take_along_axis(low, m, 2) == rule)
        has = low < K; dm = np.take_along_axis(df, np.minimum(low, K - 1)[:, :, None, :], 3)
        has = np.where(odd, np.roll(has, 1, axis=0), has); dm = np.where(odd, np.roll(dm, 1, axis=0), dm)
        hw = has[:, :, None, :]; X2 = np.where(hw, np.clip(X + dm, 0, 255), X); a, b = t * M, (t + 1) * M
        name[..., a:b] = np.where(has, obj, name[..., a:b]); O[..., a:b] = np.where(hw, X, O[..., a:b]); V[..., a:b] = np.where(hw, X2, V[..., a:b])
        X = X2
        c = np.where(act, c + I * s, c + s * (f + 1)) & (W - 1); s = np.where(act, 2 * (u & 511) + 1, s)
        z = np.where(act[:, :, None, :], (z + B) >> 1, np.maximum(z - 1, 0)); A = (fire & ~act).astype(np.int64)
        if t < VIS - 1:
            c, s, z, A = np.roll(c, 1, axis=0), np.roll(s, 1, axis=0), np.roll(z, 1, axis=0), np.roll(A, 1, axis=0)
    L = VIS * M
    return {"yn": name[..., :L].astype(np.float32), "yo": O[..., :L].reshape(N, 128, L).astype(np.float32).astype(BF), "yv": V[..., :L].reshape(N, 128, L).astype(np.float32).astype(BF),
            "yx": X.reshape(N, 128, M).astype(np.float32).astype(BF), "yc": c.astype(np.float32), "ys": s.astype(np.float32), "ya": A.astype(np.float32), "yz": z.reshape(N, 128, K).astype(np.float32).astype(BF)}

@@ -1,0 +1,673 @@
+import math
+from concourse.mybir import AluOpType as OP, ActivationFunctionType as AF
+
+HP = "float16"
+BF, F32, I32, U16 = "bfloat16", "float32", "int32", "uint16"
+VIS = 6
+BIG = float(1 << 21)
+MQ = 393216.0
+M16 = 1.5 * (1 << 27)
+M1 = 1.5 * (1 << 23)
+MEW, MFW = 320, 144
+
+PER_HALF = {
+    "GT": (2048, BF), "OFF": (128, U16), "SBI": (16, F32), "C15": (16, F32), "A32": (8, F32),
+    "NB": (128, BF), "EP": (1024, BF), "EQ": (1024, BF), "YL": (128, F32), "LQ": (128, BF), "MA": (128, BF), "MB": (128, BF), "KEY": (128, HP), "CL": (1024, HP),
+    "VI": (64, I32), "RL": (128, I32), "PR": (128, F32), "SM": (128, I32), "SM2": (128, I32), "POFF": (128, U16),
+    "VV": (64, I32), "KA": (128, BF), "GO": (1024, BF), "DD": (1024, BF), "AB": (1024, BF),
+    "KT": (192, F32), "KS": (192, F32), "KI": (8, I32), "FL": (16, I32), "P2": (16, F32), "S2": (16, I32), "S3": (16, I32),
+    "EF": (16, HP), "DOFF": (16, U16), "UY": (8, I32), "UQ": (8, F32), "UM": (8, I32), "UN": (8, I32), "US": (8, I32),
+    "MST": (128, BF), "MG": (128, BF), "MR": (128, BF), "FO": (128, BF), "FD": (128, BF), "GE": (128, BF), "MQB": (128, BF),
+    "AT": (1024, BF), "WS": (1024, BF),
+}
+SB = {k: (2 * w, d) for k, (w, d) in PER_HALF.items()}
+SB.update({
+    "LO": (2048, BF), "LV": (2048, BF), "TT": (2048, BF), "XI": (128, BF), "Z0": (256, BF),
+    "EN": (384, F32), "EA": (384, F32), "EAG": (128, F32), "ET": (256, F32), "QB": (512, BF), "MT": (64, HP),
+    "SI": (16, F32), "CI": (16, I32), "CA": (16, I32), "CA2": (16, I32), "DPW": (384, BF), "DNW": (384, BF),
+    "T0": (8, F32), "T1": (8, F32), "SL": (8, F32), "LOWU": (8, U16), "LOW2": (8, U16), "SELU": (8, U16),
+    "DE": (128, BF), "ZA": (384, BF), "ZAG": (128, BF), "ZW": (384 * VIS, BF),
+    "MES": (MEW * VIS, HP), "MEL": (MEW * VIS, HP), "MFS": (MFW * VIS, BF), "MFL": (MFW * VIS, BF), "ZL": (256 * VIS, BF),
+    "XW": (768, BF), "STT": (256, BF), "BT": (128, BF), "AA": (256, BF), "HH": (256, BF), "YN": (768, F32), "YX": (128, BF), "YC": (256, F32),
+    "NROW": (2048, BF), "NMI": (128, I32), "NMB": (128, BF), "CSI": (256, I32), "CSF": (256, F32), "SA": (2048, BF), "SH": (2048, BF),
+    "IO1": (160, F32), "PI": (8, I32), "PJ": (8, I32), "COL": (32, F32), "ONES": (128, BF), "NH": (256, BF),
+    "DG": (896, BF), "FQ": (256, HP), "WID": (576, BF), "O256H": (144, HP), "TH": (128, BF), "N8": (128, BF),
+    "BM": (128, BF), "BO": (128, BF), "TRI": (256, BF), "M0": (128, BF), "TMP": (384, F32), "RC": (128, F32),
+    "E0M": (128, F32), "CM": (512, F32), "WD": (320, HP), "EXB": (512, HP), "EX": (4096, HP),
+    "SQ": (512, F32), "SK": (1024, BF), "BIGM": (2048, BF), "RS": (192, F32), "RW": (512, BF), "TG": (32, F32),
+})
+PLACE = {}
+_fill = {}
+for _k, (_w, _d) in SB.items():
+    if _w <= 64:
+        PLACE[_k] = ("pk" + _d, _fill.get(_d, 0))
+        _fill[_d] = _fill.get(_d, 0) + (_w + 15) // 16 * 16
+    else:
+        PLACE[_k] = (_k, 0)
+SCRATCH = {k: ("sbuf", [128, w], d) for k, (w, d) in SB.items() if w > 64}
+for _d, _w in _fill.items():
+    SCRATCH["pk" + _d] = ("sbuf", [128, _w], _d)
+for _i in range(8):
+    SCRATCH["PS%d" % _i] = ("psum", [128, 512], F32)
+DMAS = ["d%d" % i for i in range(24)]
+SEMAPHORES = ["cV", "cS", "cP", "cG", "sent"] + DMAS + ["%s%d" % (k, t) for k in ("aE", "aF", "aZ") for t in range(VIS)]
+
+PM = {"cy": 1.04, "hop": 110.0, "pe": 0.6, "ga": 1.56, "sc": 3.8, "link": 2600.0, "issue": 400.0, "fix": 0.0}
+OPT = {"eq": "VVMM", "win": 150.0, "tol": 30.0}
+ASSIGN = {}
+BOOST = {}
+
+
+def R(n, a=0, b=None, s=1, p0=0, p1=128, ps=1):
+    if b is None:
+        b = 512 if n.startswith("PS") else SB[n][0]
+    return (n, a, b, s, p0, p1, ps)
+
+
+def IND(win, off):
+    return ("ind", win, off)
+
+
+def cnt(r):
+    if r[0] == "ind":
+        return 16 * cnt(r[2])
+    return len(range(r[1], r[2], r[3]))
+
+
+def two(r):
+    return (not r[0].startswith("PS")) and SB[r[0]][1] in (BF, HP, U16)
+
+
+def isap(x):
+    return isinstance(x, tuple)
+
+
+def flat(rs):
+    o = []
+    for r in rs:
+        if isap(r):
+            o += [r[1], r[2]] if r[0] == "ind" else [r]
+    return o
+
+
+def build():
+    ops = []
+    hist = {}
+    bank = {}
+    phase = ["s", 0]
+    when = [0]
+    flex = {}
+    CY, FIX = PM["cy"], PM["fix"]
+
+    def add(who, cost, kind, args, reads, writes, lat=0.0, extra=()):
+        i = len(ops)
+        deps = set(extra)
+        wr = []
+        for w in writes:
+            if w[0] == "ind":
+                wr.append(w[1]); reads = list(reads) + [w[2]]
+            else:
+                wr.append(w)
+        for isw, lst in ((False, flat(reads)), (True, wr)):
+            for r in lst:
+                h = hist.setdefault(r[0], [])
+                lo, hi = r[1], r[2]
+                for (j, w2, a, b) in h:
+                    if j != i and (isw or w2) and a < hi and lo < b:
+                        deps.add(j)
+                if isw:
+                    h[:] = [e for e in h if not (lo <= e[2] and e[3] <= hi and r[3] == 1 and r[4] == 0 and r[5] == 128 and r[6] == 1)]
+                h.append((i, isw, lo, hi))
+                if r[0].startswith("PS"):
+                    st = bank.setdefault(r[0], [None, [], []])
+                    if st[0] != who:
+                        st[0], st[2], st[1] = who, st[1], []
+                    deps.update(j for j in st[2] if j != i)
+                    if who == "P":
+                        deps.update(st[1][-1:] if i not in st[1] else [])
+                    if i not in st[1]:
+                        st[1].append(i)
+        ops.append({"eng": who, "cost": cost, "kind": kind, "args": args, "deps": deps, "lat": lat, "t": when[0],
+                    "key": "%s%d" % ("c" if phase[0] == "a" and when[0] == 0 else phase[0], phase[1])})
+        phase[1] += 1
+        return i
+
+    def pick(e):
+        if len(e) == 1:
+            return e
+        k = "%s%d" % tuple(phase)
+        flex[k] = e
+        return ASSIGN.get(k, e[0])
+
+    def vcost(out, ins, tt=False):
+        n = cnt(out)
+        if out[0] == "ind":
+            return 50 + PM["sc"] * n * CY
+        if any(x[0] == "ind" for x in ins):
+            return 50 + PM["ga"] * n * CY
+        if tt:
+            rate = 1.0 if any(x[0].startswith("PS") for x in ins) else 2.0
+        else:
+            rate = 0.5 if two(out) and all(two(x) for x in ins) else 1.0
+        return max(64, n * rate) * CY + FIX
+
+    def scost(out, in_):
+        return (65 + PM["ga"] * cnt(out) * CY) if in_[0] == "ind" else max(64, cnt(out)) * CY + FIX
+
+    def ts(out, in0, s1, op0, s2=None, op1=None):
+        return add("V", vcost(out, [in0]), "ts", (out, in0, s1, s2, op0, op1), [in0, s1, s2], [out])
+
+    def tt(out, a, b, op):
+        return add("V", vcost(out, [a, b], True), "tt", (out, a, b, op), [a, b], [out])
+
+    def cp(out, in_, e="V"):
+        e = pick(e)
+        if e == "G":
+            return add(e, 170 + 2 * cnt(out) * CY, "gcp", (out, in_), [in_], [out])
+        return add(e, vcost(out, [in_]) if e == "V" else scost(out, in_), "cp", (out, in_), [in_], [out])
+
+    def act(out, in_, f, bias=0.0, scale=1.0):
+        return add("S", scost(out, in_), "act", (out, in_, f, bias, scale), [in_, bias, scale], [out])
+
+    def aff(out, in_, scale, bias=0.0, e="VS"):
+        return ts(out, in_, scale, OP.mult, bias, OP.add) if pick(e) == "V" else act(out, in_, AF.Identity, bias, scale)
+
+    def relu(out, in_, scale, e):
+        return ts(out, in_, scale, OP.mult, 0.0, OP.max) if pick(e) == "V" else act(out, in_, AF.Relu, 0.0, scale)
+
+    def scan(out, d0, d1, init, op0, op1):
+        return add("V", vcost(out, [d0, d1]), "scan", (out, d0, d1, init, op0, op1), [d0, d1], [out])
+
+    def tr(out, in_):
+        return add("V", vcost(out, [in_]), "tr", (out, in_), [in_], [out])
+
+    def ms(out, v):
+        return add("V", vcost(out, []), "ms", (out, v), [], [out])
+
+    def iota(out, pat, base, cm):
+        return add("G", 130 + 2 * cnt(out) * CY, "iota", (out, pat, base, cm), [], [out])
+
+    def mm(groups, start=True, stop=True):
+        c = 0; rd = []; wr = []
+        for out, terms in groups:
+            wr.append(out)
+            for l, r in terms:
+                c += max(64, cnt(r)) * (4 if SB[r[0]][1] == F32 else 1) * PM["pe"]
+                rd += [l, r]
+        return add("P", c, "mm", (groups, start, stop), rd, wr)
+
+    def mms(out, terms, cuts):
+        e = [0] + cuts + [len(terms)]
+        for x in range(len(e) - 1):
+            mm([(out, terms[e[x]:e[x + 1]])], x == 0, x == len(e) - 2)
+
+    nd = [0]
+
+    def load(q, out, in_, lat=2200.0):
+        nd[0] += 1
+        return add(q, 60.0, "dma", (out, in_, DMAS[nd[0] - 1]), [in_] if in_[0] != "in" else [], [out], lat)
+
+    def store(q, out, in_):
+        nd[0] += 1
+        return add(q, 60.0, "dma", (out, in_, DMAS[nd[0] - 1]), [in_], [], 2200.0)
+
+    def send(name, src, dst):
+        i = add("G", PM["issue"], "send", (src, dst, name), [src], [])
+        return add("N", 0.0, "recv", (name,), [], [dst], PM["link"], [i])
+
+    A, S_, Mu, Mx, Mn = OP.add, OP.subtract, OP.mult, OP.max, OP.min
+    EQL, AND, SHR = OP.is_equal, OP.bitwise_and, OP.arith_shift_right
+    col = lambda j, p1=128: R("COL", j, j + 1, p1=p1)
+    blk = lambda n, j: R(n, 128 * j, 128 * j + 128)
+    ID, NID, HID, QID, KD, CD, BD = (blk("DG", j) for j in range(7))
+    ONES = R("ONES")
+    wide = lambda j, r: R("WID", 144 * j + 16 - r, 144 * j + 144 - r)
+    whole = lambda j: R("WID", 144 * j, 144 * j + 144)
+
+    load("Y", R("NMI"), ("in", "nm"))
+    ms(R("CSI"), 0)
+    for q in range(2):
+        load("S", R("LO", 1024 * q, 1024 * q + 1024), ("in", "vo", 1024 * q, 1024 * q + 1024), 3000.0)
+        load("Y", R("LV", 1024 * q, 1024 * q + 1024), ("in", "vn", 1024 * q, 1024 * q + 1024), 3000.0)
+    load("Y", R("CSI", p0=0, ps=16), ("in", "c0"))
+    load("Y", R("CSI", p0=1, ps=16), ("in", "s0"))
+    cp(R("NMB"), R("NMI"))
+    load("Y", R("NROW", p1=8), R("NMB"))
+    load("Y", R("XI"), ("in", "xo"))
+    load("Y", R("Z0"), ("in", "z0"))
+
+    iota(R("PI", 0, 1), [[0, 1]], 0, 1)
+    iota(R("IO1"), [[1, 160]], -16, 0)
+    iota(R("RC"), [[0, 8], [1, 16]], 0, 0)
+    iota(blk("SQ", 0), [[1, 16], [0, 8]], 0, 0)
+    iota(blk("SQ", 1), [[1, 16], [-1, 8]], -1, 0)
+    iota(blk("SQ", 2), [[1, 16], [1, 8]], 1, 0)
+    iota(blk("SQ", 3), [[0, 16], [-1, 8]], 14, 0)
+    iota(R("TG", 16, 24), [[16, 8]], 1, 0)
+    iota(R("TG", 24, 32), [[0, 2], [16, 4]], 0, 0)
+    iota(R("TG", 0, 8), [[1, 2], [32, 4]], 0, 0)
+    iota(R("STT", 0, 64), [[2, 64]], 0, 0)
+    iota(R("STT", 128, 192), [[2, 64]], 1, 0)
+    PI = R("PI", 0, 1)
+    PJ = lambda j: R("PJ", j, j + 1)
+    cp(col(0), PI)
+    ts(PJ(0), PI, 15, AND); cp(col(1), PJ(0))
+    tt(col(2), col(0), col(1), S_)
+    ts(col(3), col(1), 0.0, EQL); ts(col(4), col(1), 1.0, EQL); ts(col(6), col(1), 2.0, EQL)
+    tt(col(5), col(4), col(6), A); tt(col(9), col(4), col(3), S_)
+    aff(col(7), col(1), 17.0 / 256 - 1.0, -32.5, "SV"); aff(col(8), col(1), -17.0, 255.0, "SV")
+    ts(PJ(1), PI, 4, SHR, 1, AND); cp(col(10), PJ(1)); aff(col(11), col(10), -1.0, 1.0, "SV")
+    ts(PJ(2), PI, 1, SHR, 7, AND); cp(col(12), PJ(2))
+    ts(PJ(3), PI, 1, AND); ts(PJ(4), PI, 96, AND)
+    ts(col(14), PJ(3), 16.0, Mu); tt(col(13), col(14), PJ(4), A)
+    C0 = R("IO1", 16, 144)
+    ts(ID, C0, col(0), EQL); aff(NID, ID, -1.0)
+    ms(ONES, 1.0)
+    ts(whole(0), R("IO1", 0, 144), col(2), EQL)
+    aff(whole(1), whole(0), col(3)); ts(whole(2), whole(0), col(5), Mu, 256.0, Mu)
+    TA, TH = wide(0, 2), R("TH")
+    tt(TH, wide(0, 1), TA, S_)
+    ts(R("N8", p1=32), R("IO1", 16, 144, p1=32), 1.0 / 16, Mu, col(0, 32), EQL)
+    tt(blk("TMP", 1), C0, R("RC"), S_)
+    ts(R("BM"), blk("TMP", 1), col(2), EQL)
+    aff(R("M0"), R("BM"), col(3))
+    aff(blk("TMP", 0), R("RC"), col(4), col(3), "SV"); tt(R("E0M"), blk("TMP", 0), R("BM"), Mu)
+
+    def floor_mod(ps, dst, q):
+        act(R("QB", q, q + 256), R(ps, 0, 256), AF.Identity, MQ - 1023.625)
+        tt(R(dst, 0, 256), R(ps, 0, 256), R("QB", q, q + 256), S_)
+
+    cp(R("CSF"), R("CSI"))
+    mm([(R("PS0", 0, 256), [(R("E0M"), R("CSF"))])])
+    floor_mod("PS0", "EN", 0)
+    for q in range(4):
+        a, b = 512 * q, 512 * q + 512
+        mm([(R("PS%d" % (2 + q % 2)), [(ID, R("LV", a, b)), (NID, R("LO", a, b))])])
+        act(R("SA", a, b), R("PS%d" % (2 + q % 2)), AF.Abs)
+        ts(R("SH", a, b), R("SA", a, b), M16, A, M16, S_)
+        mm([(R("PS%d" % (4 + q)), [(TA, R("SA", a, b)), (TH, R("SH", a, b)), (R("N8", p1=8), R("NROW", a, b, p1=8))])])
+        cp(R("TT", a, b), R("PS%d" % (4 + q)), "VS" if q % 2 else "SV")
+
+    K = lambda j: blk("SK", j)
+    Q = lambda j: blk("SQ", j)
+    ts(K(0), Q(0), col(1), EQL); ts(K(1), Q(1), col(1), EQL); ts(K(2), Q(1), 16.0, A, col(1), EQL)
+    ts(K(3), Q(2), col(1), EQL); ts(K(4), Q(2), -16.0, A, col(1), EQL); ts(K(5), Q(3), col(1), OP.is_ge)
+    tt(K(3), K(3), K(4), A); tt(K(3), K(0), K(3), S_)
+    tt(K(5), K(5), K(0), Mu)
+    tt(K(1), K(1), K(0), A); tt(K(1), K(1), K(5), S_)
+    aff(K(1), K(1), float(4 ** 17))
+    for d in range(8):
+        v = lambda j: R("SK", 128 * j + d, 128 * j + 128, 8)
+        aff(v(6), v(5), float(4 ** (d + 1)), 0.0, "SV"); aff(v(7), v(2), float(4 ** (15 - d)), 0.0, "SV")
+    tt(K(6), K(6), K(7), A); tt(K(6), K(6), K(1), A)
+    for gq in range(8):
+        ts(col(16 + gq), col(2), 16.0 * gq, EQL)
+        for j, src in enumerate((3, 6)):
+            aff(blk("BIGM", 8 * j + gq), K(src), col(16 + gq))
+    BMX = lambda j, d: R("BIGM", 1024 * j + d, 1024 * j + 1024, 8)
+
+    aff(HID, ID, 0.5); aff(QID, ID, 1.0 / 256); aff(KD, ID, col(8)); aff(CD, ID, 1152.0); aff(BD, ID, -BIG)
+    ts(blk("FQ", 0), ID, 0.25, Mu); ts(blk("FQ", 1), ID, col(6), Mu)
+    aff(whole(3), whole(0), 256.0); ts(R("O256H"), whole(0), 256.0, Mu)
+    aff(R("BO"), R("BM"), -128.0)
+    TRI, TRH = blk("TRI", 0), blk("TRI", 1)
+    ts(blk("TMP", 2), C0, col(0), OP.is_gt); tt(blk("TMP", 2), blk("TMP", 2), R("BM"), Mu)
+    aff(TRI, ID, 16.0); tt(TRI, TRI, blk("TMP", 2), A); aff(TRH, TRI, 0.5)
+    for kh in range(2):
+        ts(blk("TMP", 0), R("RC"), 7.5, OP.is_gt if kh else OP.is_lt); tt(blk("TMP", 0), blk("TMP", 0), R("BM"), Mu)
+        aff(blk("CM", kh), blk("TMP", 0), col(3), 0.0, "SV"); aff(blk("CM", 2 + kh), blk("TMP", 0), col(9), 0.0, "SV")
+        ts(R("WD", 160 * kh, 160 * kh + 160), R("IO1"), col(0), EQL, col(10 if kh else 11), Mu)
+    ts(blk("TMP", 1), blk("TMP", 1), col(13), EQL)
+    for j in range(4):
+        e = blk("EXB", j)
+        if j == 0: ts(e, R("RC"), col(10), Mu, 1.0, A)
+        if j == 1: ts(e, R("RC"), col(10), Mu, col(11), A)
+        if j == 2: ts(e, R("RC"), col(10), OP.is_le)
+        if j == 3: ts(e, R("RC"), col(10), EQL)
+        tt(e, e, blk("TMP", 1), Mu)
+        for b in range(8 if j < 2 else 0):
+            if j == 0: ts(col(24 + b), col(12), float(b), EQL)
+            ts(blk("EX", 8 * j + b), e, col(24 + b), Mu)
+    ms(R("NH"), -0.5); ms(R("MST"), 0.0)
+    for n in ("DPW", "DNW", "EA", "ZA"):
+        ms(R(n, 256, 384), 0.0)
+    ms(R("RS"), 0.0); ms(R("RS", 0, 128, 16), -4 * BIG); ms(R("RS", 128, 192, 8), -4 * BIG)
+    ms(R("RW"), -1.0); ms(R("RW", 0, 512, 128), 1024.0)
+    ts(R("TG", 16, 32), R("TG", 16, 32), col(1), A)
+    aff(col(15), col(1), 2.0, 0.0, "SV"); ts(R("TG", 0, 8), R("TG", 0, 8), col(15), A); aff(R("TG", 8, 16), R("TG", 0, 8), -512.0, 0.0, "SV")
+    for par in range(2):
+        aff(R("STT", 128 * par, 128 * par + 64), R("STT", 128 * par, 128 * par + 64), col(3), 0.0, "SV")
+        cp(R("XW", 384 * par + 64, 384 * par + 128), R("XI", par, 128, 2), "SV")
+        aff(R("XW", 384 * par, 384 * par + 64), R("XI", par, 128, 2), -1.0, 255.0, "SV")
+
+    def read_half(h, ME, ZC):
+        pA, pB, pC, pD = ("PS%d" % (4 * h + j) for j in range(4))
+
+        def H(n, a=0, b=None, s=1):
+            w = PER_HALF[n][0]
+            return R(n, w * h + a, w * h + (w if b is None else b), s)
+
+        for j in range(2):
+            mm([(R(pD, 64 * j, 64 * j + 64), [(blk("CM", 2 * j + kh), R("EN", 128 * h + 64 * kh, 128 * h + 64 * kh + 64)) for kh in range(2)])])
+        for q in range(2):
+            mm([(R(pC, 64 * q, 64 * q + 64), [(wide(1, r), H("GT", 1024 * q + r, 1024 * q + 1024, 16)) for r in range(16)])])
+        cp(H("NB"), R(pC, 0, 128), "SV")
+        for j, pq in enumerate((pA, pB)):
+            mm([(R(pq, 128 * d, 128 * d + 128), [(BMX(0, 4 * j + d), H("NB"))]) for d in range(4)])
+            eq, ep = H("EQ", 512 * j, 512 * j + 512), H("EP", 512 * j, 512 * j + 512)
+            mode = OPT["eq"][2 * h + j]
+            phase[1] += 1 if mode == "V" else 0
+            if mode == "V":
+                ts(eq, R(pq), 0.0, EQL)
+            else:
+                act(ep, R(pq), AF.Abs)
+                ts(eq, ep, 0.0, EQL) if mode == "M" else act(eq, ep, AF.Relu, 1.0, -1.0)
+        mms(R(pC, 128, 256), [(BMX(1, d), H("EQ", 128 * d, 128 * d + 128)) for d in range(8)], [4])
+        act(H("YL"), R(pC, 128, 256), AF.Ln, 1.0)
+        aff(H("LQ"), H("YL"), 1.0 / math.log(4.0), 127.7, "SV")
+        if pick("SV") == "S":
+            act(H("MA"), H("YL"), AF.Sign, -1.0)
+        else:
+            ts(H("MA"), H("LQ"), 128.5, OP.is_gt, 2.0, Mu)
+        ma = ops[-1]["eng"]
+        if pick("SV") == "S":
+            act(H("MB"), H("YL"), AF.Sign, 22.7, -1.0)
+        else:
+            ts(H("MB"), H("LQ"), 144.0, OP.is_lt, 2.0, Mu)
+        one = (ma == "S") + (ops[-1]["eng"] == "S")
+        mm([(R(pD, 256, 384), [(QID, H("LQ")), (TRH, H("MA")), (TRH, H("MB"))] + [(TRH if one == 1 else TRI, ONES)] * (one > 0))])
+        ts(H("KEY"), R(pD, 256, 384), col(7), A, 0.0, Mx)
+        for s in range(8):
+            ts(H("CL", 128 * s, 128 * s + 128), H("KEY"), float(s), Mx, float(s + 1), Mn)
+        mms(R(pA, 0, 64), [(R("O256H", 16 - 8 * kh - s, 144 - 8 * kh - s), H("CL", 128 * s + 64 * kh, 128 * s + 64 * kh + 64)) for s in range(8) for kh in range(2)], [4, 8, 12])
+        mms(R(pB, 0, 128), [(wide(2, r), H("GT", r, 2048, 16)) for r in range(16)] + [(KD, ONES), (BD, H("MA"))] + [(BD, ONES)] * (ma == "S"), [3, 6, 9, 12, 15])
+        tr(H("KT", 0, 128), R(pB, 0, 128))
+        scan(H("KS", 0, 128), R("RS", 0, 128), H("KT", 0, 128), 0.0, A, Mx)
+        cp(H("VI"), R(pA, 0, 64))
+        ts(H("RL", 0, 64), H("VI"), 4, SHR, 15, AND); ts(H("RL", 64, 128), H("VI"), 15, AND)
+        for j in range(2):
+            a, b = 64 * j, 64 * j + 64
+            tt(H("PR", a, b), H("RL", a, b), R(pD, 64, 128), Mu)
+            tt(H("SM", a, b), H("PR", a, b), R(pD, 0, 64), A)
+            ts(H("SM2", a, b), H("SM", a, b), 2047, AND); cp(H("POFF", a, b), H("SM2", a, b))
+        ts(H("VV"), H("VI"), 255, AND)
+        ts(H("KA", 0, 64), H("VV"), -1.0, Mu, 255.0, A); ts(H("KA", 64, 128), H("VV"), 0.0, EQL, -BIG, Mu)
+        for q in range(2):
+            cp(H("GO", 512 * q, 512 * q + 512), IND(R("LO"), H("POFF", 32 * q, 32 * q + 32)), "SV")
+        for q in range(2):
+            a, b = 512 * q, 512 * q + 512
+            tt(H("DD", a, b), IND(R("LV"), H("POFF", 64 + 32 * q, 96 + 32 * q)), H("GO", a, b), S_)
+            act(H("AB", a, b), H("DD", a, b), AF.Abs)
+        mms(R(pB, 128, 192), [(ID, H("KA", 0, 64)), (ID, H("KA", 64, 128))] + [(wide(3, p), H("AB", p, 1024, 16)) for p in range(16)], [2])
+        tr(H("KT", 128, 192), R(pB, 128, 192))
+        scan(H("KS", 128, 192), R("RS", 128, 192), H("KT", 128, 192), 0.0, A, Mx)
+        for kh in range(2):
+            tt(H("KI", 4 * kh, 4 * kh + 4), H("KS", 64 * kh + 15, 64 * kh + 64, 16), H("KS", 128 + 8 * kh + 7, 192, 16), Mx)
+        ts(H("FL", 0, 8), H("KI"), 4, SHR, 15, AND); ts(H("FL", 8, 16), H("KI"), 15, AND)
+        tt(H("P2"), H("FL"), H("SBI"), Mu); tt(H("S2"), H("C15"), H("P2"), S_)
+        ts(H("S3"), H("S2"), 2047, AND); cp(H("EF"), H("S3"))
+        mm([(R(pA, 64 + xh, 80, 2), [(R("WD", 160 * xh + 16 - 16 * (gp - xh), 160 * xh + 144 - 16 * (gp - xh)), H("EF", gp, 16, 2)) for gp in range(2)]) for xh in range(2)])
+        cp(H("DOFF"), R(pA, 64, 80))
+        cp(ME(8 * h, 8 * h + 8), H("EF", 0, 8))
+        ts(H("UY"), H("KI"), 1.0 / 256, Mu, -1456.498, A)
+        tt(H("UQ"), H("UY"), H("UY"), Mu); tt(H("UM"), H("UQ"), H("A32"), A)
+        ts(H("UN"), H("UM"), 5, SHR, 127, AND); cp(H("MST", 0, 128, 16), H("UN"))
+        tr(H("MG"), H("MST"))
+        mm([(R(pC, 256, 384), [(R("M0"), H("MG"))])])
+        cp(H("MR"), R(pC, 256, 384), "SV")
+        ts(H("US"), H("KI"), 8, SHR, 511, AND); ts(ME(48 + 8 * h, 56 + 8 * h), H("US"), 2.0, Mu, 1.0, A)
+        cp(H("FO"), IND(R("LO"), H("DOFF", 0, 8)), "SV")
+        tt(H("FD"), IND(R("LV"), H("DOFF", 8, 16)), H("FO"), S_)
+        act(R(pA, 256, 384), H("FD"), AF.Abs)
+        tt(H("GE"), R(pA, 256, 384), ZC(128 * h, 128 * h + 128), OP.is_ge)
+        mms(R(pB, 256, 384), [(CD, ONES), (R("BO"), H("GE"))], [1])
+        tt(H("MQB"), R(pB, 256, 384), H("MR"), Mx)
+        ts(ME(64 + 128 * h, 192 + 128 * h), H("MQB"), 127.5, OP.is_lt)
+        relu(blk("DPW", h), H("FD"), 1.0, "SV"); relu(blk("DNW", h), H("FD"), -1.0, "SV")
+        for hi in range(8):
+            o = H("AT", 128 * hi, 128 * hi + 128)
+            if pick("SV" if hi in (2, 3, 6, 7) else "VS") == "S":
+                act(o, H("MQB"), AF.Abs, R("TG", 8 + hi, 9 + hi), 512.0)
+            else:
+                ts(o, H("MQB"), R("TG", hi, hi + 1), OP.not_equal, 512.0, Mu)
+        for q in range(2):
+            scan(H("WS", 512 * q, 512 * q + 512), R("RW"), H("AT", 512 * q, 512 * q + 512), 0.0, A, Mn)
+
+    def update(t, par, dpn, sel, psT, psX):
+        last = t == VIS - 1
+        cur, new = 384 * par + 192 * (t % 2), 384 * par + 192 * (1 - t % 2)
+        pl = lambda n: R(n, 128 * t + par, 128 * t + 128, 2)
+        a0 = 128 * par
+        ap, an = R("AA", a0, a0 + 64), R("AA", a0 + 64, a0 + 128)
+        tt(R("AA", a0, a0 + 128), dpn, R("XW", cur, cur + 128), Mn)
+        bt = R("BT", 64 * par, 64 * par + 64)
+        cp(bt, IND(R("STT", a0, a0 + 128), sel), "SV")
+        if not last:
+            ts(R("HH", a0, a0 + 128), R("AA", a0, a0 + 128), M16, A, M16, S_)
+            mms(R(psT, 0, 64), [(ID, bt), (TA, ap), (TA, an), (TH, R("HH", a0, a0 + 64)), (TH, R("HH", a0 + 64, a0 + 128))], [3])
+            cp(pl("TT"), R(psT, 0, 64), "SV")
+        else:
+            phase[1] += 4
+        cp(pl("YN"), bt, "SV")
+        mm([(R(psX, 0, 64), [(ID, R("XW", cur + 64, cur + 128)), (ID, ap), (NID, an)])])
+        cp(R("XW", new + 64, new + 128), R(psX, 0, 64), "SV")
+        if not last:
+            aff(R("XW", new, new + 64), R("XW", new + 64, new + 128), -1.0, 255.0, "SV")
+        else:
+            cp(R("YX", par, 128, 2), R("XW", new + 64, new + 128), "SV")
+        cp(pl("LO"), IND(R("XW", cur + 64, cur + 192), sel), "SV")
+        cp(pl("LV"), IND(R("XW", new + 64, new + 192), sel), "SV")
+
+    for t in range(VIS):
+        last = t == VIS - 1
+        phase[0], phase[1] = "a", 0
+        when[0] = t
+        ME = lambda a, b: R("MES", MEW * t + a, MEW * t + b)
+        MF = lambda a, b: R("MFS", MFW * t + a, MFW * t + b)
+        L = lambda a, b: R("MFL", MFW * t + a, MFW * t + b)
+        ZC = (lambda a, b: R("Z0", a, b)) if t == 0 else (lambda a, b: R("ZL", 256 * (t - 1) + a, 256 * (t - 1) + b))
+        for h in range(2):
+            ts(blk("OFF", h), blk("EN", h), MQ, A)
+        for q in range(8):
+            cp(R("GT", 512 * q, 512 * q + 512), IND(R("TT"), R("OFF", 32 * q, 32 * q + 32)), "VS" if q % 2 else "SV")
+        for par in range(2):
+            cur, new = 384 * par + 192 * (t % 2), 384 * par + 192 * (1 - t % 2)
+            for n, dst in (("LO", R("XW", cur + 128, cur + 192)), ("LV", R("XW", new + 128, new + 192)), ("TT", R("STT", 128 * par + 64, 128 * par + 128))):
+                cp(dst, R(n, 128 * t + par, 128 * t + 128, 2), "G")
+        tr(R("ET"), R("EN", 0, 256))
+        ETr = lambda r, a=0, b=256: R("ET", a + r, b, 16)
+        tt(R("SI"), ETr(1), ETr(0), S_)
+        for j in range(4):
+            cp(R("SBI", 8 * j, 8 * j + 8), R("SI", 8 * (j // 2), 8 * (j // 2) + 8), "G")
+            cp(R("C15", 8 * j, 8 * j + 8), ETr(15, 128 * (j // 2), 128 * (j // 2) + 128), "G")
+        cp(ME(16, 32), R("SI"))
+        tt(R("CA"), ETr(15), R("SI"), A); ts(R("CA2"), R("CA"), 2047, AND); cp(ME(32, 48), R("CA2"))
+        cp(R("CI"), ETr(0)); tt(R("A32"), ETr(0), R("CI"), S_); aff(R("A32"), R("A32"), 128.0, -350464.0, "SV")
+        read_half(0, ME, ZC)
+        aff(R("T1"), R("WS", 127, 1024, 128), 1.0, -128.0, "SV"); tt(R("T0"), R("T1"), R("TG", 16, 24), Mn)
+        read_half(1, ME, ZC)
+        if not last:
+            send("aE%d" % t, ME(0, MEW), R("MEL", MEW * t, MEW * t + MEW))
+        else:
+            phase[1] += 2
+        tt(MF(128, 136), R("T0"), R("WS", 1024 + 127, 2048, 128), Mn)
+        ts(R("LOWU"), MF(128, 136), 255.0, A)
+        cp(MF(0, 64), IND(R("DPW"), R("LOWU", 4, 8)), "SV"); cp(MF(64, 128), IND(R("DNW"), R("LOWU", 4, 8)), "VS")
+        ts(R("SL"), MF(128, 136), 0.0, OP.is_gt, 64.0, Mu); tt(MF(136, 144), R("SL"), R("TG", 24, 32), A)
+        send("aF%d" % t, MF(0, MFW), L(0, MFW))
+        cp(R("SELU", 0, 4), MF(136, 140))
+        cp(R("DE", 0, 64), IND(R("DPW"), R("LOWU", 0, 4)), "SV"); cp(R("DE", 64, 128), IND(R("DNW"), R("LOWU", 0, 4)), "SV")
+        update(t, 0, R("DE"), R("SELU", 0, 4), "PS6", "PS7")
+        src, ex = ("MES", 16) if last else ("MEL", 0)
+        tr(R("MT"), R(src, MEW * t, MEW * t + 64))
+        mm([(R("PS0", 32 * b, 32 * b + 32), [(blk("EX", ex + b), R("MT", 0, 32)), (blk("FQ", int(last)), R(src, MEW * t + 64 + 32 * b, MEW * t + 96 + 32 * b))]) for b in range(8)])
+        floor_mod("PS0", "EN", 0)
+        mm([(R("PS1", 32 * b, 32 * b + 32), [(blk("EX", ex + 8 + b), R("MT", 32, 64))]) for b in range(8)])
+        floor_mod("PS1", "EA", 256)
+        for x in range(4 * t, 4 * t + 4):
+            if x < 16 and not last:
+                ts(blk("EX", 16 + x), blk("EXB", 2 + x // 8), col(24 + x % 8), Mu)
+            else:
+                phase[1] += 1
+        mm([(R("PS4", 0, 256), [(HID, ZC(0, 256)), (HID, R("NH")), (HID, R("DPW", 0, 256)), (HID, R("DNW", 0, 256))])])
+        ts(R("ZA", 0, 256), R("PS4", 0, 256), M1, A, M1, S_)
+        ts(R("ZW", 384 * t, 384 * t + 256), ZC(0, 256), -1.0, A, 0.0, Mx)
+        cp(R("ZAG"), IND(R("ZA"), R("LOWU")), "SV")
+        cp(IND(R("ZW", 384 * t, 384 * t + 384), R("LOWU")), R("ZAG"))
+        if not last:
+            send("aZ%d" % t, R("ZW", 384 * t, 384 * t + 256), R("ZL", 256 * t, 256 * t + 256))
+            ts(R("LOW2"), L(128, 136), 255.0, A)
+        else:
+            phase[1] += 3
+        low = R("LOWU" if last else "LOW2")
+        cp(R("SELU", 4, 8), L(140, 144))
+        cp(R("EAG"), IND(R("EA"), low), "SV")
+        cp(IND(R("EN"), low), R("EAG"))
+        update(t, 1, L(0, 128), R("SELU", 4, 8), "PS2", "PS3")
+        if t >= VIS - 2:
+            phase[0], phase[1] = "o", 3 * (t - VIS + 2)
+            a, b = (128 * t, 128 * VIS) if last else (0, 128 * (VIS - 1))
+            store("Y", ("out", "yo", a, b), R("LO", a, b))
+            store("S" if last else "Y", ("out", "yv", a, b), R("LV", a, b))
+            store("Y", ("out", "yn", a, b), R("YN", a, b, ps=16))
+    act(R("YC"), R("EN", 0, 256), AF.Identity, MQ)
+    for j, n in enumerate(("yc", "ys", "ya")):
+        store("Y", ("out", n), R("YC", p0=j, ps=16))
+    store("Y", ("out", "yx"), R("YX"))
+    store("Y", ("out", "yz"), R("ZW", 384 * (VIS - 1), 384 * (VIS - 1) + 256))
+    return ops, flex
+
+
+def schedule(ops):
+    n = len(ops)
+    hop = PM["hop"]
+    succ = [[] for _ in range(n)]
+    for i, o in enumerate(ops):
+        for j in o["deps"]:
+            succ[j].append(i)
+    gap = lambda j, i: 0.0 if ops[j]["kind"] == "send" or (ops[j]["eng"] == "P" and ops[i]["eng"] == "P") else hop
+    prio = [0.0] * n
+    for i in range(n - 1, -1, -1):
+        prio[i] = ops[i]["cost"] + ops[i]["lat"] + max([prio[j] + gap(i, j) for j in succ[i]] + [0.0])
+    for i in range(n):
+        prio[i] += 50.0 * BOOST.get(ops[i]["key"].replace("c", "a"), 0)
+    left = [len(o["deps"]) for o in ops]
+    ready = {e: {} for e in "NVSPGY"}
+    for i in range(n):
+        if left[i] == 0:
+            ready[ops[i]["eng"]][i] = 0.0
+    free = {e: 0.0 for e in ready}
+    fin = [0.0] * n
+    order = []
+    while len(order) < n:
+        t0, e = min((max(free[e], min(c.values())), e) for e, c in ready.items() if c)
+        c = ready[e]
+        i = max((i for i in c if c[i] <= t0 + OPT["win"]), key=lambda i: (prio[i], -i))
+        if c[i] > t0 + 20.0:
+            fill = [j for j in c if max(c[j], t0) + ops[j]["cost"] <= c[i] + OPT["tol"]]
+            if fill:
+                i = max(fill, key=lambda j: (prio[j], -j))
+        st = max(t0, c.pop(i))
+        free[e] = st + ops[i]["cost"]
+        fin[i] = free[e] + ops[i]["lat"]
+        order.append((i, e, st))
+        for j in succ[i]:
+            left[j] -= 1
+            if left[j] == 0:
+                ready[ops[j]["eng"]][j] = max(fin[k] + gap(k, j) for k in ops[j]["deps"])
+    return order, max(fin)
+
+
+OTHER = "a128S a233S a234S a235V a236V a254V a262V a267V a301V a49V s103V s112S s113S s115S s116S s119S s122S s124S s127S s131S s135S s136S s138S s139S s147S s152V s34V s48S s54S s55V s80S s92S s94V"
+EARLIER = "a101:51 a102:129 a112:52 a118:57 a124:-42 a127:-45 a130:-5 a133:37 a134:39 a14:8 a142:252 a16:-39 a161:-29 a163:-33 a170:-87 a176:88 a181:28 a182:-39 a185:-50 a187:76 a188:93 a190:58 a191:62 a194:2 a2:145 a200:140 a206:80 a21:-38 a210:3 a213:2 a222:-30 a223:12 a226:-19 a230:20 a239:-48 a248:163 a249:168 a256:-49 a26:45 a261:1 a262:-91 a268:3 a269:3 a27:6 a28:-36 a280:-20 a281:30 a282:154 a286:312 a287:199 a295:-27 a296:-206 a300:-59 a31:-90 a37:-59 a4:93 a60:-86 a64:-56 a66:-59 a67:-62 a7:-12 a71:-38 a72:53 a74:-11 a77:-53 a81:-49 a82:-50 a86:-3 a88:46 a89:37 a90:-77 a92:15 a97:87 a98:62 a99:71 s1:-61 s103:-20 s108:-3 s109:-61 s11:-8 s114:-22 s117:8 s123:-3 s128:8 s129:-66 s14:-19 s153:-3 s157:-3 s159:-12 s166:20 s174:58 s176:111 s180:23 s181:31 s182:20 s183:82 s184:40 s185:32 s188:30 s195:70 s197:-58 s204:-8 s24:-3 s25:117 s26:62 s27:-3 s28:-3 s34:34 s36:50 s40:-50 s43:-8 s45:-11 s57:-42 s58:-8 s66:14 s69:31 s7:-8 s71:-20 s79:-66 s84:31 s85:42 s94:47 s97:-50"
+for _w in OTHER.split():
+    ASSIGN[_w[:-1]] = _w[-1]
+for _w in EARLIER.split():
+    BOOST[_w.split(":")[0]] = int(_w.split(":")[1])
+PLAN = []
+
+
+def rank_program(g, core, T, topo):
+    rank = T.rank_of(core)
+    if rank is None:
+        return
+    if not PLAN:
+        ops = build()[0]
+        PLAN.append((ops, schedule(ops)[0]))
+    ops, order = PLAN[0]
+    n = len(T.cores)
+    nxt, prv = T.cores[(rank + 1) % n], T.cores[(rank - 1) % n]
+    rid, pid = topo.addr(nxt, core)
+    eng = topo.engines(core, nxt)
+    mask = topo.mask(core, nxt)
+    narr = len(topo.engines(prv, core))
+    Qs = {"V": g.vector, "S": g.scalar, "P": g.tensor, "G": g, "Y": g.sync}
+
+    def ap(r):
+        if not isap(r):
+            return r
+        if r[0] == "ind":
+            return ap(r[1]).indirect(ap(r[2]))
+        if r[0] in ("in", "out"):
+            return T[r[1]][:] if len(r) == 2 else T[r[1]][:, r[2]:r[3]]
+        ps = slice(r[4], r[5], r[6]) if r[6] != 1 else slice(r[4], r[5])
+        nm, o = PLACE.get(r[0], (r[0], 0))
+        cs = slice(o + r[1], o + r[2], r[3]) if r[3] != 1 else slice(o + r[1], o + r[2])
+        return T[nm][ps, cs]
+
+    tok = {}
+    count = {"V": 0, "S": 0, "P": 0, "G": 0}
+    seen = {q: {} for q in Qs}
+    total = {}
+    for i, e, _ in order:
+        o = ops[i]
+        k, a = o["kind"], o["args"]
+        if k == "recv":
+            tok[i] = (a[0], narr); total[a[0]] = narr
+            continue
+        q = Qs[e]
+        need = {}
+        for j in o["deps"]:
+            if e == "P" and ops[j]["eng"] == "P":
+                continue
+            s, v = tok[j]
+            need[s] = max(need.get(s, 0), v)
+        for s, v in need.items():
+            if seen[e].get(s, 0) < v:
+                q.wait_ge(T.sem[s], v); seen[e][s] = v
+        if k == "send":
+            g.remote_dma(ap(a[1]), ap(a[0]), T.sem[a[2]], T.sem["sent"], pid, rid, mask)
+            total["sent"] = total.get("sent", 0) + len(eng)
+            continue
+        if k == "dma":
+            q.dma_start(ap(a[0]), ap(a[1])).then_inc(T.sem[a[2]], 16)
+            tok[i] = (a[2], 16); total[a[2]] = 16
+            continue
+        if k == "ts":
+            ins = q.tensor_scalar(ap(a[0]), ap(a[1]), ap(a[2]), None, a[4]) if a[5] is None else q.tensor_scalar(ap(a[0]), ap(a[1]), ap(a[2]), ap(a[3]), a[4], a[5])
+        elif k == "tt":
+            ins = q.tensor_tensor(ap(a[0]), ap(a[1]), ap(a[2]), a[3])
+        elif k == "cp":
+            ins = q.tensor_copy(ap(a[0]), ap(a[1])) if e == "V" else q.activation(ap(a[0]), ap(a[1]), AF.Copy)
+        elif k == "gcp":
+            ins = g.affine_select(ap(a[0]), ap(a[1]), [[0, cnt(a[0])]], OP.is_ge, 0.0, 0, 0)
+        elif k == "act":
+            ins = q.activation(ap(a[0]), ap(a[1]), a[2], ap(a[3]), ap(a[4]))
+        elif k == "scan":
+            ins = q.tensor_tensor_scan(ap(a[0]), ap(a[1]), ap(a[2]), a[3], a[4], a[5])
+        elif k == "tr":
+            ins = q.transpose(ap(a[0]), ap(a[1]))
+        elif k == "ms":
+            ins = q.memset(ap(a[0]), a[1])
+        elif k == "iota":
+            ins = g.iota(ap(a[0]), a[1], a[2], a[3], allow_small_or_imprecise_dtypes=True) if SB[a[0][0]][1] != I32 else g.iota(ap(a[0]), a[1], a[2], a[3])
+        else:
+            for out, terms in a[0]:
+                for x, (l, r) in enumerate(terms):
+                    ins = q.matmul(ap(out), ap(l), ap(r), a[1] and x == 0, a[2] and x == len(terms) - 1)
+        count[e] += 1
+        ins.then_inc(T.sem["c" + e], 1)
+        tok[i] = ("c" + e, count[e]); total["c" + e] = count[e]
+    for s, v in total.items():
+        if seen["G"].get(s, 0) < v:
+            g.wait_ge(T.sem[s], v)

@@ -4,57 +4,53 @@ from concourse.mybir import AluOpType as OP, ActivationFunctionType as AF
 HP = "float16"
 BF, F32, I32, U16 = "bfloat16", "float32", "int32", "uint16"
 VIS = 6
-BIG = float(1 << 21)
-MQ = 393216.0
-M16 = 1.5 * (1 << 27)
+BIG = float(1 << 23)
+MQ = 192
 M1 = 1.5 * (1 << 23)
-MEW, MFW = 320, 144
+QO = 49152.0
+MTW, M2W, AW, EQW = 136, 256, 336, 1040
+XP = 256 * (VIS - 1)
 
-PER_HALF = {
-    "GT": (2048, BF), "OFF": (128, U16), "SBI": (16, F32), "C15": (16, F32), "A32": (8, F32),
-    "NB": (128, BF), "EP": (1024, BF), "EQ": (1024, BF), "YL": (128, F32), "LQ": (128, BF), "MA": (128, BF), "MB": (128, BF), "KEY": (128, HP), "CL": (1024, HP),
-    "VI": (64, I32), "RL": (128, I32), "PR": (128, F32), "SM": (128, I32), "SM2": (128, I32), "POFF": (128, U16),
-    "VV": (64, I32), "KA": (128, BF), "GO": (1024, BF), "DD": (1024, BF), "AB": (1024, BF),
-    "KT": (192, F32), "KS": (192, F32), "KI": (8, I32), "FL": (16, I32), "P2": (16, F32), "S2": (16, I32), "S3": (16, I32),
-    "EF": (16, HP), "DOFF": (16, U16), "UY": (8, I32), "UQ": (8, F32), "UM": (8, I32), "UN": (8, I32), "US": (8, I32),
-    "MST": (128, BF), "MG": (128, BF), "MR": (128, BF), "FO": (128, BF), "FD": (128, BF), "GE": (128, BF), "MQB": (128, BF),
-    "AT": (1024, BF), "WS": (1024, BF),
+PER_STREAM = {
+    "TO": (2048, F32), "TV": (2048, F32), "W": (XP + 128 * VIS, F32),
+    "WZ": (512, BF), "WN": (384, BF), "ZO": (128, BF), "ZV": (128, BF), "ZM": (128, F32),
+    "MS": (MTW * VIS, HP), "ML": (MTW * (VIS + 1), HP), "M2": (M2W * VIS, BF), "L2": (192 * (VIS + 1), BF),
+    "Q": (128, BF), "OFF": (128, U16), "G1": (2048, HP), "NB": (128, HP), "NH": (128, BF), "EP": (1024, BF), "EQ": (2 * EQW, BF),
+    "YL": (128, F32), "LQ": (128, BF), "MK": (128, BF), "PD": (128, F32), "XI": (128, I32), "XJ": (128, I32), "POFF": (128, U16),
+    "DD": (2048, BF), "AB": (2048, BF), "KS": (128, I32), "KA": (8, I32), "DOFF": (8, U16), "DFI": (AW, BF), "GE": (128, BF), "BB": (128, BF),
+    "UY": (8, I32), "UQ": (8, F32), "UM": (8, I32), "UX": (8, I32), "UC": (8, I32), "XF": (8, F32), "HIP": (8, F32), "HI": (64, BF), "LO": (1024, BF),
+    "FF": (8, I32), "DC": (8, I32), "DC2": (8, I32), "US": (8, I32), "SA": (8, F32), "RT": (96, HP), "DT": (128, HP),
+    "WL": (72, F32), "WE": (72, F32), "ST": (72, F32), "POS": (8, U16), "SF": (8, F32), "SEL": (8, U16), "AC": (AW, BF),
+    "ZN": (128, BF), "PZ": (128, HP),
 }
-SB = {k: (2 * w, d) for k, (w, d) in PER_HALF.items()}
+SB = {"%s%d" % (k, s): v for k, v in PER_STREAM.items() for s in range(2)}
 SB.update({
-    "LO": (2048, BF), "LV": (2048, BF), "TT": (2048, BF), "XI": (128, BF), "Z0": (256, BF),
-    "EN": (384, F32), "EA": (384, F32), "EAG": (128, F32), "ET": (256, F32), "QB": (512, BF), "MT": (64, HP),
-    "SI": (16, F32), "CI": (16, I32), "CA": (16, I32), "CA2": (16, I32), "DPW": (384, BF), "DNW": (384, BF),
-    "T0": (8, F32), "T1": (8, F32), "SL": (8, F32), "LOWU": (8, U16), "LOW2": (8, U16), "SELU": (8, U16),
-    "DE": (128, BF), "ZA": (384, BF), "ZAG": (128, BF), "ZW": (384 * VIS, BF),
-    "MES": (MEW * VIS, HP), "MEL": (MEW * VIS, HP), "MFS": (MFW * VIS, BF), "MFL": (MFW * VIS, BF), "ZL": (256 * VIS, BF),
-    "XW": (768, BF), "STT": (256, BF), "BT": (128, BF), "AA": (256, BF), "HH": (256, BF), "YN": (768, F32), "YX": (128, BF), "YC": (256, F32),
-    "NROW": (2048, BF), "NMI": (128, I32), "NMB": (128, BF), "CSI": (256, I32), "CSF": (256, F32), "SA": (2048, BF), "SH": (2048, BF),
-    "IO1": (160, F32), "PI": (8, I32), "PJ": (8, I32), "COL": (32, F32), "ONES": (128, BF), "NH": (256, BF),
-    "DG": (896, BF), "FQ": (256, HP), "WID": (576, BF), "O256H": (144, HP), "TH": (128, BF), "N8": (128, BF),
-    "BM": (128, BF), "BO": (128, BF), "TRI": (256, BF), "M0": (128, BF), "TMP": (384, F32), "RC": (128, F32),
-    "E0M": (128, F32), "CM": (512, F32), "WD": (320, HP), "EXB": (512, HP), "EX": (4096, HP),
-    "SQ": (512, F32), "SK": (1024, BF), "BIGM": (2048, BF), "RS": (192, F32), "RW": (512, BF), "TG": (32, F32),
+    "LO": (2048, BF), "LV": (2048, BF), "XO": (128, BF), "Z0": (256, BF), "NI": (256, I32), "NJ": (256, I32), "NP": (256, BF), "CI": (256, I32),
+    "QD": (256, BF), "YO": (768, BF), "YV": (768, BF), "YN": (768, F32), "NW": (256, BF), "YZ": (256, BF), "YQ": (64, BF), "YC": (64, F32),
+    "PI": (8, I32), "PJ": (16, I32), "COL": (64, F32), "IO": (160, F32), "I3": (128, I32), "J3": (256, I32), "K3": (384, BF), "K4": (256, BF), "TMP": (1344, F32),
+    "ONE": (128, BF), "ZERO": (EQW, BF), "CST": (128, BF), "QOT": (256, HP), "NF": (8, BF), "ID": (128, BF), "NID": (128, BF), "HID": (128, BF), "IH": (128, HP), "IF": (128, F32),
+    "REP": (128, BF), "NS": (16, HP), "P8": (8, BF), "WB": (144, BF), "SK": (256, BF), "BM": (1024, BF), "BD": (1024, HP), "BN": (128, BF), "NM": (2048, BF),
+    "RE": (128, HP), "RS": (128, HP), "RX": (128, HP), "RA": (8, HP), "OM": (120, HP), "JT": (128, HP), "RK": (64, F32), "TX": (128, BF),
+    "YT": (64, F32), "HL": (8, U16), "MTAB": (8, F32), "NBT": (128, BF), "NN": (8, BF), "OH": (16, F32),
 })
 PLACE = {}
 _fill = {}
 for _k, (_w, _d) in SB.items():
-    if _w <= 64:
+    if _w <= 128:
         PLACE[_k] = ("pk" + _d, _fill.get(_d, 0))
         _fill[_d] = _fill.get(_d, 0) + (_w + 15) // 16 * 16
     else:
         PLACE[_k] = (_k, 0)
-SCRATCH = {k: ("sbuf", [128, w], d) for k, (w, d) in SB.items() if w > 64}
+SCRATCH = {k: ("sbuf", [128, w], d) for k, (w, d) in SB.items() if w > 128}
 for _d, _w in _fill.items():
     SCRATCH["pk" + _d] = ("sbuf", [128, _w], _d)
 for _i in range(8):
     SCRATCH["PS%d" % _i] = ("psum", [128, 512], F32)
-DMAS = ["d%d" % i for i in range(24)]
-SEMAPHORES = ["cV", "cS", "cP", "cG", "sent"] + DMAS + ["%s%d" % (k, t) for k in ("aE", "aF", "aZ") for t in range(VIS)]
+DMAS = ["d%d" % i for i in range(100)]
+SEMAPHORES = ["cV", "cS", "cP", "cG", "sent"] + DMAS + ["a%s%d%d" % (k, s, t) for k in "MX" for s in range(2) for t in range(VIS)]
 
-PM = {"cy": 1.04, "hop": 110.0, "pe": 0.6, "ga": 1.56, "sc": 3.8, "link": 2600.0, "issue": 400.0, "fix": 0.0}
-OPT = {"eq": "VVMM", "win": 150.0, "tol": 30.0}
-ASSIGN = {}
+PM = {"cy": 1.04, "hop": 110.0, "pe": 0.6, "ga": 1.56, "sc": 3.8, "link": 2600.0, "issue": 400.0, "dma": 2200.0}
+OPT = {"seed": 1, "tries": 2600, "lead": 8500.0, "win": 200.0, "tol": 30.0, "g1": "S2 V2 S2 S2", "eq": "MV", "floor": "SS", "q": "S", "lq": "SS", "mk": "S", "g2": ((0, 256, 512, 1024), (0, 512, 768, 1024)), "zn": "S", "dt": "S", "tw": "SSSS", "we": "S", "dq": "S", "evac": "VSVS", "bm": "VVS", "nm": "VVS", "rt": "S"}
 BOOST = {}
 
 
@@ -94,10 +90,9 @@ def build():
     ops = []
     hist = {}
     bank = {}
-    phase = ["s", 0]
-    when = [0]
-    flex = {}
-    CY, FIX = PM["cy"], PM["fix"]
+    tag = ["set-up"]
+    nth = {}
+    CY = PM["cy"]
 
     def add(who, cost, kind, args, reads, writes, lat=0.0, extra=()):
         i = len(ops)
@@ -111,13 +106,13 @@ def build():
         for isw, lst in ((False, flat(reads)), (True, wr)):
             for r in lst:
                 h = hist.setdefault(r[0], [])
-                lo, hi = r[1], r[2]
-                for (j, w2, a, b) in h:
-                    if j != i and (isw or w2) and a < hi and lo < b:
+                lo, hi, pl, ph = r[1], r[2], r[4], r[5]
+                for (j, w2, a, b, c, d) in h:
+                    if j != i and (isw or w2) and a < hi and lo < b and c < ph and pl < d:
                         deps.add(j)
-                if isw:
-                    h[:] = [e for e in h if not (lo <= e[2] and e[3] <= hi and r[3] == 1 and r[4] == 0 and r[5] == 128 and r[6] == 1)]
-                h.append((i, isw, lo, hi))
+                if isw and r[3] == 1 and r[6] == 1:
+                    h[:] = [e for e in h if not (lo <= e[2] and e[3] <= hi and pl <= e[4] and e[5] <= ph)]
+                h.append((i, isw, lo, hi, pl, ph))
                 if r[0].startswith("PS"):
                     st = bank.setdefault(r[0], [None, [], []])
                     if st[0] != who:
@@ -127,17 +122,10 @@ def build():
                         deps.update(st[1][-1:] if i not in st[1] else [])
                     if i not in st[1]:
                         st[1].append(i)
-        ops.append({"eng": who, "cost": cost, "kind": kind, "args": args, "deps": deps, "lat": lat, "t": when[0],
-                    "key": "%s%d" % ("c" if phase[0] == "a" and when[0] == 0 else phase[0], phase[1])})
-        phase[1] += 1
+        ops.append({"eng": who, "cost": cost, "kind": kind, "args": args, "deps": deps, "lat": lat, "tag": tag[0]})
+        nth[tag[0]] = nth.get(tag[0], 0) + 1
+        ops[-1]["key"] = "%s%d" % (tag[0].split()[-1], nth[tag[0]])
         return i
-
-    def pick(e):
-        if len(e) == 1:
-            return e
-        k = "%s%d" % tuple(phase)
-        flex[k] = e
-        return ASSIGN.get(k, e[0])
 
     def vcost(out, ins, tt=False):
         n = cnt(out)
@@ -149,10 +137,10 @@ def build():
             rate = 1.0 if any(x[0].startswith("PS") for x in ins) else 2.0
         else:
             rate = 0.5 if two(out) and all(two(x) for x in ins) else 1.0
-        return max(64, n * rate) * CY + FIX
+        return max(64, n * rate) * CY
 
     def scost(out, in_):
-        return (65 + PM["ga"] * cnt(out) * CY) if in_[0] == "ind" else max(64, cnt(out)) * CY + FIX
+        return (65 + PM["ga"] * cnt(out) * CY) if in_[0] == "ind" else max(64, cnt(out)) * CY
 
     def ts(out, in0, s1, op0, s2=None, op1=None):
         return add("V", vcost(out, [in0]), "ts", (out, in0, s1, s2, op0, op1), [in0, s1, s2], [out])
@@ -161,55 +149,40 @@ def build():
         return add("V", vcost(out, [a, b], True), "tt", (out, a, b, op), [a, b], [out])
 
     def cp(out, in_, e="V"):
-        e = pick(e)
-        if e == "G":
-            return add(e, 170 + 2 * cnt(out) * CY, "gcp", (out, in_), [in_], [out])
         return add(e, vcost(out, [in_]) if e == "V" else scost(out, in_), "cp", (out, in_), [in_], [out])
 
-    def act(out, in_, f, bias=0.0, scale=1.0):
-        return add("S", scost(out, in_), "act", (out, in_, f, bias, scale), [in_, bias, scale], [out])
+    def act(out, in_, f, bias=0.0, scale=1.0, more=0.0, after=()):
+        return add("S", scost(out, in_) + more, "act", (out, in_, f, bias, scale), [in_, bias, scale], [out], 0.0, after)
 
-    def aff(out, in_, scale, bias=0.0, e="VS"):
-        return ts(out, in_, scale, OP.mult, bias, OP.add) if pick(e) == "V" else act(out, in_, AF.Identity, bias, scale)
-
-    def relu(out, in_, scale, e):
-        return ts(out, in_, scale, OP.mult, 0.0, OP.max) if pick(e) == "V" else act(out, in_, AF.Relu, 0.0, scale)
+    def aff(out, in_, scale, bias=0.0, e="V"):
+        return ts(out, in_, scale, OP.mult, bias, OP.add) if e == "V" else act(out, in_, AF.Identity, bias, scale)
 
     def scan(out, d0, d1, init, op0, op1):
         return add("V", vcost(out, [d0, d1]), "scan", (out, d0, d1, init, op0, op1), [d0, d1], [out])
 
-    def tr(out, in_):
-        return add("V", vcost(out, [in_]), "tr", (out, in_), [in_], [out])
-
     def ms(out, v):
+        if not out[0].startswith("PS") and SB[out[0]][1] == HP:
+            return ts(out, R("ONE", 0, cnt(out), 1, out[4], out[5]), v, OP.mult)
         return add("V", vcost(out, []), "ms", (out, v), [], [out])
 
-    def iota(out, pat, base, cm):
+    def iota(out, pat, base, cm=0):
         return add("G", 130 + 2 * cnt(out) * CY, "iota", (out, pat, base, cm), [], [out])
 
     def mm(groups, start=True, stop=True):
         c = 0; rd = []; wr = []
         for out, terms in groups:
-            wr.append(out)
-            for l, r in terms:
-                c += max(64, cnt(r)) * (4 if SB[r[0]][1] == F32 else 1) * PM["pe"]
+            for x in terms:
+                l, r = x[0], x[1]
+                wr.append(x[2] if len(x) > 2 else out)
+                c += max(min(64, cnt(l)), cnt(r)) * (4 if SB[r[0]][1] == F32 else 1) * PM["pe"]
                 rd += [l, r]
         return add("P", c, "mm", (groups, start, stop), rd, wr)
 
-    def mms(out, terms, cuts):
-        e = [0] + cuts + [len(terms)]
-        for x in range(len(e) - 1):
-            mm([(out, terms[e[x]:e[x + 1]])], x == 0, x == len(e) - 2)
-
     nd = [0]
 
-    def load(q, out, in_, lat=2200.0):
+    def dma(q, out, in_, lat=None):
         nd[0] += 1
-        return add(q, 60.0, "dma", (out, in_, DMAS[nd[0] - 1]), [in_] if in_[0] != "in" else [], [out], lat)
-
-    def store(q, out, in_):
-        nd[0] += 1
-        return add(q, 60.0, "dma", (out, in_, DMAS[nd[0] - 1]), [in_], [], 2200.0)
+        return add(q, 60.0, "dma", (out, in_, DMAS[nd[0] - 1]), [in_] if in_[0] != "in" else [], [out] if out[0] != "out" else [], lat or PM["dma"])
 
     def send(name, src, dst):
         i = add("G", PM["issue"], "send", (src, dst, name), [src], [])
@@ -217,373 +190,374 @@ def build():
 
     A, S_, Mu, Mx, Mn = OP.add, OP.subtract, OP.mult, OP.max, OP.min
     EQL, AND, SHR = OP.is_equal, OP.bitwise_and, OP.arith_shift_right
-    col = lambda j, p1=128: R("COL", j, j + 1, p1=p1)
+    col = lambda j, p0=0, p1=128: R("COL", j, j + 1, p0=p0, p1=p1)
     blk = lambda n, j: R(n, 128 * j, 128 * j + 128)
-    ID, NID, HID, QID, KD, CD, BD = (blk("DG", j) for j in range(7))
-    ONES = R("ONES")
-    wide = lambda j, r: R("WID", 144 * j + 16 - r, 144 * j + 144 - r)
-    whole = lambda j: R("WID", 144 * j, 144 * j + 144)
+    ID, NID, HID, IH, IF, REP, ONE = (R(n) for n in ("ID", "NID", "HID", "IH", "IF", "REP", "ONE"))
+    wide = lambda b: R("WB", 16 - b, 144 - b)
+    half = lambda n, s, a, b, st=1: R(n, a, b, st, 64 * s, 64 * s + 64)
+    banks = lambda s: ["PS%d" % (4 * s + j) for j in range(4)]
 
-    load("Y", R("NMI"), ("in", "nm"))
-    ms(R("CSI"), 0)
-    for q in range(2):
-        load("S", R("LO", 1024 * q, 1024 * q + 1024), ("in", "vo", 1024 * q, 1024 * q + 1024), 3000.0)
-        load("Y", R("LV", 1024 * q, 1024 * q + 1024), ("in", "vn", 1024 * q, 1024 * q + 1024), 3000.0)
-    load("Y", R("CSI", p0=0, ps=16), ("in", "c0"))
-    load("Y", R("CSI", p0=1, ps=16), ("in", "s0"))
-    cp(R("NMB"), R("NMI"))
-    load("Y", R("NROW", p1=8), R("NMB"))
-    load("Y", R("XI"), ("in", "xo"))
-    load("Y", R("Z0"), ("in", "z0"))
-
-    iota(R("PI", 0, 1), [[0, 1]], 0, 1)
-    iota(R("IO1"), [[1, 160]], -16, 0)
-    iota(R("RC"), [[0, 8], [1, 16]], 0, 0)
-    iota(blk("SQ", 0), [[1, 16], [0, 8]], 0, 0)
-    iota(blk("SQ", 1), [[1, 16], [-1, 8]], -1, 0)
-    iota(blk("SQ", 2), [[1, 16], [1, 8]], 1, 0)
-    iota(blk("SQ", 3), [[0, 16], [-1, 8]], 14, 0)
-    iota(R("TG", 16, 24), [[16, 8]], 1, 0)
-    iota(R("TG", 24, 32), [[0, 2], [16, 4]], 0, 0)
-    iota(R("TG", 0, 8), [[1, 2], [32, 4]], 0, 0)
-    iota(R("STT", 0, 64), [[2, 64]], 0, 0)
-    iota(R("STT", 128, 192), [[2, 64]], 1, 0)
-    PI = R("PI", 0, 1)
-    PJ = lambda j: R("PJ", j, j + 1)
-    cp(col(0), PI)
-    ts(PJ(0), PI, 15, AND); cp(col(1), PJ(0))
-    tt(col(2), col(0), col(1), S_)
-    ts(col(3), col(1), 0.0, EQL); ts(col(4), col(1), 1.0, EQL); ts(col(6), col(1), 2.0, EQL)
-    tt(col(5), col(4), col(6), A); tt(col(9), col(4), col(3), S_)
-    aff(col(7), col(1), 17.0 / 256 - 1.0, -32.5, "SV"); aff(col(8), col(1), -17.0, 255.0, "SV")
-    ts(PJ(1), PI, 4, SHR, 1, AND); cp(col(10), PJ(1)); aff(col(11), col(10), -1.0, 1.0, "SV")
-    ts(PJ(2), PI, 1, SHR, 7, AND); cp(col(12), PJ(2))
-    ts(PJ(3), PI, 1, AND); ts(PJ(4), PI, 96, AND)
-    ts(col(14), PJ(3), 16.0, Mu); tt(col(13), col(14), PJ(4), A)
-    C0 = R("IO1", 16, 144)
-    ts(ID, C0, col(0), EQL); aff(NID, ID, -1.0)
-    ms(ONES, 1.0)
-    ts(whole(0), R("IO1", 0, 144), col(2), EQL)
-    aff(whole(1), whole(0), col(3)); ts(whole(2), whole(0), col(5), Mu, 256.0, Mu)
-    TA, TH = wide(0, 2), R("TH")
-    tt(TH, wide(0, 1), TA, S_)
-    ts(R("N8", p1=32), R("IO1", 16, 144, p1=32), 1.0 / 16, Mu, col(0, 32), EQL)
-    tt(blk("TMP", 1), C0, R("RC"), S_)
-    ts(R("BM"), blk("TMP", 1), col(2), EQL)
-    aff(R("M0"), R("BM"), col(3))
-    aff(blk("TMP", 0), R("RC"), col(4), col(3), "SV"); tt(R("E0M"), blk("TMP", 0), R("BM"), Mu)
-
-    def floor_mod(ps, dst, q):
-        act(R("QB", q, q + 256), R(ps, 0, 256), AF.Identity, MQ - 1023.625)
-        tt(R(dst, 0, 256), R(ps, 0, 256), R("QB", q, q + 256), S_)
-
-    cp(R("CSF"), R("CSI"))
-    mm([(R("PS0", 0, 256), [(R("E0M"), R("CSF"))])])
-    floor_mod("PS0", "EN", 0)
-    for q in range(4):
-        a, b = 512 * q, 512 * q + 512
-        mm([(R("PS%d" % (2 + q % 2)), [(ID, R("LV", a, b)), (NID, R("LO", a, b))])])
-        act(R("SA", a, b), R("PS%d" % (2 + q % 2)), AF.Abs)
-        ts(R("SH", a, b), R("SA", a, b), M16, A, M16, S_)
-        mm([(R("PS%d" % (4 + q)), [(TA, R("SA", a, b)), (TH, R("SH", a, b)), (R("N8", p1=8), R("NROW", a, b, p1=8))])])
-        cp(R("TT", a, b), R("PS%d" % (4 + q)), "VS" if q % 2 else "SV")
-
-    K = lambda j: blk("SK", j)
-    Q = lambda j: blk("SQ", j)
-    ts(K(0), Q(0), col(1), EQL); ts(K(1), Q(1), col(1), EQL); ts(K(2), Q(1), 16.0, A, col(1), EQL)
-    ts(K(3), Q(2), col(1), EQL); ts(K(4), Q(2), -16.0, A, col(1), EQL); ts(K(5), Q(3), col(1), OP.is_ge)
-    tt(K(3), K(3), K(4), A); tt(K(3), K(0), K(3), S_)
-    tt(K(5), K(5), K(0), Mu)
-    tt(K(1), K(1), K(0), A); tt(K(1), K(1), K(5), S_)
-    aff(K(1), K(1), float(4 ** 17))
-    for d in range(8):
-        v = lambda j: R("SK", 128 * j + d, 128 * j + 128, 8)
-        aff(v(6), v(5), float(4 ** (d + 1)), 0.0, "SV"); aff(v(7), v(2), float(4 ** (15 - d)), 0.0, "SV")
-    tt(K(6), K(6), K(7), A); tt(K(6), K(6), K(1), A)
-    for gq in range(8):
-        ts(col(16 + gq), col(2), 16.0 * gq, EQL)
-        for j, src in enumerate((3, 6)):
-            aff(blk("BIGM", 8 * j + gq), K(src), col(16 + gq))
-    BMX = lambda j, d: R("BIGM", 1024 * j + d, 1024 * j + 1024, 8)
-
-    aff(HID, ID, 0.5); aff(QID, ID, 1.0 / 256); aff(KD, ID, col(8)); aff(CD, ID, 1152.0); aff(BD, ID, -BIG)
-    ts(blk("FQ", 0), ID, 0.25, Mu); ts(blk("FQ", 1), ID, col(6), Mu)
-    aff(whole(3), whole(0), 256.0); ts(R("O256H"), whole(0), 256.0, Mu)
-    aff(R("BO"), R("BM"), -128.0)
-    TRI, TRH = blk("TRI", 0), blk("TRI", 1)
-    ts(blk("TMP", 2), C0, col(0), OP.is_gt); tt(blk("TMP", 2), blk("TMP", 2), R("BM"), Mu)
-    aff(TRI, ID, 16.0); tt(TRI, TRI, blk("TMP", 2), A); aff(TRH, TRI, 0.5)
-    for kh in range(2):
-        ts(blk("TMP", 0), R("RC"), 7.5, OP.is_gt if kh else OP.is_lt); tt(blk("TMP", 0), blk("TMP", 0), R("BM"), Mu)
-        aff(blk("CM", kh), blk("TMP", 0), col(3), 0.0, "SV"); aff(blk("CM", 2 + kh), blk("TMP", 0), col(9), 0.0, "SV")
-        ts(R("WD", 160 * kh, 160 * kh + 160), R("IO1"), col(0), EQL, col(10 if kh else 11), Mu)
-    ts(blk("TMP", 1), blk("TMP", 1), col(13), EQL)
-    for j in range(4):
-        e = blk("EXB", j)
-        if j == 0: ts(e, R("RC"), col(10), Mu, 1.0, A)
-        if j == 1: ts(e, R("RC"), col(10), Mu, col(11), A)
-        if j == 2: ts(e, R("RC"), col(10), OP.is_le)
-        if j == 3: ts(e, R("RC"), col(10), EQL)
-        tt(e, e, blk("TMP", 1), Mu)
-        for b in range(8 if j < 2 else 0):
-            if j == 0: ts(col(24 + b), col(12), float(b), EQL)
-            ts(blk("EX", 8 * j + b), e, col(24 + b), Mu)
-    ms(R("NH"), -0.5); ms(R("MST"), 0.0)
-    for n in ("DPW", "DNW", "EA", "ZA"):
-        ms(R(n, 256, 384), 0.0)
-    ms(R("RS"), 0.0); ms(R("RS", 0, 128, 16), -4 * BIG); ms(R("RS", 128, 192, 8), -4 * BIG)
-    ms(R("RW"), -1.0); ms(R("RW", 0, 512, 128), 1024.0)
-    ts(R("TG", 16, 32), R("TG", 16, 32), col(1), A)
-    aff(col(15), col(1), 2.0, 0.0, "SV"); ts(R("TG", 0, 8), R("TG", 0, 8), col(15), A); aff(R("TG", 8, 16), R("TG", 0, 8), -512.0, 0.0, "SV")
-    for par in range(2):
-        aff(R("STT", 128 * par, 128 * par + 64), R("STT", 128 * par, 128 * par + 64), col(3), 0.0, "SV")
-        cp(R("XW", 384 * par + 64, 384 * par + 128), R("XI", par, 128, 2), "SV")
-        aff(R("XW", 384 * par, 384 * par + 64), R("XI", par, 128, 2), -1.0, 255.0, "SV")
-
-    def read_half(h, ME, ZC):
-        pA, pB, pC, pD = ("PS%d" % (4 * h + j) for j in range(4))
-
-        def H(n, a=0, b=None, s=1):
-            w = PER_HALF[n][0]
-            return R(n, w * h + a, w * h + (w if b is None else b), s)
-
-        for j in range(2):
-            mm([(R(pD, 64 * j, 64 * j + 64), [(blk("CM", 2 * j + kh), R("EN", 128 * h + 64 * kh, 128 * h + 64 * kh + 64)) for kh in range(2)])])
+    ms(R("CI", p1=64), 0)
+    ms(ONE, 1.0)
+    for s in range(2):
+        for pc in range(2):
+            dma("YS"[pc], half("NI", pc, 128 * s, 128 * s + 128), ("in", "nm", 4 * s, 4 * s + 4))
         for q in range(2):
-            mm([(R(pC, 64 * q, 64 * q + 64), [(wide(1, r), H("GT", 1024 * q + r, 1024 * q + 1024, 16)) for r in range(16)])])
-        cp(H("NB"), R(pC, 0, 128), "SV")
-        for j, pq in enumerate((pA, pB)):
-            mm([(R(pq, 128 * d, 128 * d + 128), [(BMX(0, 4 * j + d), H("NB"))]) for d in range(4)])
-            eq, ep = H("EQ", 512 * j, 512 * j + 512), H("EP", 512 * j, 512 * j + 512)
-            mode = OPT["eq"][2 * h + j]
-            phase[1] += 1 if mode == "V" else 0
-            if mode == "V":
+            dma("YS"[q], half("LO", s, 1024 * q, 1024 * q + 1024), ("in", "vo", 64 * s, 64 * s + 64, 1024 * q, 1024 * q + 1024), 2600.0)
+        for gq in range(4 * s, 4 * s + 4):
+            dma("Y", R("CI", 32 * gq, 32 * gq + 32, p0=0, p1=8), ("in", "c0", gq, gq + 1))
+            dma("S", R("CI", 32 * gq, 32 * gq + 32, p0=32, p1=40), ("in", "s0", gq, gq + 1))
+        dma("Y", half("LV", s, 0, 2048), ("in", "vn", 64 * s, 64 * s + 64), 3000.0)
+    dma("Y", R("XO"), ("in", "xo", 0, 128))
+    dma("Y", R("Z0"), ("in", "z0", 0, 128))
+
+    PI = R("PI", 0, 1)
+    iota(PI, [[0, 1]], 0, 1)
+    iota(R("IO"), [[1, 160]], -16)
+    C0 = R("IO", 16, 144)
+    T_ = lambda j: blk("TMP", j)
+    cp(col(0), PI)
+    for j, (sh, mk) in enumerate(((0, 15), (0, 112), (0, 63), (6, 1), (0, 7), (3, 15), (0, 48))):
+        ts(R("PJ", j, j + 1), PI, sh, SHR, mk, AND)
+    cp(R("COL", 1, 8), R("PJ", 0, 7))
+    tt(col(8), col(7), col(4), A)
+    iota(T_(0), [[0, 2], [1, 64]], 0)
+    ts(REP, T_(0), col(3), EQL)
+    ts(R("BN"), T_(0), col(8), EQL, 256.0, Mu)
+    ts(R("COL", 16, 32), R("IO", 16, 32), col(1), EQL)
+    for eh in range(16):
+        aff(blk("NM", eh), R("BN"), col(16 + eh), 0.0, OPT["nm"][eh % len(OPT["nm"])])
+    ts(half("NJ", 0, 0, 256), half("NI", 0, 0, 256), 7, AND); ts(half("NJ", 1, 0, 256), half("NI", 1, 0, 256), 3, SHR)
+    ts(col(34), col(4), -0.5, Mu, -7.5, A); ts(R("NP"), R("NJ"), col(34), A)
+    oh = lambda j: R("OH", j, j + 1)
+    ts(R("OH"), R("IO", 16, 32), col(6), EQL)
+    tt(col(9), oh(2), oh(4), A)
+    tt(col(10), oh(0), oh(1), A); tt(col(10), col(10), oh(12), S_); ts(col(11), oh(2), 16.0, Mu, col(10), A)
+    ts(col(12), col(0), 40.0, EQL, 2048.0, Mu); ts(col(13), col(0), 41.0, EQL, -1369.0, Mu)
+    tt(col(14), oh(3), oh(8), S_)
+    ts(col(15), col(12), MQ / 2048.0, Mu); ts(col(32), col(13), -256.0 / 1369.0, Mu, col(15), A)
+    iota(T_(1), [[1, 8], [0, 16]], 0); iota(T_(2), [[0, 8], [-1, 16]], 15)
+    ts(T_(1), T_(1), col(5), EQL)
+    ts(T_(2), T_(2), col(9), Mu, col(11), A); tt(T_(2), T_(2), T_(1), Mu); ts(R("RE"), T_(2), col(12), A)
+    ts(R("RS"), T_(1), col(9), Mu); ts(R("RX"), R("RS"), -144.0, Mu)
+    ts(R("TMP", 1008, 1016), R("TMP", 128, 256, 16), col(14), Mu, 32.0, Mu); ts(R("RA"), R("TMP", 1008, 1016), col(13), A)
+    ts(ID, C0, col(0), EQL); aff(NID, ID, -1.0); aff(HID, ID, 0.5); cp(IH, ID); cp(IF, ID, "S")
+    for s in range(2):
+        ms(half("ML%d" % s, 1, 0, 128), 0.0)
+        for h in range(2):
+            ts(half("ML%d" % s, 0, 64 * h, 64 * h + 64), half("CI", 0, 128 * s + h, 128 * s + 128, 2), col(32, 0, 64), A)
+
+    def table(s, dst, src, qs):
+        for q in qs:
+            ps = banks(s)[2 + q % 2]
+            mm([(R(ps), [(half("REP", s, 0, 128), half(src, s, 512 * q, 512 * q + 512))] +
+                 [(blk("NM", 4 * q + j), blk("NP", s), blk(ps, j)) for j in range(4)])])
+            cp(R(dst, 512 * q, 512 * q + 512), R(ps), OPT["evac"][q])
+
+    table(0, "TO0", "LO", range(4))
+
+    U = lambda a, b, st=1: R("TMP", 1280 + a, 1280 + b, st)
+    iota(U(0, 16), [[1, 2], [16, 8]], 0)
+    ts(R("NS", 0, 8), U(0, 8), col(0), EQL, (1 - 2.0 ** -11) / 256, Mu); ts(R("NS", 8, 16), U(8, 16), col(0), EQL, 1.0 / 256, Mu)
+    ts(R("P8"), U(0, 8), col(0), EQL)
+    ts(R("NN"), U(8, 16), col(0), EQL, 8.0, Mu); tt(R("NN"), R("NN"), R("P8"), A); ts(R("NN"), R("NN"), 1.0 / 256, Mu)
+    ts(R("WB"), R("IO", 0, 144), col(2), EQL, 2048.0, Mu)
+    iota(U(16, 24), [[0, 2], [-16, 4]], 43); ts(U(16, 24), U(16, 24), col(1), S_)
+    ts(col(33), col(1), -2.0, Mu, 43.0, A); tt(U(24, 25), col(33), col(4), S_)
+    e1 = act(U(32, 41), U(16, 25), AF.Exp, 0.0, 1.0, 1300.0)
+    iota(T_(3), [[1, 16], [0, 8]], 0); iota(T_(4), [[1, 16], [1, 8]], -7); iota(T_(5), [[-1, 16], [1, 8]], -7)
+    iota(T_(6), [[0, 16], [-1, 8]], 115); iota(T_(7), [[-1, 16], [2, 8]], 102)
+    K3 = lambda j: blk("K3", j)
+    ts(col(35), col(1), -1.0, Mu)
+    ts(K3(0), T_(3), col(1), EQL)
+    act(T_(3), T_(4), AF.Abs, col(35)); ts(K3(1), T_(3), 8.0, EQL)
+    act(T_(5), T_(5), AF.Abs, col(1)); ts(K3(2), T_(5), 8.0, EQL)
+    tt(blk("SK", 0), K3(0), K3(1), S_)
+    ts(T_(4), T_(4), 7.5, OP.is_lt, 16.0, Mu); tt(T_(4), T_(4), T_(6), A); tt(T_(4), T_(4), K3(0), Mu)
+    act(T_(7), T_(7), AF.Identity, col(1)); tt(T_(7), T_(7), K3(2), Mu); tt(T_(4), T_(4), T_(7), A)
+    ts(R("TMP", 512 + 7, 640, 8), R("TMP", 512 + 7, 640, 8), -math.log(2.0), A)
+    act(blk("SK", 1), T_(4), AF.Exp, -100.0, after=[e1])
+    ts(R("COL", 36, 44), U(0, 8), col(2), EQL)
+    for gq in range(8):
+        for j, k in enumerate(("BD", "BM")):
+            aff(blk(k, gq), blk("SK", j), col(36 + gq), 0.0, OPT["bm"][(2 * gq + j) % len(OPT["bm"])])
+    table(0, "TV0", "LV", range(4))
+    table(1, "TO1", "LO", range(4))
+    iota(T_(8), [[16, 128]], 0); act(R("JT"), T_(8), AF.Identity, col(1))
+    ms(R("RK"), 0.0); ms(R("RK", 0, 64, 16), -16 * BIG)
+    ms(R("CST"), -0.5); iota(R("NF"), [[0, 8]], -15360); iota(R("ZERO"), [[0, EQW]], 0)
+    ts(col(47), col(16), 128.0, Mu, QO, A); act(R("QOT"), R("ZERO", 0, 256), AF.Identity, col(47))
+    iota(T_(9), [[0, 2], [64, 4], [1, 16]], 0)
+    ts(col(48), col(7), -4.0, Mu); act(R("TX"), T_(9), AF.Identity, col(48))
+    iota(R("YT"), [[0, 8], [1, 2], [32, 4]], 0)
+    iota(U(48, 52), [[2, 4]], 0); ts(col(44), col(1), 7.5, OP.is_gt); ts(R("HL", 0, 4), U(48, 52), col(44), A)
+    ts(col(45), col(1), 2.0, Mu); ts(R("MTAB"), R("YT", 0, 8), col(45), A)
+    ts(col(46), col(4), -1.0, Mu, 44.47, A)
+    iota(R("I3"), [[1, 128]], 0)
+    ts(blk("J3", 0), R("I3"), 7, AND); ts(blk("J3", 1), R("I3"), 3, SHR)
+    ts(blk("K4", 0), blk("J3", 0), -7.5, A, col(16), Mu); ts(blk("K4", 1), blk("J3", 1), -8.0, A, col(17), Mu); tt(blk("K4", 0), blk("K4", 0), blk("K4", 1), A)
+    aff(R("NBT"), blk("K4", 0), 256.0, 0.0, "S")
+    cp(half("NW", 0, 0, 256), half("NI", 0, 0, 256))
+    for s in range(2):
+        pA, pB, pC, pD = banks(s)
+        n = lambda k: "%s%d" % (k, s)
+        ms(R(pA, 384, 512), 1.0)
+        cp(R(pB, 400, 472, 9), U(32, 40))
+        ms(R(n("RT")), 0.0); ms(R(n("RT"), 40, 41), float(MQ)); ms(R(n("RT"), 41, 42), 256.0); ms(R(n("RT"), 64, 72), 1.0)
+        dma("Y", R(n("DFI")), R("ZERO", 0, AW)); dma("Y", R(n("AC")), R("ZERO", 0, AW))
+        for q in range(2):
+            dma("Y", R(n("EQ"), EQW * q, EQW * q + EQW), R("ZERO"))
+        mm([(R(pD, 0, 128), [(half("REP", s, 0, 128), half("XO", s, 0, 128)), (ID, R("NBT"))])])
+        cp(R(n("W"), XP, XP + 128), R(pD, 0, 128), "S")
+        for h in range(2):
+            dma("Y", half(n("WZ"), h, 384, 512), ("in", "xo", 64 * s, 64 * s + 64))
+        dma("Y", R(n("WZ"), 0, 128), blk("LO", VIS - 1)); dma("Y", R(n("WZ"), 128, 256), blk("LV", VIS - 1))
+        iota(R(n("WN")), [[0, 3], [1, 128]], 0)
+        dma("Y", R(n("WN"), 0, 128, p0=0, p1=64, ps=16), R("NW", 128 * s, 128 * s + 128, p0=VIS - 1, p1=64, ps=16))
+        mm([(half(pC, h, 0, 128), [(half("ID", s, 64 * s, 64 * s + 64), half("Z0", s, h, 256, 2))]) for h in range(2)])
+        cp(R(n("L2"), 64, 192), R(pC, 0, 128), "S")
+    table(1, "TV1", "LV", range(4))
+    for s in range(2):
+        for t in range(VIS - 1):
+            for j, k in enumerate(("TO", "TV")):
+                dma("Y", blk("W%d" % s, 2 * t + j), blk("%s%d" % (k, s), t))
+    ms(R("OM"), 0.0)
+    for j, c in enumerate((11, 9, 14)):
+        ts(R("OM", 24 + 32 * j, 32 + 32 * j), R("TMP", 128, 256, 16), col(c), Mu, col(12), A)
+
+    def visit(s, t):
+        last = t == VIS - 1
+        pA, pB, pC, pD = banks(s)
+        H = lambda k, a=0, b=None, st=1: R("%s%d" % (k, s), a, b, st)
+        MT = H("ML", MTW * t, MTW * t + 128)
+        Z = H("L2", 192 * t + 64, 192 * t + 192)
+        MS = lambda a, b: H("MS", MTW * t + a, MTW * t + b)
+        M2 = lambda a, b: H("M2", M2W * t + a, M2W * t + b)
+        E2, SBC, EX, A32 = R(pB, 0, 128), R(pB, 128, 256), R(pB, 256, 384), R(pB, 384, 392)
+        tag[0] = "%d.%d places" % (t, s)
+        mm([(R(pA, 256, 384), [(MT, R("RE"))])])
+        aff(H("Q"), R(pA, 256, 384), 1.0, -1023.625, OPT["q"])
+        mm([(SBC, [(MT, R("RS"))]), (EX, [(MT, R("RE")), (MT, R("RX"))]), (A32, [(MT, R("RA"))])])
+        mm([(E2, [(MT, R("RE"))])], True, False)
+        mm([(E2, [(NID, H("Q"))])], False, True)
+        cp(H("OFF"), E2)
+        cp(H("RT", 8, 24), R(pB, 15, 256, 16), OPT["rt"])
+        if s == 1 and t > 0:
+            outputs(t - 1)
+        tag[0] = "%d.%d names" % (t, s)
+        a = 0
+        for piece in OPT["g1"].split():
+            b = a + 256 * int(piece[1])
+            cp(H("G1", a, b), IND(H("TO"), H("OFF", a // 16, b // 16)), piece[0])
+            a = b
+        for q, pq in enumerate((pC, pD)):
+            a, e0 = 64 * q, EQW * q
+            Hq = lambda k: H(k, a, a + 64)
+            mm([(half(pq, b % 2, b // 2, 128, 8), [(H("G1", 1024 * q + b, 1024 * q + 1024, 16), R("NS"))]) for b in range(16)])
+            aff(Hq("NH"), R(pq, 64, 128), 8.0, 1148.015625, OPT["floor"][q]); tt(Hq("NB"), R(pq, 0, 64), Hq("NH"), A)
+            mm([(R(pq, 64 * d, 64 * d + 64), [(R("BD", d, 1024, 8), Hq("NB"))]) for d in range(8)])
+            eq, ep = H("EQ", e0 + 1, e0 + 1025, 2), H("EP", 512 * q, 512 * q + 512)
+            if OPT["eq"][q] == "V":
                 ts(eq, R(pq), 0.0, EQL)
             else:
                 act(ep, R(pq), AF.Abs)
-                ts(eq, ep, 0.0, EQL) if mode == "M" else act(eq, ep, AF.Relu, 1.0, -1.0)
-        mms(R(pC, 128, 256), [(BMX(1, d), H("EQ", 128 * d, 128 * d + 128)) for d in range(8)], [4])
-        act(H("YL"), R(pC, 128, 256), AF.Ln, 1.0)
-        aff(H("LQ"), H("YL"), 1.0 / math.log(4.0), 127.7, "SV")
-        if pick("SV") == "S":
-            act(H("MA"), H("YL"), AF.Sign, -1.0)
-        else:
-            ts(H("MA"), H("LQ"), 128.5, OP.is_gt, 2.0, Mu)
-        ma = ops[-1]["eng"]
-        if pick("SV") == "S":
-            act(H("MB"), H("YL"), AF.Sign, 22.7, -1.0)
-        else:
-            ts(H("MB"), H("LQ"), 144.0, OP.is_lt, 2.0, Mu)
-        one = (ma == "S") + (ops[-1]["eng"] == "S")
-        mm([(R(pD, 256, 384), [(QID, H("LQ")), (TRH, H("MA")), (TRH, H("MB"))] + [(TRH if one == 1 else TRI, ONES)] * (one > 0))])
-        ts(H("KEY"), R(pD, 256, 384), col(7), A, 0.0, Mx)
-        for s in range(8):
-            ts(H("CL", 128 * s, 128 * s + 128), H("KEY"), float(s), Mx, float(s + 1), Mn)
-        mms(R(pA, 0, 64), [(R("O256H", 16 - 8 * kh - s, 144 - 8 * kh - s), H("CL", 128 * s + 64 * kh, 128 * s + 64 * kh + 64)) for s in range(8) for kh in range(2)], [4, 8, 12])
-        mms(R(pB, 0, 128), [(wide(2, r), H("GT", r, 2048, 16)) for r in range(16)] + [(KD, ONES), (BD, H("MA"))] + [(BD, ONES)] * (ma == "S"), [3, 6, 9, 12, 15])
-        tr(H("KT", 0, 128), R(pB, 0, 128))
-        scan(H("KS", 0, 128), R("RS", 0, 128), H("KT", 0, 128), 0.0, A, Mx)
-        cp(H("VI"), R(pA, 0, 64))
-        ts(H("RL", 0, 64), H("VI"), 4, SHR, 15, AND); ts(H("RL", 64, 128), H("VI"), 15, AND)
-        for j in range(2):
-            a, b = 64 * j, 64 * j + 64
-            tt(H("PR", a, b), H("RL", a, b), R(pD, 64, 128), Mu)
-            tt(H("SM", a, b), H("PR", a, b), R(pD, 0, 64), A)
-            ts(H("SM2", a, b), H("SM", a, b), 2047, AND); cp(H("POFF", a, b), H("SM2", a, b))
-        ts(H("VV"), H("VI"), 255, AND)
-        ts(H("KA", 0, 64), H("VV"), -1.0, Mu, 255.0, A); ts(H("KA", 64, 128), H("VV"), 0.0, EQL, -BIG, Mu)
-        for q in range(2):
-            cp(H("GO", 512 * q, 512 * q + 512), IND(R("LO"), H("POFF", 32 * q, 32 * q + 32)), "SV")
-        for q in range(2):
-            a, b = 512 * q, 512 * q + 512
-            tt(H("DD", a, b), IND(R("LV"), H("POFF", 64 + 32 * q, 96 + 32 * q)), H("GO", a, b), S_)
-            act(H("AB", a, b), H("DD", a, b), AF.Abs)
-        mms(R(pB, 128, 192), [(ID, H("KA", 0, 64)), (ID, H("KA", 64, 128))] + [(wide(3, p), H("AB", p, 1024, 16)) for p in range(16)], [2])
-        tr(H("KT", 128, 192), R(pB, 128, 192))
-        scan(H("KS", 128, 192), R("RS", 128, 192), H("KT", 128, 192), 0.0, A, Mx)
-        for kh in range(2):
-            tt(H("KI", 4 * kh, 4 * kh + 4), H("KS", 64 * kh + 15, 64 * kh + 64, 16), H("KS", 128 + 8 * kh + 7, 192, 16), Mx)
-        ts(H("FL", 0, 8), H("KI"), 4, SHR, 15, AND); ts(H("FL", 8, 16), H("KI"), 15, AND)
-        tt(H("P2"), H("FL"), H("SBI"), Mu); tt(H("S2"), H("C15"), H("P2"), S_)
-        ts(H("S3"), H("S2"), 2047, AND); cp(H("EF"), H("S3"))
-        mm([(R(pA, 64 + xh, 80, 2), [(R("WD", 160 * xh + 16 - 16 * (gp - xh), 160 * xh + 144 - 16 * (gp - xh)), H("EF", gp, 16, 2)) for gp in range(2)]) for xh in range(2)])
-        cp(H("DOFF"), R(pA, 64, 80))
-        cp(ME(8 * h, 8 * h + 8), H("EF", 0, 8))
-        ts(H("UY"), H("KI"), 1.0 / 256, Mu, -1456.498, A)
-        tt(H("UQ"), H("UY"), H("UY"), Mu); tt(H("UM"), H("UQ"), H("A32"), A)
-        ts(H("UN"), H("UM"), 5, SHR, 127, AND); cp(H("MST", 0, 128, 16), H("UN"))
-        tr(H("MG"), H("MST"))
-        mm([(R(pC, 256, 384), [(R("M0"), H("MG"))])])
-        cp(H("MR"), R(pC, 256, 384), "SV")
-        ts(H("US"), H("KI"), 8, SHR, 511, AND); ts(ME(48 + 8 * h, 56 + 8 * h), H("US"), 2.0, Mu, 1.0, A)
-        cp(H("FO"), IND(R("LO"), H("DOFF", 0, 8)), "SV")
-        tt(H("FD"), IND(R("LV"), H("DOFF", 8, 16)), H("FO"), S_)
-        act(R(pA, 256, 384), H("FD"), AF.Abs)
-        tt(H("GE"), R(pA, 256, 384), ZC(128 * h, 128 * h + 128), OP.is_ge)
-        mms(R(pB, 256, 384), [(CD, ONES), (R("BO"), H("GE"))], [1])
-        tt(H("MQB"), R(pB, 256, 384), H("MR"), Mx)
-        ts(ME(64 + 128 * h, 192 + 128 * h), H("MQB"), 127.5, OP.is_lt)
-        relu(blk("DPW", h), H("FD"), 1.0, "SV"); relu(blk("DNW", h), H("FD"), -1.0, "SV")
-        for hi in range(8):
-            o = H("AT", 128 * hi, 128 * hi + 128)
-            if pick("SV" if hi in (2, 3, 6, 7) else "VS") == "S":
-                act(o, H("MQB"), AF.Abs, R("TG", 8 + hi, 9 + hi), 512.0)
+                ts(eq, ep, 0.0, EQL) if OPT["eq"][q] == "M" else act(eq, ep, AF.Relu, 1.0, -1.0)
+            mm([(R(pq, 0, 64), [(H("EQ", e0 + 128 * d + 1 - be, e0 + 128 * d + 129 - be), R("BM", 512 * be + d, 512 + 512 * be, 8))
+                                for d in range(8) for be in range(2)])])
+            act(Hq("YL"), R(pq, 0, 64), AF.Ln, 1.0, 1.0, 1500.0 if t + s + q == 0 else 0.0)
+            aff(Hq("LQ"), Hq("YL"), 1.0, 143.77, OPT["lq"][q])
+            tt(Hq("PD"), Hq("LQ"), R(pB, 128 + a, 192 + a), Mu); tt(Hq("XI"), Hq("PD"), R(pB, 256 + a, 320 + a), A)
+            ts(Hq("XJ"), Hq("XI"), 2047, AND); cp(Hq("POFF"), Hq("XJ"))
+            if OPT["mk"] == "V":
+                ts(Hq("MK"), Hq("LQ"), 160.5, OP.is_gt, 4 * BIG, Mu)
             else:
-                ts(o, H("MQB"), R("TG", hi, hi + 1), OP.not_equal, 512.0, Mu)
-        for q in range(2):
-            scan(H("WS", 512 * q, 512 * q + 512), R("RW"), H("AT", 512 * q, 512 * q + 512), 0.0, A, Mn)
+                act(Hq("MK"), Hq("LQ"), AF.Relu, -640.0 * BIG, 4 * BIG)
+        tag[0] = "%d.%d sums" % (t, s)
+        for q, pq in enumerate((pC, pD)):
+            o = R(pq, 64, 128)
+            cuts = [1024 * q + c for c in OPT["g2"][q]]
+            for a, b in zip(cuts, cuts[1:]):
+                tt(H("DD", a, b), IND(H("TV"), H("POFF", a // 16, b // 16)), H("G1", a, b), S_)
+                act(H("AB", a, b), H("DD", a, b), AF.Abs)
+            mm([(o, [(IH, R("JT", 64 * q, 64 * q + 64)), (NID, H("MK", 64 * q, 64 * q + 64))])], True, False)
+            mm([(o, [(wide(b), H("AB", 1024 * q + b, 1024 * q + 1024, 16)) for b in range(16)])], False, True)
+            scan(H("KS", 64 * q, 64 * q + 64), R("RK"), o, 0.0, A, Mx)
+        KI = H("KS", 15, 128, 16)
+        tag[0] = "%d.%d fire" % (t, s)
+        ts(H("KA"), KI, 2047, AND); cp(H("DOFF"), H("KA"))
+        tt(H("GE"), IND(H("AB"), H("DOFF")), Z, OP.is_lt)
+        cp(H("DFI", 1, 257, 2), IND(H("DD"), H("DOFF")), "S")
+        mm([(R(pD, 0, 8), [(ID, R("NF"))] + [(wide(b), H("GE", b, 128, 16)) for b in range(16)])])
+        ts(H("UY"), KI, 1.0 / 2048, Mu, -(1456 + 1023.5 / 2048), A)
+        tt(H("UQ"), H("UY"), H("UY"), Mu); tt(H("UM"), H("UQ"), A32, A)
+        ts(H("UX"), H("UM"), 6, SHR, 15, AND); cp(H("XF"), H("UX")); ts(H("UC"), H("UM"), 5, SHR, 97, AND)
+        for r8 in range(8):
+            ts(H("LO", 128 * r8, 128 * r8 + 128), R("TX"), H("XF", r8, r8 + 1), EQL, U(40, 41), Mu)
+        tt(H("HIP"), R(pD, 0, 8), H("UC"), Mx)
+        tt(H("HI"), IND(H("HIP"), R("HL", 0, 4)), R("YT"), EQL)
+        tag[0] = "%d.%d who" % (t, s)
+        mm([(R(pB, 408 - r8, 472, 9), [(H("LO", 128 * r8, 128 * r8 + 128), H("HI", 8 * r8, 8 * r8 + 8))]) for r8 in range(8)])
+        act(H("WL"), R(pB, 400, 472), AF.Ln, math.exp(-32.0))
+        if OPT["we"] == "V":
+            ts(H("WE"), H("WL"), -30.0, OP.is_lt)
+        else:
+            act(H("WE"), H("WL"), AF.Relu, -15.0, -0.5)
+        scan(H("ST"), H("WE"), H("WL"), 0.0, Mu, A)
+        ST = H("ST", 8, 72, 9)
+        ts(H("POS"), ST, -1.0, Mu, col(46), A)
+        for par in range(2):
+            cp(IND(H("AC"), H("POS", 4 * par, 4 * par + 4)), R("ONE", 0, 64))
+        ts(H("RT", 24, 32), H("HIP"), 127.5, OP.is_lt)
+        ts(H("FF"), KI, 4, SHR, 15, AND); tt(H("DC"), H("FF"), H("RT", 16, 24), Mu); ts(H("DC2"), H("DC"), 2047, AND); cp(H("RT", 0, 8), H("DC2"))
+        ts(H("US"), KI, 11, SHR, 511, AND); ts(H("SA"), H("US"), 2.0, Mu, 1.0, A); tt(H("RT", 32, 40), H("SA"), H("RT", 16, 24), S_)
+        mm([(R(pD, 128, 256, p1=96), [(H("RT", 0, 96), IH)]), (R(pD, 128, 256, p0=96), [(H("RT", 0, 32), IH)])])
+        cp(H("DT"), R(pD, 128, 256), OPT["dt"])
+        mm([(R(pA, 384 + b, 512, 16, q0, q0 + 8), [(H("AC", 1 + 2 * b, 257, 32), R("P8"))]) for q0 in (0, 32, 64) for b in range(16)])
+        tt(MS(0, 128), R(pA, 384, 512), H("DT"), Mu)
+        ts(H("SF"), ST, -212.5, OP.is_gt, 256.0 if last else float(XP - 128 * t), Mu); tt(MS(128, 136), H("SF"), R("MTAB"), A)
+        a0 = 128 if last else 0
+        send("aM%d%d" % (s, t), MS(a0, MTW), H("ML", MTW * (t + 1) + a0, MTW * (t + 2)))
+        tag[0] = "%d.%d act" % (t, s)
+        cp(H("SEL", 0, 4), MS(128, 132))
+        cp(M2(0, 128), IND(H("DFI"), H("POS")), "S")
+        act(H("BB"), H("DFI", 1, 257, 2), AF.Abs)
+        if OPT["zn"] == "S":
+            act(H("ZN"), Z, AF.Relu, -1.0)
+        else:
+            ts(H("ZN"), Z, -1.0, A, 0.0, Mx)
+        mm([(R(pC, 128, 256), [(HID, Z), (HID, R("CST", 0, 128)), (NID, H("ZN")), (HID, H("BB"))])])
+        tt(H("PZ"), R(pC, 128, 256), H("AC", 1, 257, 2), Mu)
+        if not last:
+            dma("Y", H("AC"), R("ZERO", 0, AW))
+            mm([(R(pC, 256, 384), [(ID, H("ZN")), (IH, H("PZ"))])])
+            ts(M2(128, 256), R(pC, 256, 384), M1, A, M1, S_)
+        else:
+            mm([(half(pC, s, 256 + h, 512, 2), [(R("ID", 64 * h, 64 * h + 64), H("ZN")), (R("IH", 64 * h, 64 * h + 64), H("PZ"))]) for h in range(2)])
+            ts(half("YZ", s, 0, 256), half(pC, s, 256, 512), M1, A, M1, S_)
+            dma("Y", ("out", "yz", 64 * s, 64 * s + 64), half("YZ", s, 0, 256))
+        w2 = 64 if last else 192
+        send("aX%d%d" % (s, t), M2(64, 64 + w2), H("L2", 192 * (t + 1), 192 * (t + 1) + w2))
+        cp(H("SEL", 4, 8), H("ML", MTW * (t + 1) + 132, MTW * (t + 1) + 136))
+        xc = XP + 128 * t
+        sel = lambda par: H("SEL", 4 * par, 4 * par + 4)
+        pl = lambda k, par: H(k, 128 * t + par, 128 * t + 128, 2)
+        x0, x1 = (H("WZ", 256 + 128 * (u % 2), 384 + 128 * (u % 2)) for u in (t + 1, t))
+        for par in range(2):
+            if not last:
+                cp(pl("TO", par), IND(H("W", 256 * t, xc + 128), sel(par)), OPT["tw"][par])
+            else:
+                cp(H("ZO", par, 128, 2), IND(H("WZ", 0, 384), sel(par)), "SV"[par])
+                cp(H("ZM", par, 128, 2), IND(H("WN"), sel(par)), "S")
+        o = R(pD, 256, 384)
+        mm([(o, [(ID, x0), (REP, M2(0, 64), R(pD, 256, 384, 2))])], True, False)
+        mm([(o, [(REP, H("L2", 192 * (t + 1), 192 * (t + 1) + 64), R(pD, 257, 384, 2))])], False, True)
+        ts(x1, o, 0.0, Mx, 255.0, Mn)
+        if not last:
+            mm([(o, [(ID, R("NBT")), (ID, x1)])])
+            cp(H("W", xc + 128, xc + 256), o, "S")
+        for par in range(2):
+            if not last:
+                cp(pl("TV", par), IND(H("W", 256 * t + 128, xc + 256), sel(par)), OPT["tw"][2 + par])
+            else:
+                cp(H("ZV", par, 128, 2), IND(H("WZ", 128, 512), sel(par)), "SV"[par])
+        if last:
+            dma("Y", ("out", "yo", 64 * s, 64 * s + 64, 128 * t, 128 * VIS), half("ZO%d" % s, s, 0, 128))
+            dma("Y", ("out", "yn", 4 * s, 4 * s + 4, 128 * t, 128 * VIS), R("ZM%d" % s, p0=0, p1=64, ps=16))
+            dma("Y", ("out", "yx", 64 * s, 64 * s + 64), half("WZ%d" % s, s, 384, 512))
+            dma("S", ("out", "yv", 64 * s, 64 * s + 64, 128 * t, 128 * VIS), half("ZV%d" % s, s, 0, 128))
+            o = lambda h: R(pA, h, 32, 2, 0, 96)
+            mm([(o(h), [(R("OM", 24 - 8 * gq, 120 - 8 * gq), MS(64 * h + 16 * gq, 64 * h + 16 * gq + 16)) for gq in range(4)]) for h in range(2)])
+            a, b = 32 * s, 32 * s + 32
+            aff(R("YQ", a, b, p1=96), R(pA, 0, 32, p1=96), 1.0, -1023.625, "V")
+            tt(R("YC", a, b, p1=96), R(pA, 0, 32, p1=96), R("YQ", a, b, p1=96), S_)
+            for j, k in enumerate(("yc", "ys", "ya")):
+                dma("YS"[j % 2], ("out", k, 4 * s, 4 * s + 4), R("YC", a, b, p0=32 * j, p1=32 * j + 32))
 
-    def update(t, par, dpn, sel, psT, psX):
-        last = t == VIS - 1
-        cur, new = 384 * par + 192 * (t % 2), 384 * par + 192 * (1 - t % 2)
-        pl = lambda n: R(n, 128 * t + par, 128 * t + 128, 2)
-        a0 = 128 * par
-        ap, an = R("AA", a0, a0 + 64), R("AA", a0 + 64, a0 + 128)
-        tt(R("AA", a0, a0 + 128), dpn, R("XW", cur, cur + 128), Mn)
-        bt = R("BT", 64 * par, 64 * par + 64)
-        cp(bt, IND(R("STT", a0, a0 + 128), sel), "SV")
-        if not last:
-            ts(R("HH", a0, a0 + 128), R("AA", a0, a0 + 128), M16, A, M16, S_)
-            mms(R(psT, 0, 64), [(ID, bt), (TA, ap), (TA, an), (TH, R("HH", a0, a0 + 64)), (TH, R("HH", a0 + 64, a0 + 128))], [3])
-            cp(pl("TT"), R(psT, 0, 64), "SV")
-        else:
-            phase[1] += 4
-        cp(pl("YN"), bt, "SV")
-        mm([(R(psX, 0, 64), [(ID, R("XW", cur + 64, cur + 128)), (ID, ap), (NID, an)])])
-        cp(R("XW", new + 64, new + 128), R(psX, 0, 64), "SV")
-        if not last:
-            aff(R("XW", new, new + 64), R("XW", new + 64, new + 128), -1.0, 255.0, "SV")
-        else:
-            cp(R("YX", par, 128, 2), R("XW", new + 64, new + 128), "SV")
-        cp(pl("LO"), IND(R("XW", cur + 64, cur + 192), sel), "SV")
-        cp(pl("LV"), IND(R("XW", new + 64, new + 192), sel), "SV")
+    def outputs(t):
+        tag[0] = "%d out" % t
+        pA = banks(1)[0]
+        a, b = 128 * t, 128 * t + 128
+        mm([(half(pA, s, 0, 256), [(R("IH", 0, 64), R("QOT"))] +
+             [(R("IF", 0, 64), R("%s%d" % (k, s), a, b), half(pA, s, 128 * j, 128 * j + 128)) for j, k in enumerate(("TO", "TV"))]) for s in range(2)])
+        aff(R("QD"), R(pA, 0, 256), 1.0, -127.5, OPT["dq"])
+        tt(R("YO", a, b), R(pA, 0, 128), R("QD", 0, 128), S_); tt(R("YV", a, b), R(pA, 128, 256), R("QD", 128, 256), S_)
+        mm([(R(pA, 256, 384, p1=8), [(R("NN"), R("QD", 0, 128))])])
+        aff(R("YN", a, b, p1=8), R(pA, 256, 384, p1=8), 1.0, 71.0 - 9.0 * QO / 256, "S")
+        if t == VIS - 2:
+            dma("Y", ("out", "yo", 0, 128, 0, b), R("YO", 0, b))
+            dma("Y", ("out", "yv", 0, 128, 0, b), R("YV", 0, b))
+            dma("Y", ("out", "yn", 0, 8, 0, b), R("YN", 0, b, p1=8))
 
     for t in range(VIS):
-        last = t == VIS - 1
-        phase[0], phase[1] = "a", 0
-        when[0] = t
-        ME = lambda a, b: R("MES", MEW * t + a, MEW * t + b)
-        MF = lambda a, b: R("MFS", MFW * t + a, MFW * t + b)
-        L = lambda a, b: R("MFL", MFW * t + a, MFW * t + b)
-        ZC = (lambda a, b: R("Z0", a, b)) if t == 0 else (lambda a, b: R("ZL", 256 * (t - 1) + a, 256 * (t - 1) + b))
-        for h in range(2):
-            ts(blk("OFF", h), blk("EN", h), MQ, A)
-        for q in range(8):
-            cp(R("GT", 512 * q, 512 * q + 512), IND(R("TT"), R("OFF", 32 * q, 32 * q + 32)), "VS" if q % 2 else "SV")
-        for par in range(2):
-            cur, new = 384 * par + 192 * (t % 2), 384 * par + 192 * (1 - t % 2)
-            for n, dst in (("LO", R("XW", cur + 128, cur + 192)), ("LV", R("XW", new + 128, new + 192)), ("TT", R("STT", 128 * par + 64, 128 * par + 128))):
-                cp(dst, R(n, 128 * t + par, 128 * t + 128, 2), "G")
-        tr(R("ET"), R("EN", 0, 256))
-        ETr = lambda r, a=0, b=256: R("ET", a + r, b, 16)
-        tt(R("SI"), ETr(1), ETr(0), S_)
-        for j in range(4):
-            cp(R("SBI", 8 * j, 8 * j + 8), R("SI", 8 * (j // 2), 8 * (j // 2) + 8), "G")
-            cp(R("C15", 8 * j, 8 * j + 8), ETr(15, 128 * (j // 2), 128 * (j // 2) + 128), "G")
-        cp(ME(16, 32), R("SI"))
-        tt(R("CA"), ETr(15), R("SI"), A); ts(R("CA2"), R("CA"), 2047, AND); cp(ME(32, 48), R("CA2"))
-        cp(R("CI"), ETr(0)); tt(R("A32"), ETr(0), R("CI"), S_); aff(R("A32"), R("A32"), 128.0, -350464.0, "SV")
-        read_half(0, ME, ZC)
-        aff(R("T1"), R("WS", 127, 1024, 128), 1.0, -128.0, "SV"); tt(R("T0"), R("T1"), R("TG", 16, 24), Mn)
-        read_half(1, ME, ZC)
-        if not last:
-            send("aE%d" % t, ME(0, MEW), R("MEL", MEW * t, MEW * t + MEW))
-        else:
-            phase[1] += 2
-        tt(MF(128, 136), R("T0"), R("WS", 1024 + 127, 2048, 128), Mn)
-        ts(R("LOWU"), MF(128, 136), 255.0, A)
-        cp(MF(0, 64), IND(R("DPW"), R("LOWU", 4, 8)), "SV"); cp(MF(64, 128), IND(R("DNW"), R("LOWU", 4, 8)), "VS")
-        ts(R("SL"), MF(128, 136), 0.0, OP.is_gt, 64.0, Mu); tt(MF(136, 144), R("SL"), R("TG", 24, 32), A)
-        send("aF%d" % t, MF(0, MFW), L(0, MFW))
-        cp(R("SELU", 0, 4), MF(136, 140))
-        cp(R("DE", 0, 64), IND(R("DPW"), R("LOWU", 0, 4)), "SV"); cp(R("DE", 64, 128), IND(R("DNW"), R("LOWU", 0, 4)), "SV")
-        update(t, 0, R("DE"), R("SELU", 0, 4), "PS6", "PS7")
-        src, ex = ("MES", 16) if last else ("MEL", 0)
-        tr(R("MT"), R(src, MEW * t, MEW * t + 64))
-        mm([(R("PS0", 32 * b, 32 * b + 32), [(blk("EX", ex + b), R("MT", 0, 32)), (blk("FQ", int(last)), R(src, MEW * t + 64 + 32 * b, MEW * t + 96 + 32 * b))]) for b in range(8)])
-        floor_mod("PS0", "EN", 0)
-        mm([(R("PS1", 32 * b, 32 * b + 32), [(blk("EX", ex + 8 + b), R("MT", 32, 64))]) for b in range(8)])
-        floor_mod("PS1", "EA", 256)
-        for x in range(4 * t, 4 * t + 4):
-            if x < 16 and not last:
-                ts(blk("EX", 16 + x), blk("EXB", 2 + x // 8), col(24 + x % 8), Mu)
-            else:
-                phase[1] += 1
-        mm([(R("PS4", 0, 256), [(HID, ZC(0, 256)), (HID, R("NH")), (HID, R("DPW", 0, 256)), (HID, R("DNW", 0, 256))])])
-        ts(R("ZA", 0, 256), R("PS4", 0, 256), M1, A, M1, S_)
-        ts(R("ZW", 384 * t, 384 * t + 256), ZC(0, 256), -1.0, A, 0.0, Mx)
-        cp(R("ZAG"), IND(R("ZA"), R("LOWU")), "SV")
-        cp(IND(R("ZW", 384 * t, 384 * t + 384), R("LOWU")), R("ZAG"))
-        if not last:
-            send("aZ%d" % t, R("ZW", 384 * t, 384 * t + 256), R("ZL", 256 * t, 256 * t + 256))
-            ts(R("LOW2"), L(128, 136), 255.0, A)
-        else:
-            phase[1] += 3
-        low = R("LOWU" if last else "LOW2")
-        cp(R("SELU", 4, 8), L(140, 144))
-        cp(R("EAG"), IND(R("EA"), low), "SV")
-        cp(IND(R("EN"), low), R("EAG"))
-        update(t, 1, L(0, 128), R("SELU", 4, 8), "PS2", "PS3")
-        if t >= VIS - 2:
-            phase[0], phase[1] = "o", 3 * (t - VIS + 2)
-            a, b = (128 * t, 128 * VIS) if last else (0, 128 * (VIS - 1))
-            store("Y", ("out", "yo", a, b), R("LO", a, b))
-            store("S" if last else "Y", ("out", "yv", a, b), R("LV", a, b))
-            store("Y", ("out", "yn", a, b), R("YN", a, b, ps=16))
-    act(R("YC"), R("EN", 0, 256), AF.Identity, MQ)
-    for j, n in enumerate(("yc", "ys", "ya")):
-        store("Y", ("out", n), R("YC", p0=j, ps=16))
-    store("Y", ("out", "yx"), R("YX"))
-    store("Y", ("out", "yz"), R("ZW", 384 * (VIS - 1), 384 * (VIS - 1) + 256))
-    return ops, flex
+        visit(0, t)
+        visit(1, t)
+    return ops
 
 
 def schedule(ops):
     n = len(ops)
-    hop = PM["hop"]
+    eng, cost, lat, key = ([o[k] for o in ops] for k in ("eng", "cost", "lat", "key"))
     succ = [[] for _ in range(n)]
     for i, o in enumerate(ops):
         for j in o["deps"]:
-            succ[j].append(i)
-    gap = lambda j, i: 0.0 if ops[j]["kind"] == "send" or (ops[j]["eng"] == "P" and ops[i]["eng"] == "P") else hop
-    prio = [0.0] * n
+            succ[j].append((i, lat[j] + (0.0 if ops[j]["kind"] == "send" or eng[j] + eng[i] == "PP" else PM["hop"])))
+    chain = [0.0] * n
     for i in range(n - 1, -1, -1):
-        prio[i] = ops[i]["cost"] + ops[i]["lat"] + max([prio[j] + gap(i, j) for j in succ[i]] + [0.0])
-    for i in range(n):
-        prio[i] += 50.0 * BOOST.get(ops[i]["key"].replace("c", "a"), 0)
-    left = [len(o["deps"]) for o in ops]
-    ready = {e: {} for e in "NVSPGY"}
-    for i in range(n):
-        if left[i] == 0:
-            ready[ops[i]["eng"]][i] = 0.0
-    free = {e: 0.0 for e in ready}
-    fin = [0.0] * n
-    order = []
-    while len(order) < n:
-        t0, e = min((max(free[e], min(c.values())), e) for e, c in ready.items() if c)
-        c = ready[e]
-        i = max((i for i in c if c[i] <= t0 + OPT["win"]), key=lambda i: (prio[i], -i))
-        if c[i] > t0 + 20.0:
-            fill = [j for j in c if max(c[j], t0) + ops[j]["cost"] <= c[i] + OPT["tol"]]
-            if fill:
-                i = max(fill, key=lambda j: (prio[j], -j))
-        st = max(t0, c.pop(i))
-        free[e] = st + ops[i]["cost"]
-        fin[i] = free[e] + ops[i]["lat"]
-        order.append((i, e, st))
-        for j in succ[i]:
-            left[j] -= 1
-            if left[j] == 0:
-                ready[ops[j]["eng"]][j] = max(fin[k] + gap(k, j) for k in ops[j]["deps"])
-    return order, max(fin)
+        chain[i] = cost[i] + max([chain[j] + w for j, w in succ[i]] + [lat[i]])
+    chain = [chain[i] + (OPT["lead"] if ".0 " in ops[i]["tag"] else 0.0) - 1e-3 * i for i in range(n)]
+    win, tol = OPT["win"], OPT["tol"]
+
+    def timetable(shift):
+        prio = [chain[i] + shift.get(key[i], 0.0) for i in range(n)]
+        left = [len(o["deps"]) for o in ops]
+        due = [0.0] * n
+        ready = {e: [] for e in "NVSPGY"}
+        for i in range(n):
+            if left[i] == 0:
+                ready[eng[i]].append(i)
+        free = {e: 0.0 for e in ready}
+        order = []
+        end = 0.0
+        while len(order) < n:
+            t0, e = min((max(free[e], min(due[i] for i in c)), e) for e, c in ready.items() if c)
+            c = ready[e]
+            i = max((i for i in c if due[i] <= t0 + win), key=lambda i: prio[i])
+            if due[i] > t0 + 20.0:
+                fill = [j for j in c if max(due[j], t0) + cost[j] <= due[i] + tol]
+                if fill:
+                    i = max(fill, key=lambda j: prio[j])
+            c.remove(i)
+            st = max(t0, due[i])
+            f = free[e] = st + cost[i]
+            end = max(end, f + lat[i])
+            order.append((i, e, st))
+            for j, w in succ[i]:
+                due[j] = max(due[j], f + w)
+                left[j] -= 1
+                if left[j] == 0:
+                    ready[eng[j]].append(j)
+        return order, end
+
+    steps = list(dict.fromkeys(key))
+    shift = dict(BOOST)
+    best = timetable(shift)
+    x = OPT["seed"]
+    for _ in range(OPT["tries"]):
+        trial = dict(shift)
+        for _ in range(1 + x % 2):
+            x = (x * 1103515245 + 12345) % (1 << 31)
+            k = steps[(x >> 8) % len(steps)]
+            x = (x * 1103515245 + 12345) % (1 << 31)
+            by = (-6000.0, -2000.0, -700.0, -250.0, 250.0, 700.0, 2000.0, 6000.0)[(x >> 8) % 8]
+            a = steps.index(k)
+            for k in steps[a:a + (1, 1, 1, 4, 12)[(x >> 12) % 5]]:
+                trial[k] = trial.get(k, 0.0) + by
+        got = timetable(trial)
+        if got[1] <= best[1]:
+            best, shift = got, trial
+    return best
 
 
-OTHER = "a128S a233S a234S a235V a236V a254V a262V a267V a301V a49V s103V s112S s113S s115S s116S s119S s122S s124S s127S s131S s135S s136S s138S s139S s147S s152V s34V s48S s54S s55V s80S s92S s94V"
-EARLIER = "a101:51 a102:129 a112:52 a118:57 a124:-42 a127:-45 a130:-5 a133:37 a134:39 a14:8 a142:252 a16:-39 a161:-29 a163:-33 a170:-87 a176:88 a181:28 a182:-39 a185:-50 a187:76 a188:93 a190:58 a191:62 a194:2 a2:145 a200:140 a206:80 a21:-38 a210:3 a213:2 a222:-30 a223:12 a226:-19 a230:20 a239:-48 a248:163 a249:168 a256:-49 a26:45 a261:1 a262:-91 a268:3 a269:3 a27:6 a28:-36 a280:-20 a281:30 a282:154 a286:312 a287:199 a295:-27 a296:-206 a300:-59 a31:-90 a37:-59 a4:93 a60:-86 a64:-56 a66:-59 a67:-62 a7:-12 a71:-38 a72:53 a74:-11 a77:-53 a81:-49 a82:-50 a86:-3 a88:46 a89:37 a90:-77 a92:15 a97:87 a98:62 a99:71 s1:-61 s103:-20 s108:-3 s109:-61 s11:-8 s114:-22 s117:8 s123:-3 s128:8 s129:-66 s14:-19 s153:-3 s157:-3 s159:-12 s166:20 s174:58 s176:111 s180:23 s181:31 s182:20 s183:82 s184:40 s185:32 s188:30 s195:70 s197:-58 s204:-8 s24:-3 s25:117 s26:62 s27:-3 s28:-3 s34:34 s36:50 s40:-50 s43:-8 s45:-11 s57:-42 s58:-8 s66:14 s69:31 s7:-8 s71:-20 s79:-66 s84:31 s85:42 s94:47 s97:-50"
-for _w in OTHER.split():
-    ASSIGN[_w[:-1]] = _w[-1]
-for _w in EARLIER.split():
-    BOOST[_w.split(":")[0]] = int(_w.split(":")[1])
 PLAN = []
 
 
@@ -592,7 +566,7 @@ def rank_program(g, core, T, topo):
     if rank is None:
         return
     if not PLAN:
-        ops = build()[0]
+        ops = build()
         PLAN.append((ops, schedule(ops)[0]))
     ops, order = PLAN[0]
     n = len(T.cores)
@@ -609,7 +583,7 @@ def rank_program(g, core, T, topo):
         if r[0] == "ind":
             return ap(r[1]).indirect(ap(r[2]))
         if r[0] in ("in", "out"):
-            return T[r[1]][:] if len(r) == 2 else T[r[1]][:, r[2]:r[3]]
+            return T[r[1]][r[2]:r[3], :] if len(r) == 4 else T[r[1]][r[2]:r[3], r[4]:r[5]]
         ps = slice(r[4], r[5], r[6]) if r[6] != 1 else slice(r[4], r[5])
         nm, o = PLACE.get(r[0], (r[0], 0))
         cs = slice(o + r[1], o + r[2], r[3]) if r[3] != 1 else slice(o + r[1], o + r[2])
@@ -649,22 +623,18 @@ def rank_program(g, core, T, topo):
             ins = q.tensor_tensor(ap(a[0]), ap(a[1]), ap(a[2]), a[3])
         elif k == "cp":
             ins = q.tensor_copy(ap(a[0]), ap(a[1])) if e == "V" else q.activation(ap(a[0]), ap(a[1]), AF.Copy)
-        elif k == "gcp":
-            ins = g.affine_select(ap(a[0]), ap(a[1]), [[0, cnt(a[0])]], OP.is_ge, 0.0, 0, 0)
         elif k == "act":
             ins = q.activation(ap(a[0]), ap(a[1]), a[2], ap(a[3]), ap(a[4]))
         elif k == "scan":
             ins = q.tensor_tensor_scan(ap(a[0]), ap(a[1]), ap(a[2]), a[3], a[4], a[5])
-        elif k == "tr":
-            ins = q.transpose(ap(a[0]), ap(a[1]))
         elif k == "ms":
             ins = q.memset(ap(a[0]), a[1])
         elif k == "iota":
             ins = g.iota(ap(a[0]), a[1], a[2], a[3], allow_small_or_imprecise_dtypes=True) if SB[a[0][0]][1] != I32 else g.iota(ap(a[0]), a[1], a[2], a[3])
         else:
             for out, terms in a[0]:
-                for x, (l, r) in enumerate(terms):
-                    ins = q.matmul(ap(out), ap(l), ap(r), a[1] and x == 0, a[2] and x == len(terms) - 1)
+                for x, term in enumerate(terms):
+                    ins = q.matmul(ap(term[2] if len(term) > 2 else out), ap(term[0]), ap(term[1]), a[1] and x == 0, a[2] and x == len(terms) - 1)
         count[e] += 1
         ins.then_inc(T.sem["c" + e], 1)
         tok[i] = ("c" + e, count[e]); total["c" + e] = count[e]

@@ -8,7 +8,7 @@ BIG = float(1 << 23)
 MQ = 192
 M1 = 1.5 * (1 << 23)
 QO = 49152.0
-MTW, M2W, AW, EQW = 136, 256, 336, 1040
+MTW, M2W, AW, EQW = 136, 256, 400, 1040
 XP = 256 * (VIS - 1)
 
 PER_STREAM = {
@@ -16,11 +16,11 @@ PER_STREAM = {
     "WZ": (512, BF), "WN": (384, BF), "ZO": (128, BF), "ZV": (128, BF), "ZM": (128, F32),
     "MS": (MTW * VIS, HP), "ML": (MTW * (VIS + 1), HP), "M2": (M2W * VIS, BF), "L2": (192 * (VIS + 1), BF),
     "Q": (128, BF), "OFF": (128, U16), "G1": (2048, HP), "NB": (128, HP), "NH": (128, BF), "EP": (1024, BF), "EQ": (2 * EQW, BF),
-    "YL": (128, F32), "LQ": (128, BF), "MK": (128, BF), "PD": (128, F32), "XI": (128, I32), "XJ": (128, I32), "POFF": (128, U16),
+    "YL": (128, F32), "LQ": (256, BF), "MK": (128, BF), "XI": (256, I32), "XJ": (128, I32), "POFF": (128, U16),
     "DD": (2048, BF), "AB": (2048, BF), "KS": (128, I32), "KA": (8, I32), "DOFF": (8, U16), "DFI": (AW, BF), "GE": (128, BF), "BB": (128, BF),
     "UY": (8, I32), "UQ": (8, F32), "UM": (8, I32), "UX": (8, I32), "UC": (8, I32), "XF": (8, F32), "HIP": (8, F32), "HI": (64, BF), "LO": (1024, BF),
     "FF": (8, I32), "DC": (8, I32), "DC2": (8, I32), "US": (8, I32), "SA": (8, F32), "RT": (96, HP), "DT": (128, HP),
-    "WL": (72, F32), "WE": (72, F32), "ST": (72, F32), "POS": (8, U16), "SF": (8, F32), "SEL": (8, U16), "AC": (AW, BF),
+    "WL": (88, F32), "WE": (88, F32), "ST": (88, F32), "POS": (8, U16), "SF": (8, F32), "SEL": (8, U16), "AC": (AW, BF),
     "ZN": (128, BF), "PZ": (128, HP),
 }
 SB = {"%s%d" % (k, s): v for k, v in PER_STREAM.items() for s in range(2)}
@@ -49,8 +49,9 @@ for _i in range(8):
 DMAS = ["d%d" % i for i in range(100)]
 SEMAPHORES = ["cV", "cS", "cP", "cG", "sent"] + DMAS + ["a%s%d%d" % (k, s, t) for k in "MX" for s in range(2) for t in range(VIS)]
 
-PM = {"cy": 1.04, "hop": 110.0, "pe": 0.6, "ga": 1.56, "sc": 3.8, "link": 2600.0, "issue": 400.0, "dma": 2200.0}
-OPT = {"seed": 1, "tries": 2600, "lead": 8500.0, "win": 200.0, "tol": 30.0, "g1": "S2 V2 S2 S2", "eq": "MV", "floor": "SS", "q": "S", "lq": "SS", "mk": "S", "g2": ((0, 256, 512, 1024), (0, 512, 768, 1024)), "zn": "S", "dt": "S", "tw": "SSSS", "we": "S", "dq": "S", "evac": "VSVS", "bm": "VVS", "nm": "VVS", "rt": "S"}
+PM = {"cy": 1.04, "hop": 170.0, "pe": 0.52, "ga": 1.56, "sc": 3.8, "link": 2200.0, "issue": 400.0, "dma": 2200.0}
+SPREAD = ({}, {"cy": 0.9, "hop": 210.0, "pe": 0.46, "ga": 1.3, "link": 2000.0}, {"cy": 1.15, "hop": 120.0, "pe": 0.65, "ga": 1.7, "link": 2800.0})
+OPT = {"heat": 0.0, "swaps": 2500, "seed": 5, "tries": 2500, "lead": 8500.0, "win": 200.0, "tol": 30.0, "g1": "S2 V2 S2 S2", "g1a": "S2 V2 S2 V2", "eq": "MV", "floor": "SS", "q": "S", "lq": "SS", "mk": "S", "g2": ((0, 256, 512, 1024), (0, 512, 768, 1024)), "zn": "S", "dt": "S", "tw": "SSSS", "we": "S", "dq": "S", "evac": "SVSS", "bm": "VVS", "nm": "VVS", "rt": "S"}
 BOOST = {}
 
 
@@ -302,9 +303,10 @@ def build():
         pA, pB, pC, pD = banks(s)
         n = lambda k: "%s%d" % (k, s)
         ms(R(pA, 384, 512), 1.0)
-        cp(R(pB, 400, 472, 9), U(32, 40))
+        ms(R(pB, 400, 488), 0.0)
+        cp(R(pB, 402, 444, 11), U(32, 36)); cp(R(pB, 444, 488, 11), U(36, 40))
         ms(R(n("RT")), 0.0); ms(R(n("RT"), 40, 41), float(MQ)); ms(R(n("RT"), 41, 42), 256.0); ms(R(n("RT"), 64, 72), 1.0)
-        dma("Y", R(n("DFI")), R("ZERO", 0, AW)); dma("Y", R(n("AC")), R("ZERO", 0, AW))
+        dma("Y", R(n("DFI")), R("ZERO", 0, AW)); dma("Y", R(n("AC")), R("ZERO", 0, AW)); dma("Y", R(n("LQ")), R("ZERO", 0, 256))
         for q in range(2):
             dma("Y", R(n("EQ"), EQW * q, EQW * q + EQW), R("ZERO"))
         mm([(R(pD, 0, 128), [(half("REP", s, 0, 128), half("XO", s, 0, 128)), (ID, R("NBT"))])])
@@ -333,7 +335,7 @@ def build():
         Z = H("L2", 192 * t + 64, 192 * t + 192)
         MS = lambda a, b: H("MS", MTW * t + a, MTW * t + b)
         M2 = lambda a, b: H("M2", M2W * t + a, M2W * t + b)
-        E2, SBC, EX, A32 = R(pB, 0, 128), R(pB, 128, 256), R(pB, 256, 384), R(pB, 384, 392)
+        E2, SBC, EX, A32 = R(pB, 0, 128), R(pB, 128, 384, 2), R(pB, 129, 384, 2), R(pB, 384, 392)
         tag[0] = "%d.%d places" % (t, s)
         mm([(R(pA, 256, 384), [(MT, R("RE"))])])
         aff(H("Q"), R(pA, 256, 384), 1.0, -1023.625, OPT["q"])
@@ -341,12 +343,13 @@ def build():
         mm([(E2, [(MT, R("RE"))])], True, False)
         mm([(E2, [(NID, H("Q"))])], False, True)
         cp(H("OFF"), E2)
-        cp(H("RT", 8, 24), R(pB, 15, 256, 16), OPT["rt"])
+        cp(H("RT", 8, 16), R(pB, 15, 128, 16), OPT["rt"]); cp(H("RT", 16, 24), R(pB, 128, 384, 32), OPT["rt"])
         if s == 1 and t > 0:
             outputs(t - 1)
         tag[0] = "%d.%d names" % (t, s)
         a = 0
-        for piece in OPT["g1"].split():
+        alone = (t, s) in ((0, 0), (VIS - 1, 1))
+        for piece in OPT["g1a" if alone else "g1"].split():
             b = a + 256 * int(piece[1])
             cp(H("G1", a, b), IND(H("TO"), H("OFF", a // 16, b // 16)), piece[0])
             a = b
@@ -365,13 +368,14 @@ def build():
             mm([(R(pq, 0, 64), [(H("EQ", e0 + 128 * d + 1 - be, e0 + 128 * d + 129 - be), R("BM", 512 * be + d, 512 + 512 * be, 8))
                                 for d in range(8) for be in range(2)])])
             act(Hq("YL"), R(pq, 0, 64), AF.Ln, 1.0, 1.0, 1500.0 if t + s + q == 0 else 0.0)
-            aff(Hq("LQ"), Hq("YL"), 1.0, 143.77, OPT["lq"][q])
-            tt(Hq("PD"), Hq("LQ"), R(pB, 128 + a, 192 + a), Mu); tt(Hq("XI"), Hq("PD"), R(pB, 256 + a, 320 + a), A)
-            ts(Hq("XJ"), Hq("XI"), 2047, AND); cp(Hq("POFF"), Hq("XJ"))
+            lq = H("LQ", 2 * a + 1, 2 * a + 128, 2)
+            aff(lq, Hq("YL"), 1.0, 143.77, OPT["lq"][q])
+            scan(H("XI", 2 * a, 2 * a + 128), H("LQ", 2 * a, 2 * a + 128), R(pB, 128 + 2 * a, 256 + 2 * a), 0.0, Mu, A)
+            ts(Hq("XJ"), H("XI", 2 * a + 1, 2 * a + 128, 2), 2047, AND); cp(Hq("POFF"), Hq("XJ"))
             if OPT["mk"] == "V":
-                ts(Hq("MK"), Hq("LQ"), 160.5, OP.is_gt, 4 * BIG, Mu)
+                ts(Hq("MK"), lq, 160.5, OP.is_gt, 4 * BIG, Mu)
             else:
-                act(Hq("MK"), Hq("LQ"), AF.Relu, -640.0 * BIG, 4 * BIG)
+                act(Hq("MK"), lq, AF.Relu, -640.0 * BIG, 4 * BIG)
         tag[0] = "%d.%d sums" % (t, s)
         for q, pq in enumerate((pC, pD)):
             o = R(pq, 64, 128)
@@ -396,17 +400,16 @@ def build():
         tt(H("HIP"), R(pD, 0, 8), H("UC"), Mx)
         tt(H("HI"), IND(H("HIP"), R("HL", 0, 4)), R("YT"), EQL)
         tag[0] = "%d.%d who" % (t, s)
-        mm([(R(pB, 408 - r8, 472, 9), [(H("LO", 128 * r8, 128 * r8 + 128), H("HI", 8 * r8, 8 * r8 + 8))]) for r8 in range(8)])
-        act(H("WL"), R(pB, 400, 472), AF.Ln, math.exp(-32.0))
+        mm([(R(pB, 410 - r8, 488, 11), [(H("LO", 128 * r8, 128 * r8 + 128), H("HI", 8 * r8, 8 * r8 + 8))]) for r8 in range(8)])
+        act(H("WL"), R(pB, 400, 488), AF.Ln, math.exp(-32.0))
         if OPT["we"] == "V":
             ts(H("WE"), H("WL"), -30.0, OP.is_lt)
         else:
             act(H("WE"), H("WL"), AF.Relu, -15.0, -0.5)
         scan(H("ST"), H("WE"), H("WL"), 0.0, Mu, A)
-        ST = H("ST", 8, 72, 9)
+        ST = H("ST", 10, 88, 11)
         ts(H("POS"), ST, -1.0, Mu, col(46), A)
-        for par in range(2):
-            cp(IND(H("AC"), H("POS", 4 * par, 4 * par + 4)), R("ONE", 0, 64))
+        cp(IND(H("AC"), H("POS")), ONE)
         ts(H("RT", 24, 32), H("HIP"), 127.5, OP.is_lt)
         ts(H("FF"), KI, 4, SHR, 15, AND); tt(H("DC"), H("FF"), H("RT", 16, 24), Mu); ts(H("DC2"), H("DC"), 2047, AND); cp(H("RT", 0, 8), H("DC2"))
         ts(H("US"), KI, 11, SHR, 511, AND); ts(H("SA"), H("US"), 2.0, Mu, 1.0, A); tt(H("RT", 32, 40), H("SA"), H("RT", 16, 24), S_)
@@ -516,33 +519,41 @@ def schedule(ops):
             if left[i] == 0:
                 ready[eng[i]].append(i)
         free = {e: 0.0 for e in ready}
+        soon = {e: 0.0 if c else 1e18 for e, c in ready.items()}
         order = []
         end = 0.0
-        while len(order) < n:
-            t0, e = min((max(free[e], min(due[i] for i in c)), e) for e, c in ready.items() if c)
-            c = ready[e]
-            i = max((i for i in c if due[i] <= t0 + win), key=lambda i: prio[i])
-            if due[i] > t0 + 20.0:
-                fill = [j for j in c if max(due[j], t0) + cost[j] <= due[i] + tol]
-                if fill:
-                    i = max(fill, key=lambda j: prio[j])
+        for _ in range(n):
+            e = min(soon, key=soon.get)
+            t0, c = soon[e], ready[e]
+            i = c[0]
+            if len(c) > 1:
+                i = max([i for i in c if due[i] <= t0 + win], key=lambda j: prio[j])
+                if due[i] > t0 + 20.0:
+                    fill = [j for j in c if max(due[j], t0) + cost[j] <= due[i] + tol]
+                    if fill:
+                        i = max(fill, key=lambda j: prio[j])
             c.remove(i)
             st = max(t0, due[i])
             f = free[e] = st + cost[i]
-            end = max(end, f + lat[i])
+            soon[e] = max(f, min([due[j] for j in c])) if c else 1e18
+            if f + lat[i] > end:
+                end = f + lat[i]
             order.append((i, e, st))
             for j, w in succ[i]:
-                due[j] = max(due[j], f + w)
+                if f + w > due[j]:
+                    due[j] = f + w
                 left[j] -= 1
                 if left[j] == 0:
                     ready[eng[j]].append(j)
+                    soon[eng[j]] = min(soon[eng[j]], max(free[eng[j]], due[j]))
         return order, end
 
     steps = list(dict.fromkeys(key))
     shift = dict(BOOST)
     best = timetable(shift)
+    now = best[1]
     x = OPT["seed"]
-    for _ in range(OPT["tries"]):
+    for turn in range(OPT["tries"]):
         trial = dict(shift)
         for _ in range(1 + x % 2):
             x = (x * 1103515245 + 12345) % (1 << 31)
@@ -553,9 +564,99 @@ def schedule(ops):
             for k in steps[a:a + (1, 1, 1, 4, 12)[(x >> 12) % 5]]:
                 trial[k] = trial.get(k, 0.0) + by
         got = timetable(trial)
-        if got[1] <= best[1]:
-            best, shift = got, trial
+        if got[1] <= now + OPT["heat"] * (1.0 - turn / OPT["tries"]):
+            now, shift = got[1], trial
+            if now < best[1]:
+                best = got
+    OPT["shift"] = shift
     return best
+
+
+def refine(order):
+    sets = []
+    first = dict(PM)
+    for other in SPREAD:
+        PM.update(first); PM.update(other)
+        ops = build()
+        eng, cost, lat = ([o[k] for o in ops] for k in ("eng", "cost", "lat"))
+        sets.append((cost, lat, [[(j, cost[j] + lat[j] + (0.0 if ops[j]["kind"] == "send" or eng[j] + eng[i] == "PP" else PM["hop"]))
+                                  for j in o["deps"]] for i, o in enumerate(ops)]))
+    PM.update(first)
+    n = len(ops)
+    succ = [[] for _ in range(n)]
+    for i, o in enumerate(ops):
+        for j in o["deps"]:
+            succ[j].append(i)
+    turn = [-1 if o["tag"] == "set-up" else 2 * int(o["tag"][0]) + (3 if "out" in o["tag"] else int(o["tag"][2])) for o in ops]
+    at = {(ops[i]["key"], turn[i]): i for i in range(n)}
+
+    def run(key):
+        tail = {}
+        left = [len(o["deps"]) for o in ops]
+        nxt, prv = [-1] * n, [-1] * n
+        for _, i in sorted(zip(key, range(n))):
+            a = tail.get(eng[i], -1)
+            if a >= 0:
+                nxt[a] = i; prv[i] = a; left[i] += 1
+            tail[eng[i]] = i
+        todo = [i for i in range(n) if left[i] == 0]
+        for i in todo:
+            for j in succ[i] + ([nxt[i]] if nxt[i] >= 0 else []):
+                left[j] -= 1
+                if left[j] == 0:
+                    todo.append(j)
+        if len(todo) < n:
+            return None
+        total, waits, times = 0.0, [], None
+        for cost, lat, pred in sets:
+            st, why = [0.0] * n, [-1] * n
+            end, last = 0.0, 0
+            for i in todo:
+                t, y = 0.0, -1
+                for j, w in pred[i]:
+                    if st[j] + w > t:
+                        t, y = st[j] + w, j
+                j = prv[i]
+                if j >= 0 and st[j] + cost[j] > t:
+                    t, y = st[j] + cost[j], -2 - j
+                st[i], why[i] = t, y
+                if t + cost[i] + lat[i] > end:
+                    end, last = t + cost[i] + lat[i], i
+            while last != -1:
+                y = why[last]
+                if y <= -2:
+                    y = -2 - y
+                    waits.append((y, last))
+                last = y
+            total += end
+            times = times or st
+        for k, i in enumerate(todo):
+            times[i] += 1e-4 * k
+        return total / len(sets), times, waits
+
+    key = [0.0] * n
+    for k, (i, e, t) in enumerate(order):
+        key[i] = t + 1e-4 * k
+    best = run(key)
+    x = OPT["seed"]
+    for _ in range(OPT["swaps"]):
+        x = (x * 1103515245 + 12345) % (1 << 31)
+        a, b = best[2][(x >> 8) % len(best[2])]
+        x = (x * 1103515245 + 12345) % (1 << 31)
+        far, step = (0.01, 0.01, 200.0, 700.0)[(x >> 10) % 4], (0, 1, 2, 2)[(x >> 12) % 4]
+        key = list(best[1])
+        for d in (range(-12, 13, step) if step and min(turn[a], turn[b]) >= 0 else (0,)):
+            a2, b2 = at.get((ops[a]["key"], turn[a] + d)), at.get((ops[b]["key"], turn[b] + d))
+            if a2 is None or b2 is None or key[b2] < key[a2]:
+                continue
+            if (x >> 8) % 2:
+                key[b2] = key[a2] - far
+            else:
+                key[a2] = key[b2] + far
+        got = run(key)
+        if got and got[0] <= best[0]:
+            best = got
+    return [(i, eng[i], t) for t, i in sorted(zip(best[1], range(n)))], best[0]
 
 
 PLAN = []
@@ -567,14 +668,15 @@ def rank_program(g, core, T, topo):
         return
     if not PLAN:
         ops = build()
-        PLAN.append((ops, schedule(ops)[0]))
+        PLAN.append((ops, refine(schedule(ops)[0])[0]))
     ops, order = PLAN[0]
     n = len(T.cores)
-    nxt, prv = T.cores[(rank + 1) % n], T.cores[(rank - 1) % n]
+    nxt = T.cores[(rank + 1) % n]
     rid, pid = topo.addr(nxt, core)
+    narr = min(len(topo.engines(T.cores[i], T.cores[(i + 1) % n])) for i in range(n))
     eng = topo.engines(core, nxt)
-    mask = topo.mask(core, nxt)
-    narr = len(topo.engines(prv, core))
+    eng = eng[::len(eng) // narr]
+    mask = sum(1 << e for e in eng)
     Qs = {"V": g.vector, "S": g.scalar, "P": g.tensor, "G": g, "Y": g.sync}
 
     def ap(r):

import math
from concourse.mybir import AluOpType as OP, ActivationFunctionType as AF

HP = "float16"
BF, F32, I32, U16 = "bfloat16", "float32", "int32", "uint16"
VIS = 6
BIG = float(1 << 23)
MQ = 192
M1 = 1.5 * (1 << 23)
QO = 49152.0
MTW, M2W, AW, EQW = 136, 256, 400, 1040
XP = 256 * (VIS - 1)

PER_STREAM = {
    "TO": (2048, F32), "TV": (2048, F32), "W": (XP + 128 * VIS, F32),
    "WZ": (512, BF), "WN": (384, BF), "ZO": (128, BF), "ZV": (128, BF), "ZM": (128, F32),
    "MS": (MTW * VIS, HP), "ML": (MTW * (VIS + 1), HP), "M2": (M2W * VIS, BF), "L2": (192 * (VIS + 1), BF),
    "Q": (128, BF), "OFF": (128, U16), "G1": (2048, HP), "NB": (128, HP), "NH": (128, BF), "EP": (1024, BF), "EQ": (2 * EQW, BF),
    "YL": (128, F32), "LQ": (256, BF), "MK": (128, BF), "XI": (256, I32), "XJ": (128, I32), "POFF": (128, U16),
    "DD": (2048, BF), "AB": (2048, BF), "KS": (128, I32), "KA": (8, I32), "DOFF": (8, U16), "DFI": (AW, BF), "GE": (128, BF), "BB": (128, BF),
    "UY": (8, I32), "UQ": (8, F32), "UM": (8, I32), "UX": (8, I32), "UC": (8, I32), "XF": (8, F32), "HIP": (8, F32), "HI": (64, BF), "LO": (1024, BF),
    "FF": (8, I32), "DC": (8, I32), "DC2": (8, I32), "US": (8, I32), "SA": (8, F32), "RT": (96, HP), "DT": (128, HP),
    "WL": (88, F32), "WE": (88, F32), "ST": (88, F32), "POS": (8, U16), "SF": (8, F32), "SEL": (8, U16), "AC": (AW, BF),
    "ZN": (128, BF), "PZ": (128, HP),
}
SB = {"%s%d" % (k, s): v for k, v in PER_STREAM.items() for s in range(2)}
SB.update({
    "LO": (2048, BF), "LV": (2048, BF), "XO": (128, BF), "Z0": (256, BF), "NI": (256, I32), "NJ": (256, I32), "NP": (256, BF), "CI": (256, I32),
    "QD": (256, BF), "YO": (768, BF), "YV": (768, BF), "YN": (768, F32), "NW": (256, BF), "YZ": (256, BF), "YQ": (64, BF), "YC": (64, F32),
    "PI": (8, I32), "PJ": (16, I32), "COL": (64, F32), "IO": (160, F32), "I3": (128, I32), "J3": (256, I32), "K3": (384, BF), "K4": (256, BF), "TMP": (1344, F32),
    "ONE": (128, BF), "ZERO": (EQW, BF), "CST": (128, BF), "QOT": (256, HP), "NF": (8, BF), "ID": (128, BF), "NID": (128, BF), "HID": (128, BF), "IH": (128, HP), "IF": (128, F32),
    "REP": (128, BF), "NS": (16, HP), "P8": (8, BF), "WB": (144, BF), "SK": (256, BF), "BM": (1024, BF), "BD": (1024, HP), "BN": (128, BF), "NM": (2048, BF),
    "RE": (128, HP), "RS": (128, HP), "RX": (128, HP), "RA": (8, HP), "OM": (120, HP), "JT": (128, HP), "RK": (64, F32), "TX": (128, BF),
    "YT": (64, F32), "HL": (8, U16), "MTAB": (8, F32), "NBT": (128, BF), "NN": (8, BF), "OH": (16, F32),
})
PLACE = {}
_fill = {}
for _k, (_w, _d) in SB.items():
    if _w <= 128:
        PLACE[_k] = ("pk" + _d, _fill.get(_d, 0))
        _fill[_d] = _fill.get(_d, 0) + (_w + 15) // 16 * 16
    else:
        PLACE[_k] = (_k, 0)
SCRATCH = {k: ("sbuf", [128, w], d) for k, (w, d) in SB.items() if w > 128}
for _d, _w in _fill.items():
    SCRATCH["pk" + _d] = ("sbuf", [128, _w], _d)
for _i in range(8):
    SCRATCH["PS%d" % _i] = ("psum", [128, 512], F32)
DMAS = ["d%d" % i for i in range(100)]
SEMAPHORES = ["cV", "cS", "cP", "cG", "sent"] + DMAS + ["a%s%d%d" % (k, s, t) for k in "MX" for s in range(2) for t in range(VIS)]

PM = {"cy": 1.04, "hop": 170.0, "pe": 0.52, "ga": 1.56, "sc": 3.8, "link": 2200.0, "issue": 400.0, "dma": 2200.0}
SPREAD = ({}, {"cy": 0.9, "hop": 210.0, "pe": 0.46, "ga": 1.3, "link": 2000.0}, {"cy": 1.15, "hop": 120.0, "pe": 0.65, "ga": 1.7, "link": 2800.0})
OPT = {"heat": 0.0, "swaps": 2500, "seed": 5, "tries": 2500, "lead": 8500.0, "win": 200.0, "tol": 30.0, "g1": "S2 V2 S2 S2", "g1a": "S2 V2 S2 V2", "eq": "MV", "floor": "SS", "q": "S", "lq": "SS", "mk": "S", "g2": ((0, 256, 512, 1024), (0, 512, 768, 1024)), "zn": "S", "dt": "S", "tw": "SSSS", "we": "S", "dq": "S", "evac": "SVSS", "bm": "VVS", "nm": "VVS", "rt": "S"}
BOOST = {}


def R(n, a=0, b=None, s=1, p0=0, p1=128, ps=1):
    if b is None:
        b = 512 if n.startswith("PS") else SB[n][0]
    return (n, a, b, s, p0, p1, ps)


def IND(win, off):
    return ("ind", win, off)


def cnt(r):
    if r[0] == "ind":
        return 16 * cnt(r[2])
    return len(range(r[1], r[2], r[3]))


def two(r):
    return (not r[0].startswith("PS")) and SB[r[0]][1] in (BF, HP, U16)


def isap(x):
    return isinstance(x, tuple)


def flat(rs):
    o = []
    for r in rs:
        if isap(r):
            o += [r[1], r[2]] if r[0] == "ind" else [r]
    return o


def build():
    ops = []
    hist = {}
    bank = {}
    tag = ["set-up"]
    nth = {}
    CY = PM["cy"]

    def add(who, cost, kind, args, reads, writes, lat=0.0, extra=()):
        i = len(ops)
        deps = set(extra)
        wr = []
        for w in writes:
            if w[0] == "ind":
                wr.append(w[1]); reads = list(reads) + [w[2]]
            else:
                wr.append(w)
        for isw, lst in ((False, flat(reads)), (True, wr)):
            for r in lst:
                h = hist.setdefault(r[0], [])
                lo, hi, pl, ph = r[1], r[2], r[4], r[5]
                for (j, w2, a, b, c, d) in h:
                    if j != i and (isw or w2) and a < hi and lo < b and c < ph and pl < d:
                        deps.add(j)
                if isw and r[3] == 1 and r[6] == 1:
                    h[:] = [e for e in h if not (lo <= e[2] and e[3] <= hi and pl <= e[4] and e[5] <= ph)]
                h.append((i, isw, lo, hi, pl, ph))
                if r[0].startswith("PS"):
                    st = bank.setdefault(r[0], [None, [], []])
                    if st[0] != who:
                        st[0], st[2], st[1] = who, st[1], []
                    deps.update(j for j in st[2] if j != i)
                    if who == "P":
                        deps.update(st[1][-1:] if i not in st[1] else [])
                    if i not in st[1]:
                        st[1].append(i)
        ops.append({"eng": who, "cost": cost, "kind": kind, "args": args, "deps": deps, "lat": lat, "tag": tag[0]})
        nth[tag[0]] = nth.get(tag[0], 0) + 1
        ops[-1]["key"] = "%s%d" % (tag[0].split()[-1], nth[tag[0]])
        return i

    def vcost(out, ins, tt=False):
        n = cnt(out)
        if out[0] == "ind":
            return 50 + PM["sc"] * n * CY
        if any(x[0] == "ind" for x in ins):
            return 50 + PM["ga"] * n * CY
        if tt:
            rate = 1.0 if any(x[0].startswith("PS") for x in ins) else 2.0
        else:
            rate = 0.5 if two(out) and all(two(x) for x in ins) else 1.0
        return max(64, n * rate) * CY

    def scost(out, in_):
        return (65 + PM["ga"] * cnt(out) * CY) if in_[0] == "ind" else max(64, cnt(out)) * CY

    def ts(out, in0, s1, op0, s2=None, op1=None):
        return add("V", vcost(out, [in0]), "ts", (out, in0, s1, s2, op0, op1), [in0, s1, s2], [out])

    def tt(out, a, b, op):
        return add("V", vcost(out, [a, b], True), "tt", (out, a, b, op), [a, b], [out])

    def cp(out, in_, e="V"):
        return add(e, vcost(out, [in_]) if e == "V" else scost(out, in_), "cp", (out, in_), [in_], [out])

    def act(out, in_, f, bias=0.0, scale=1.0, more=0.0, after=()):
        return add("S", scost(out, in_) + more, "act", (out, in_, f, bias, scale), [in_, bias, scale], [out], 0.0, after)

    def aff(out, in_, scale, bias=0.0, e="V"):
        return ts(out, in_, scale, OP.mult, bias, OP.add) if e == "V" else act(out, in_, AF.Identity, bias, scale)

    def scan(out, d0, d1, init, op0, op1):
        return add("V", vcost(out, [d0, d1]), "scan", (out, d0, d1, init, op0, op1), [d0, d1], [out])

    def ms(out, v):
        if not out[0].startswith("PS") and SB[out[0]][1] == HP:
            return ts(out, R("ONE", 0, cnt(out), 1, out[4], out[5]), v, OP.mult)
        return add("V", vcost(out, []), "ms", (out, v), [], [out])

    def iota(out, pat, base, cm=0):
        return add("G", 130 + 2 * cnt(out) * CY, "iota", (out, pat, base, cm), [], [out])

    def mm(groups, start=True, stop=True):
        c = 0; rd = []; wr = []
        for out, terms in groups:
            for x in terms:
                l, r = x[0], x[1]
                wr.append(x[2] if len(x) > 2 else out)
                c += max(min(64, cnt(l)), cnt(r)) * (4 if SB[r[0]][1] == F32 else 1) * PM["pe"]
                rd += [l, r]
        return add("P", c, "mm", (groups, start, stop), rd, wr)

    nd = [0]

    def dma(q, out, in_, lat=None):
        nd[0] += 1
        return add(q, 60.0, "dma", (out, in_, DMAS[nd[0] - 1]), [in_] if in_[0] != "in" else [], [out] if out[0] != "out" else [], lat or PM["dma"])

    def send(name, src, dst):
        i = add("G", PM["issue"], "send", (src, dst, name), [src], [])
        return add("N", 0.0, "recv", (name,), [], [dst], PM["link"], [i])

    A, S_, Mu, Mx, Mn = OP.add, OP.subtract, OP.mult, OP.max, OP.min
    EQL, AND, SHR = OP.is_equal, OP.bitwise_and, OP.arith_shift_right
    col = lambda j, p0=0, p1=128: R("COL", j, j + 1, p0=p0, p1=p1)
    blk = lambda n, j: R(n, 128 * j, 128 * j + 128)
    ID, NID, HID, IH, IF, REP, ONE = (R(n) for n in ("ID", "NID", "HID", "IH", "IF", "REP", "ONE"))
    wide = lambda b: R("WB", 16 - b, 144 - b)
    half = lambda n, s, a, b, st=1: R(n, a, b, st, 64 * s, 64 * s + 64)
    banks = lambda s: ["PS%d" % (4 * s + j) for j in range(4)]

    ms(R("CI", p1=64), 0)
    ms(ONE, 1.0)
    for s in range(2):
        for pc in range(2):
            dma("YS"[pc], half("NI", pc, 128 * s, 128 * s + 128), ("in", "nm", 4 * s, 4 * s + 4))
        for q in range(2):
            dma("YS"[q], half("LO", s, 1024 * q, 1024 * q + 1024), ("in", "vo", 64 * s, 64 * s + 64, 1024 * q, 1024 * q + 1024), 2600.0)
        for gq in range(4 * s, 4 * s + 4):
            dma("Y", R("CI", 32 * gq, 32 * gq + 32, p0=0, p1=8), ("in", "c0", gq, gq + 1))
            dma("S", R("CI", 32 * gq, 32 * gq + 32, p0=32, p1=40), ("in", "s0", gq, gq + 1))
        dma("Y", half("LV", s, 0, 2048), ("in", "vn", 64 * s, 64 * s + 64), 3000.0)
    dma("Y", R("XO"), ("in", "xo", 0, 128))
    dma("Y", R("Z0"), ("in", "z0", 0, 128))

    PI = R("PI", 0, 1)
    iota(PI, [[0, 1]], 0, 1)
    iota(R("IO"), [[1, 160]], -16)
    C0 = R("IO", 16, 144)
    T_ = lambda j: blk("TMP", j)
    cp(col(0), PI)
    for j, (sh, mk) in enumerate(((0, 15), (0, 112), (0, 63), (6, 1), (0, 7), (3, 15), (0, 48))):
        ts(R("PJ", j, j + 1), PI, sh, SHR, mk, AND)
    cp(R("COL", 1, 8), R("PJ", 0, 7))
    tt(col(8), col(7), col(4), A)
    iota(T_(0), [[0, 2], [1, 64]], 0)
    ts(REP, T_(0), col(3), EQL)
    ts(R("BN"), T_(0), col(8), EQL, 256.0, Mu)
    ts(R("COL", 16, 32), R("IO", 16, 32), col(1), EQL)
    for eh in range(16):
        aff(blk("NM", eh), R("BN"), col(16 + eh), 0.0, OPT["nm"][eh % len(OPT["nm"])])
    ts(half("NJ", 0, 0, 256), half("NI", 0, 0, 256), 7, AND); ts(half("NJ", 1, 0, 256), half("NI", 1, 0, 256), 3, SHR)
    ts(col(34), col(4), -0.5, Mu, -7.5, A); ts(R("NP"), R("NJ"), col(34), A)
    oh = lambda j: R("OH", j, j + 1)
    ts(R("OH"), R("IO", 16, 32), col(6), EQL)
    tt(col(9), oh(2), oh(4), A)
    tt(col(10), oh(0), oh(1), A); tt(col(10), col(10), oh(12), S_); ts(col(11), oh(2), 16.0, Mu, col(10), A)
    ts(col(12), col(0), 40.0, EQL, 2048.0, Mu); ts(col(13), col(0), 41.0, EQL, -1369.0, Mu)
    tt(col(14), oh(3), oh(8), S_)
    ts(col(15), col(12), MQ / 2048.0, Mu); ts(col(32), col(13), -256.0 / 1369.0, Mu, col(15), A)
    iota(T_(1), [[1, 8], [0, 16]], 0); iota(T_(2), [[0, 8], [-1, 16]], 15)
    ts(T_(1), T_(1), col(5), EQL)
    ts(T_(2), T_(2), col(9), Mu, col(11), A); tt(T_(2), T_(2), T_(1), Mu); ts(R("RE"), T_(2), col(12), A)
    ts(R("RS"), T_(1), col(9), Mu); ts(R("RX"), R("RS"), -144.0, Mu)
    ts(R("TMP", 1008, 1016), R("TMP", 128, 256, 16), col(14), Mu, 32.0, Mu); ts(R("RA"), R("TMP", 1008, 1016), col(13), A)
    ts(ID, C0, col(0), EQL); aff(NID, ID, -1.0); aff(HID, ID, 0.5); cp(IH, ID); cp(IF, ID, "S")
    for s in range(2):
        ms(half("ML%d" % s, 1, 0, 128), 0.0)
        for h in range(2):
            ts(half("ML%d" % s, 0, 64 * h, 64 * h + 64), half("CI", 0, 128 * s + h, 128 * s + 128, 2), col(32, 0, 64), A)

    def table(s, dst, src, qs):
        for q in qs:
            ps = banks(s)[2 + q % 2]
            mm([(R(ps), [(half("REP", s, 0, 128), half(src, s, 512 * q, 512 * q + 512))] +
                 [(blk("NM", 4 * q + j), blk("NP", s), blk(ps, j)) for j in range(4)])])
            cp(R(dst, 512 * q, 512 * q + 512), R(ps), OPT["evac"][q])

    table(0, "TO0", "LO", range(4))

    U = lambda a, b, st=1: R("TMP", 1280 + a, 1280 + b, st)
    iota(U(0, 16), [[1, 2], [16, 8]], 0)
    ts(R("NS", 0, 8), U(0, 8), col(0), EQL, (1 - 2.0 ** -11) / 256, Mu); ts(R("NS", 8, 16), U(8, 16), col(0), EQL, 1.0 / 256, Mu)
    ts(R("P8"), U(0, 8), col(0), EQL)
    ts(R("NN"), U(8, 16), col(0), EQL, 8.0, Mu); tt(R("NN"), R("NN"), R("P8"), A); ts(R("NN"), R("NN"), 1.0 / 256, Mu)
    ts(R("WB"), R("IO", 0, 144), col(2), EQL, 2048.0, Mu)
    iota(U(16, 24), [[0, 2], [-16, 4]], 43); ts(U(16, 24), U(16, 24), col(1), S_)
    ts(col(33), col(1), -2.0, Mu, 43.0, A); tt(U(24, 25), col(33), col(4), S_)
    e1 = act(U(32, 41), U(16, 25), AF.Exp, 0.0, 1.0, 1300.0)
    iota(T_(3), [[1, 16], [0, 8]], 0); iota(T_(4), [[1, 16], [1, 8]], -7); iota(T_(5), [[-1, 16], [1, 8]], -7)
    iota(T_(6), [[0, 16], [-1, 8]], 115); iota(T_(7), [[-1, 16], [2, 8]], 102)
    K3 = lambda j: blk("K3", j)
    ts(col(35), col(1), -1.0, Mu)
    ts(K3(0), T_(3), col(1), EQL)
    act(T_(3), T_(4), AF.Abs, col(35)); ts(K3(1), T_(3), 8.0, EQL)
    act(T_(5), T_(5), AF.Abs, col(1)); ts(K3(2), T_(5), 8.0, EQL)
    tt(blk("SK", 0), K3(0), K3(1), S_)
    ts(T_(4), T_(4), 7.5, OP.is_lt, 16.0, Mu); tt(T_(4), T_(4), T_(6), A); tt(T_(4), T_(4), K3(0), Mu)
    act(T_(7), T_(7), AF.Identity, col(1)); tt(T_(7), T_(7), K3(2), Mu); tt(T_(4), T_(4), T_(7), A)
    ts(R("TMP", 512 + 7, 640, 8), R("TMP", 512 + 7, 640, 8), -math.log(2.0), A)
    act(blk("SK", 1), T_(4), AF.Exp, -100.0, after=[e1])
    ts(R("COL", 36, 44), U(0, 8), col(2), EQL)
    for gq in range(8):
        for j, k in enumerate(("BD", "BM")):
            aff(blk(k, gq), blk("SK", j), col(36 + gq), 0.0, OPT["bm"][(2 * gq + j) % len(OPT["bm"])])
    table(0, "TV0", "LV", range(4))
    table(1, "TO1", "LO", range(4))
    iota(T_(8), [[16, 128]], 0); act(R("JT"), T_(8), AF.Identity, col(1))
    ms(R("RK"), 0.0); ms(R("RK", 0, 64, 16), -16 * BIG)
    ms(R("CST"), -0.5); iota(R("NF"), [[0, 8]], -15360); iota(R("ZERO"), [[0, EQW]], 0)
    ts(col(47), col(16), 128.0, Mu, QO, A); act(R("QOT"), R("ZERO", 0, 256), AF.Identity, col(47))
    iota(T_(9), [[0, 2], [64, 4], [1, 16]], 0)
    ts(col(48), col(7), -4.0, Mu); act(R("TX"), T_(9), AF.Identity, col(48))
    iota(R("YT"), [[0, 8], [1, 2], [32, 4]], 0)
    iota(U(48, 52), [[2, 4]], 0); ts(col(44), col(1), 7.5, OP.is_gt); ts(R("HL", 0, 4), U(48, 52), col(44), A)
    ts(col(45), col(1), 2.0, Mu); ts(R("MTAB"), R("YT", 0, 8), col(45), A)
    ts(col(46), col(4), -1.0, Mu, 44.47, A)
    iota(R("I3"), [[1, 128]], 0)
    ts(blk("J3", 0), R("I3"), 7, AND); ts(blk("J3", 1), R("I3"), 3, SHR)
    ts(blk("K4", 0), blk("J3", 0), -7.5, A, col(16), Mu); ts(blk("K4", 1), blk("J3", 1), -8.0, A, col(17), Mu); tt(blk("K4", 0), blk("K4", 0), blk("K4", 1), A)
    aff(R("NBT"), blk("K4", 0), 256.0, 0.0, "S")
    cp(half("NW", 0, 0, 256), half("NI", 0, 0, 256))
    for s in range(2):
        pA, pB, pC, pD = banks(s)
        n = lambda k: "%s%d" % (k, s)
        ms(R(pA, 384, 512), 1.0)
        ms(R(pB, 400, 488), 0.0)
        cp(R(pB, 402, 444, 11), U(32, 36)); cp(R(pB, 444, 488, 11), U(36, 40))
        ms(R(n("RT")), 0.0); ms(R(n("RT"), 40, 41), float(MQ)); ms(R(n("RT"), 41, 42), 256.0); ms(R(n("RT"), 64, 72), 1.0)
        dma("Y", R(n("DFI")), R("ZERO", 0, AW)); dma("Y", R(n("AC")), R("ZERO", 0, AW)); dma("Y", R(n("LQ")), R("ZERO", 0, 256))
        for q in range(2):
            dma("Y", R(n("EQ"), EQW * q, EQW * q + EQW), R("ZERO"))
        mm([(R(pD, 0, 128), [(half("REP", s, 0, 128), half("XO", s, 0, 128)), (ID, R("NBT"))])])
        cp(R(n("W"), XP, XP + 128), R(pD, 0, 128), "S")
        for h in range(2):
            dma("Y", half(n("WZ"), h, 384, 512), ("in", "xo", 64 * s, 64 * s + 64))
        dma("Y", R(n("WZ"), 0, 128), blk("LO", VIS - 1)); dma("Y", R(n("WZ"), 128, 256), blk("LV", VIS - 1))
        iota(R(n("WN")), [[0, 3], [1, 128]], 0)
        dma("Y", R(n("WN"), 0, 128, p0=0, p1=64, ps=16), R("NW", 128 * s, 128 * s + 128, p0=VIS - 1, p1=64, ps=16))
        mm([(half(pC, h, 0, 128), [(half("ID", s, 64 * s, 64 * s + 64), half("Z0", s, h, 256, 2))]) for h in range(2)])
        cp(R(n("L2"), 64, 192), R(pC, 0, 128), "S")
    table(1, "TV1", "LV", range(4))
    for s in range(2):
        for t in range(VIS - 1):
            for j, k in enumerate(("TO", "TV")):
                dma("Y", blk("W%d" % s, 2 * t + j), blk("%s%d" % (k, s), t))
    ms(R("OM"), 0.0)
    for j, c in enumerate((11, 9, 14)):
        ts(R("OM", 24 + 32 * j, 32 + 32 * j), R("TMP", 128, 256, 16), col(c), Mu, col(12), A)

    def visit(s, t):
        last = t == VIS - 1
        pA, pB, pC, pD = banks(s)
        H = lambda k, a=0, b=None, st=1: R("%s%d" % (k, s), a, b, st)
        MT = H("ML", MTW * t, MTW * t + 128)
        Z = H("L2", 192 * t + 64, 192 * t + 192)
        MS = lambda a, b: H("MS", MTW * t + a, MTW * t + b)
        M2 = lambda a, b: H("M2", M2W * t + a, M2W * t + b)
        E2, SBC, EX, A32 = R(pB, 0, 128), R(pB, 128, 384, 2), R(pB, 129, 384, 2), R(pB, 384, 392)
        tag[0] = "%d.%d places" % (t, s)
        mm([(R(pA, 256, 384), [(MT, R("RE"))])])
        aff(H("Q"), R(pA, 256, 384), 1.0, -1023.625, OPT["q"])
        mm([(SBC, [(MT, R("RS"))]), (EX, [(MT, R("RE")), (MT, R("RX"))]), (A32, [(MT, R("RA"))])])
        mm([(E2, [(MT, R("RE"))])], True, False)
        mm([(E2, [(NID, H("Q"))])], False, True)
        cp(H("OFF"), E2)
        cp(H("RT", 8, 16), R(pB, 15, 128, 16), OPT["rt"]); cp(H("RT", 16, 24), R(pB, 128, 384, 32), OPT["rt"])
        if s == 1 and t > 0:
            outputs(t - 1)
        tag[0] = "%d.%d names" % (t, s)
        a = 0
        alone = (t, s) in ((0, 0), (VIS - 1, 1))
        for piece in OPT["g1a" if alone else "g1"].split():
            b = a + 256 * int(piece[1])
            cp(H("G1", a, b), IND(H("TO"), H("OFF", a // 16, b // 16)), piece[0])
            a = b
        for q, pq in enumerate((pC, pD)):
            a, e0 = 64 * q, EQW * q
            Hq = lambda k: H(k, a, a + 64)
            mm([(half(pq, b % 2, b // 2, 128, 8), [(H("G1", 1024 * q + b, 1024 * q + 1024, 16), R("NS"))]) for b in range(16)])
            aff(Hq("NH"), R(pq, 64, 128), 8.0, 1148.015625, OPT["floor"][q]); tt(Hq("NB"), R(pq, 0, 64), Hq("NH"), A)
            mm([(R(pq, 64 * d, 64 * d + 64), [(R("BD", d, 1024, 8), Hq("NB"))]) for d in range(8)])
            eq, ep = H("EQ", e0 + 1, e0 + 1025, 2), H("EP", 512 * q, 512 * q + 512)
            if OPT["eq"][q] == "V":
                ts(eq, R(pq), 0.0, EQL)
            else:
                act(ep, R(pq), AF.Abs)
                ts(eq, ep, 0.0, EQL) if OPT["eq"][q] == "M" else act(eq, ep, AF.Relu, 1.0, -1.0)
            mm([(R(pq, 0, 64), [(H("EQ", e0 + 128 * d + 1 - be, e0 + 128 * d + 129 - be), R("BM", 512 * be + d, 512 + 512 * be, 8))
                                for d in range(8) for be in range(2)])])
            act(Hq("YL"), R(pq, 0, 64), AF.Ln, 1.0, 1.0, 1500.0 if t + s + q == 0 else 0.0)
            lq = H("LQ", 2 * a + 1, 2 * a + 128, 2)
            aff(lq, Hq("YL"), 1.0, 143.77, OPT["lq"][q])
            scan(H("XI", 2 * a, 2 * a + 128), H("LQ", 2 * a, 2 * a + 128), R(pB, 128 + 2 * a, 256 + 2 * a), 0.0, Mu, A)
            ts(Hq("XJ"), H("XI", 2 * a + 1, 2 * a + 128, 2), 2047, AND); cp(Hq("POFF"), Hq("XJ"))
            if OPT["mk"] == "V":
                ts(Hq("MK"), lq, 160.5, OP.is_gt, 4 * BIG, Mu)
            else:
                act(Hq("MK"), lq, AF.Relu, -640.0 * BIG, 4 * BIG)
        tag[0] = "%d.%d sums" % (t, s)
        for q, pq in enumerate((pC, pD)):
            o = R(pq, 64, 128)
            cuts = [1024 * q + c for c in OPT["g2"][q]]
            for a, b in zip(cuts, cuts[1:]):
                tt(H("DD", a, b), IND(H("TV"), H("POFF", a // 16, b // 16)), H("G1", a, b), S_)
                act(H("AB", a, b), H("DD", a, b), AF.Abs)
            mm([(o, [(IH, R("JT", 64 * q, 64 * q + 64)), (NID, H("MK", 64 * q, 64 * q + 64))])], True, False)
            mm([(o, [(wide(b), H("AB", 1024 * q + b, 1024 * q + 1024, 16)) for b in range(16)])], False, True)
            scan(H("KS", 64 * q, 64 * q + 64), R("RK"), o, 0.0, A, Mx)
        KI = H("KS", 15, 128, 16)
        tag[0] = "%d.%d fire" % (t, s)
        ts(H("KA"), KI, 2047, AND); cp(H("DOFF"), H("KA"))
        tt(H("GE"), IND(H("AB"), H("DOFF")), Z, OP.is_lt)
        cp(H("DFI", 1, 257, 2), IND(H("DD"), H("DOFF")), "S")
        mm([(R(pD, 0, 8), [(ID, R("NF"))] + [(wide(b), H("GE", b, 128, 16)) for b in range(16)])])
        ts(H("UY"), KI, 1.0 / 2048, Mu, -(1456 + 1023.5 / 2048), A)
        tt(H("UQ"), H("UY"), H("UY"), Mu); tt(H("UM"), H("UQ"), A32, A)
        ts(H("UX"), H("UM"), 6, SHR, 15, AND); cp(H("XF"), H("UX")); ts(H("UC"), H("UM"), 5, SHR, 97, AND)
        for r8 in range(8):
            ts(H("LO", 128 * r8, 128 * r8 + 128), R("TX"), H("XF", r8, r8 + 1), EQL, U(40, 41), Mu)
        tt(H("HIP"), R(pD, 0, 8), H("UC"), Mx)
        tt(H("HI"), IND(H("HIP"), R("HL", 0, 4)), R("YT"), EQL)
        tag[0] = "%d.%d who" % (t, s)
        mm([(R(pB, 410 - r8, 488, 11), [(H("LO", 128 * r8, 128 * r8 + 128), H("HI", 8 * r8, 8 * r8 + 8))]) for r8 in range(8)])
        act(H("WL"), R(pB, 400, 488), AF.Ln, math.exp(-32.0))
        if OPT["we"] == "V":
            ts(H("WE"), H("WL"), -30.0, OP.is_lt)
        else:
            act(H("WE"), H("WL"), AF.Relu, -15.0, -0.5)
        scan(H("ST"), H("WE"), H("WL"), 0.0, Mu, A)
        ST = H("ST", 10, 88, 11)
        ts(H("POS"), ST, -1.0, Mu, col(46), A)
        cp(IND(H("AC"), H("POS")), ONE)
        ts(H("RT", 24, 32), H("HIP"), 127.5, OP.is_lt)
        ts(H("FF"), KI, 4, SHR, 15, AND); tt(H("DC"), H("FF"), H("RT", 16, 24), Mu); ts(H("DC2"), H("DC"), 2047, AND); cp(H("RT", 0, 8), H("DC2"))
        ts(H("US"), KI, 11, SHR, 511, AND); ts(H("SA"), H("US"), 2.0, Mu, 1.0, A); tt(H("RT", 32, 40), H("SA"), H("RT", 16, 24), S_)
        mm([(R(pD, 128, 256, p1=96), [(H("RT", 0, 96), IH)]), (R(pD, 128, 256, p0=96), [(H("RT", 0, 32), IH)])])
        cp(H("DT"), R(pD, 128, 256), OPT["dt"])
        mm([(R(pA, 384 + b, 512, 16, q0, q0 + 8), [(H("AC", 1 + 2 * b, 257, 32), R("P8"))]) for q0 in (0, 32, 64) for b in range(16)])
        tt(MS(0, 128), R(pA, 384, 512), H("DT"), Mu)
        ts(H("SF"), ST, -212.5, OP.is_gt, 256.0 if last else float(XP - 128 * t), Mu); tt(MS(128, 136), H("SF"), R("MTAB"), A)
        a0 = 128 if last else 0
        send("aM%d%d" % (s, t), MS(a0, MTW), H("ML", MTW * (t + 1) + a0, MTW * (t + 2)))
        tag[0] = "%d.%d act" % (t, s)
        cp(H("SEL", 0, 4), MS(128, 132))
        cp(M2(0, 128), IND(H("DFI"), H("POS")), "S")
        act(H("BB"), H("DFI", 1, 257, 2), AF.Abs)
        if OPT["zn"] == "S":
            act(H("ZN"), Z, AF.Relu, -1.0)
        else:
            ts(H("ZN"), Z, -1.0, A, 0.0, Mx)
        mm([(R(pC, 128, 256), [(HID, Z), (HID, R("CST", 0, 128)), (NID, H("ZN")), (HID, H("BB"))])])
        tt(H("PZ"), R(pC, 128, 256), H("AC", 1, 257, 2), Mu)
        if not last:
            dma("Y", H("AC"), R("ZERO", 0, AW))
            mm([(R(pC, 256, 384), [(ID, H("ZN")), (IH, H("PZ"))])])
            ts(M2(128, 256), R(pC, 256, 384), M1, A, M1, S_)
        else:
            mm([(half(pC, s, 256 + h, 512, 2), [(R("ID", 64 * h, 64 * h + 64), H("ZN")), (R("IH", 64 * h, 64 * h + 64), H("PZ"))]) for h in range(2)])
            ts(half("YZ", s, 0, 256), half(pC, s, 256, 512), M1, A, M1, S_)
            dma("Y", ("out", "yz", 64 * s, 64 * s + 64), half("YZ", s, 0, 256))
        w2 = 64 if last else 192
        send("aX%d%d" % (s, t), M2(64, 64 + w2), H("L2", 192 * (t + 1), 192 * (t + 1) + w2))
        cp(H("SEL", 4, 8), H("ML", MTW * (t + 1) + 132, MTW * (t + 1) + 136))
        xc = XP + 128 * t
        sel = lambda par: H("SEL", 4 * par, 4 * par + 4)
        pl = lambda k, par: H(k, 128 * t + par, 128 * t + 128, 2)
        x0, x1 = (H("WZ", 256 + 128 * (u % 2), 384 + 128 * (u % 2)) for u in (t + 1, t))
        for par in range(2):
            if not last:
                cp(pl("TO", par), IND(H("W", 256 * t, xc + 128), sel(par)), OPT["tw"][par])
            else:
                cp(H("ZO", par, 128, 2), IND(H("WZ", 0, 384), sel(par)), "SV"[par])
                cp(H("ZM", par, 128, 2), IND(H("WN"), sel(par)), "S")
        o = R(pD, 256, 384)
        mm([(o, [(ID, x0), (REP, M2(0, 64), R(pD, 256, 384, 2))])], True, False)
        mm([(o, [(REP, H("L2", 192 * (t + 1), 192 * (t + 1) + 64), R(pD, 257, 384, 2))])], False, True)
        ts(x1, o, 0.0, Mx, 255.0, Mn)
        if not last:
            mm([(o, [(ID, R("NBT")), (ID, x1)])])
            cp(H("W", xc + 128, xc + 256), o, "S")
        for par in range(2):
            if not last:
                cp(pl("TV", par), IND(H("W", 256 * t + 128, xc + 256), sel(par)), OPT["tw"][2 + par])
            else:
                cp(H("ZV", par, 128, 2), IND(H("WZ", 128, 512), sel(par)), "SV"[par])
        if last:
            dma("Y", ("out", "yo", 64 * s, 64 * s + 64, 128 * t, 128 * VIS), half("ZO%d" % s, s, 0, 128))
            dma("Y", ("out", "yn", 4 * s, 4 * s + 4, 128 * t, 128 * VIS), R("ZM%d" % s, p0=0, p1=64, ps=16))
            dma("Y", ("out", "yx", 64 * s, 64 * s + 64), half("WZ%d" % s, s, 384, 512))
            dma("S", ("out", "yv", 64 * s, 64 * s + 64, 128 * t, 128 * VIS), half("ZV%d" % s, s, 0, 128))
            o = lambda h: R(pA, h, 32, 2, 0, 96)
            mm([(o(h), [(R("OM", 24 - 8 * gq, 120 - 8 * gq), MS(64 * h + 16 * gq, 64 * h + 16 * gq + 16)) for gq in range(4)]) for h in range(2)])
            a, b = 32 * s, 32 * s + 32
            aff(R("YQ", a, b, p1=96), R(pA, 0, 32, p1=96), 1.0, -1023.625, "V")
            tt(R("YC", a, b, p1=96), R(pA, 0, 32, p1=96), R("YQ", a, b, p1=96), S_)
            for j, k in enumerate(("yc", "ys", "ya")):
                dma("YS"[j % 2], ("out", k, 4 * s, 4 * s + 4), R("YC", a, b, p0=32 * j, p1=32 * j + 32))

    def outputs(t):
        tag[0] = "%d out" % t
        pA = banks(1)[0]
        a, b = 128 * t, 128 * t + 128
        mm([(half(pA, s, 0, 256), [(R("IH", 0, 64), R("QOT"))] +
             [(R("IF", 0, 64), R("%s%d" % (k, s), a, b), half(pA, s, 128 * j, 128 * j + 128)) for j, k in enumerate(("TO", "TV"))]) for s in range(2)])
        aff(R("QD"), R(pA, 0, 256), 1.0, -127.5, OPT["dq"])
        tt(R("YO", a, b), R(pA, 0, 128), R("QD", 0, 128), S_); tt(R("YV", a, b), R(pA, 128, 256), R("QD", 128, 256), S_)
        mm([(R(pA, 256, 384, p1=8), [(R("NN"), R("QD", 0, 128))])])
        aff(R("YN", a, b, p1=8), R(pA, 256, 384, p1=8), 1.0, 71.0 - 9.0 * QO / 256, "S")
        if t == VIS - 2:
            dma("Y", ("out", "yo", 0, 128, 0, b), R("YO", 0, b))
            dma("Y", ("out", "yv", 0, 128, 0, b), R("YV", 0, b))
            dma("Y", ("out", "yn", 0, 8, 0, b), R("YN", 0, b, p1=8))

    for t in range(VIS):
        visit(0, t)
        visit(1, t)
    return ops


def schedule(ops):
    n = len(ops)
    eng, cost, lat, key = ([o[k] for o in ops] for k in ("eng", "cost", "lat", "key"))
    succ = [[] for _ in range(n)]
    for i, o in enumerate(ops):
        for j in o["deps"]:
            succ[j].append((i, lat[j] + (0.0 if ops[j]["kind"] == "send" or eng[j] + eng[i] == "PP" else PM["hop"])))
    chain = [0.0] * n
    for i in range(n - 1, -1, -1):
        chain[i] = cost[i] + max([chain[j] + w for j, w in succ[i]] + [lat[i]])
    chain = [chain[i] + (OPT["lead"] if ".0 " in ops[i]["tag"] else 0.0) - 1e-3 * i for i in range(n)]
    win, tol = OPT["win"], OPT["tol"]

    def timetable(shift):
        prio = [chain[i] + shift.get(key[i], 0.0) for i in range(n)]
        left = [len(o["deps"]) for o in ops]
        due = [0.0] * n
        ready = {e: [] for e in "NVSPGY"}
        for i in range(n):
            if left[i] == 0:
                ready[eng[i]].append(i)
        free = {e: 0.0 for e in ready}
        soon = {e: 0.0 if c else 1e18 for e, c in ready.items()}
        order = []
        end = 0.0
        for _ in range(n):
            e = min(soon, key=soon.get)
            t0, c = soon[e], ready[e]
            i = c[0]
            if len(c) > 1:
                i = max([i for i in c if due[i] <= t0 + win], key=lambda j: prio[j])
                if due[i] > t0 + 20.0:
                    fill = [j for j in c if max(due[j], t0) + cost[j] <= due[i] + tol]
                    if fill:
                        i = max(fill, key=lambda j: prio[j])
            c.remove(i)
            st = max(t0, due[i])
            f = free[e] = st + cost[i]
            soon[e] = max(f, min([due[j] for j in c])) if c else 1e18
            if f + lat[i] > end:
                end = f + lat[i]
            order.append((i, e, st))
            for j, w in succ[i]:
                if f + w > due[j]:
                    due[j] = f + w
                left[j] -= 1
                if left[j] == 0:
                    ready[eng[j]].append(j)
                    soon[eng[j]] = min(soon[eng[j]], max(free[eng[j]], due[j]))
        return order, end

    steps = list(dict.fromkeys(key))
    shift = dict(BOOST)
    best = timetable(shift)
    now = best[1]
    x = OPT["seed"]
    for turn in range(OPT["tries"]):
        trial = dict(shift)
        for _ in range(1 + x % 2):
            x = (x * 1103515245 + 12345) % (1 << 31)
            k = steps[(x >> 8) % len(steps)]
            x = (x * 1103515245 + 12345) % (1 << 31)
            by = (-6000.0, -2000.0, -700.0, -250.0, 250.0, 700.0, 2000.0, 6000.0)[(x >> 8) % 8]
            a = steps.index(k)
            for k in steps[a:a + (1, 1, 1, 4, 12)[(x >> 12) % 5]]:
                trial[k] = trial.get(k, 0.0) + by
        got = timetable(trial)
        if got[1] <= now + OPT["heat"] * (1.0 - turn / OPT["tries"]):
            now, shift = got[1], trial
            if now < best[1]:
                best = got
    OPT["shift"] = shift
    return best


def refine(order):
    sets = []
    first = dict(PM)
    for other in SPREAD:
        PM.update(first); PM.update(other)
        ops = build()
        eng, cost, lat = ([o[k] for o in ops] for k in ("eng", "cost", "lat"))
        sets.append((cost, lat, [[(j, cost[j] + lat[j] + (0.0 if ops[j]["kind"] == "send" or eng[j] + eng[i] == "PP" else PM["hop"]))
                                  for j in o["deps"]] for i, o in enumerate(ops)]))
    PM.update(first)
    n = len(ops)
    succ = [[] for _ in range(n)]
    for i, o in enumerate(ops):
        for j in o["deps"]:
            succ[j].append(i)
    turn = [-1 if o["tag"] == "set-up" else 2 * int(o["tag"][0]) + (3 if "out" in o["tag"] else int(o["tag"][2])) for o in ops]
    at = {(ops[i]["key"], turn[i]): i for i in range(n)}

    def run(key):
        tail = {}
        left = [len(o["deps"]) for o in ops]
        nxt, prv = [-1] * n, [-1] * n
        for _, i in sorted(zip(key, range(n))):
            a = tail.get(eng[i], -1)
            if a >= 0:
                nxt[a] = i; prv[i] = a; left[i] += 1
            tail[eng[i]] = i
        todo = [i for i in range(n) if left[i] == 0]
        for i in todo:
            for j in succ[i] + ([nxt[i]] if nxt[i] >= 0 else []):
                left[j] -= 1
                if left[j] == 0:
                    todo.append(j)
        if len(todo) < n:
            return None
        total, waits, times = 0.0, [], None
        for cost, lat, pred in sets:
            st, why = [0.0] * n, [-1] * n
            end, last = 0.0, 0
            for i in todo:
                t, y = 0.0, -1
                for j, w in pred[i]:
                    if st[j] + w > t:
                        t, y = st[j] + w, j
                j = prv[i]
                if j >= 0 and st[j] + cost[j] > t:
                    t, y = st[j] + cost[j], -2 - j
                st[i], why[i] = t, y
                if t + cost[i] + lat[i] > end:
                    end, last = t + cost[i] + lat[i], i
            while last != -1:
                y = why[last]
                if y <= -2:
                    y = -2 - y
                    waits.append((y, last))
                last = y
            total += end
            times = times or st
        for k, i in enumerate(todo):
            times[i] += 1e-4 * k
        return total / len(sets), times, waits

    key = [0.0] * n
    for k, (i, e, t) in enumerate(order):
        key[i] = t + 1e-4 * k
    best = run(key)
    x = OPT["seed"]
    for _ in range(OPT["swaps"]):
        x = (x * 1103515245 + 12345) % (1 << 31)
        a, b = best[2][(x >> 8) % len(best[2])]
        x = (x * 1103515245 + 12345) % (1 << 31)
        far, step = (0.01, 0.01, 200.0, 700.0)[(x >> 10) % 4], (0, 1, 2, 2)[(x >> 12) % 4]
        key = list(best[1])
        for d in (range(-12, 13, step) if step and min(turn[a], turn[b]) >= 0 else (0,)):
            a2, b2 = at.get((ops[a]["key"], turn[a] + d)), at.get((ops[b]["key"], turn[b] + d))
            if a2 is None or b2 is None or key[b2] < key[a2]:
                continue
            if (x >> 8) % 2:
                key[b2] = key[a2] - far
            else:
                key[a2] = key[b2] + far
        got = run(key)
        if got and got[0] <= best[0]:
            best = got
    return [(i, eng[i], t) for t, i in sorted(zip(best[1], range(n)))], best[0]


PLAN = []


def rank_program(g, core, T, topo):
    rank = T.rank_of(core)
    if rank is None:
        return
    if not PLAN:
        ops = build()
        PLAN.append((ops, refine(schedule(ops)[0])[0]))
    ops, order = PLAN[0]
    n = len(T.cores)
    nxt = T.cores[(rank + 1) % n]
    rid, pid = topo.addr(nxt, core)
    narr = min(len(topo.engines(T.cores[i], T.cores[(i + 1) % n])) for i in range(n))
    eng = topo.engines(core, nxt)
    eng = eng[::len(eng) // narr]
    mask = sum(1 << e for e in eng)
    Qs = {"V": g.vector, "S": g.scalar, "P": g.tensor, "G": g, "Y": g.sync}

    def ap(r):
        if not isap(r):
            return r
        if r[0] == "ind":
            return ap(r[1]).indirect(ap(r[2]))
        if r[0] in ("in", "out"):
            return T[r[1]][r[2]:r[3], :] if len(r) == 4 else T[r[1]][r[2]:r[3], r[4]:r[5]]
        ps = slice(r[4], r[5], r[6]) if r[6] != 1 else slice(r[4], r[5])
        nm, o = PLACE.get(r[0], (r[0], 0))
        cs = slice(o + r[1], o + r[2], r[3]) if r[3] != 1 else slice(o + r[1], o + r[2])
        return T[nm][ps, cs]

    tok = {}
    count = {"V": 0, "S": 0, "P": 0, "G": 0}
    seen = {q: {} for q in Qs}
    total = {}
    for i, e, _ in order:
        o = ops[i]
        k, a = o["kind"], o["args"]
        if k == "recv":
            tok[i] = (a[0], narr); total[a[0]] = narr
            continue
        q = Qs[e]
        need = {}
        for j in o["deps"]:
            if e == "P" and ops[j]["eng"] == "P":
                continue
            s, v = tok[j]
            need[s] = max(need.get(s, 0), v)
        for s, v in need.items():
            if seen[e].get(s, 0) < v:
                q.wait_ge(T.sem[s], v); seen[e][s] = v
        if k == "send":
            g.remote_dma(ap(a[1]), ap(a[0]), T.sem[a[2]], T.sem["sent"], pid, rid, mask)
            total["sent"] = total.get("sent", 0) + len(eng)
            continue
        if k == "dma":
            q.dma_start(ap(a[0]), ap(a[1])).then_inc(T.sem[a[2]], 16)
            tok[i] = (a[2], 16); total[a[2]] = 16
            continue
        if k == "ts":
            ins = q.tensor_scalar(ap(a[0]), ap(a[1]), ap(a[2]), None, a[4]) if a[5] is None else q.tensor_scalar(ap(a[0]), ap(a[1]), ap(a[2]), ap(a[3]), a[4], a[5])
        elif k == "tt":
            ins = q.tensor_tensor(ap(a[0]), ap(a[1]), ap(a[2]), a[3])
        elif k == "cp":
            ins = q.tensor_copy(ap(a[0]), ap(a[1])) if e == "V" else q.activation(ap(a[0]), ap(a[1]), AF.Copy)
        elif k == "act":
            ins = q.activation(ap(a[0]), ap(a[1]), a[2], ap(a[3]), ap(a[4]))
        elif k == "scan":
            ins = q.tensor_tensor_scan(ap(a[0]), ap(a[1]), ap(a[2]), a[3], a[4], a[5])
        elif k == "ms":
            ins = q.memset(ap(a[0]), a[1])
        elif k == "iota":
            ins = g.iota(ap(a[0]), a[1], a[2], a[3], allow_small_or_imprecise_dtypes=True) if SB[a[0][0]][1] != I32 else g.iota(ap(a[0]), a[1], a[2], a[3])
        else:
            for out, terms in a[0]:
                for x, term in enumerate(terms):
                    ins = q.matmul(ap(term[2] if len(term) > 2 else out), ap(term[0]), ap(term[1]), a[1] and x == 0, a[2] and x == len(terms) - 1)
        count[e] += 1
        ins.then_inc(T.sem["c" + e], 1)
        tok[i] = ("c" + e, count[e]); total["c" + e] = count[e]
    for s, v in total.items():
        if seen["G"].get(s, 0) < v:
            g.wait_ge(T.sem[s], v)
